import numpy as np
import ml_dtypes


def mxq(x, axis, fmt="e4m3"):
    dtype, down = {"e4m3": (ml_dtypes.float8_e4m3fn, 7), "e5m2": (ml_dtypes.float8_e5m2, 14)}[fmt]
    v = np.moveaxis(np.asarray(x, np.float32).astype(ml_dtypes.bfloat16).astype(np.float64), axis, -1)
    blocks = v.reshape(v.shape[:-1] + (-1, 32))
    amax = np.abs(blocks).max(-1, keepdims=True)
    byte = np.maximum(np.where(amax > 0, np.frexp(amax)[1] - 1 + 127, 0) - down, 1)
    scale = np.exp2(byte - 127.0)
    codes = (blocks / scale).astype(np.float32).astype(dtype).astype(np.float64)
    return np.moveaxis((codes * scale).reshape(v.shape), -1, axis)


WIDE = False


def mx_kscale(k):
    if not WIDE:
        return np.ones(k)
    levels = np.array([10, -10, 5, -5, 0])
    if k % 512:
        return np.exp2(np.random.permutation(np.resize(levels, k // 32))).repeat(32)
    a = np.empty((k // 512, 16))
    for p in range(k // 512):
        a[p, :8] = np.random.permutation(np.resize(levels, 8))
        for g in range(8):
            far = levels[np.abs(levels - a[p, g]) >= 10]
            a[p, g + 8] = far[np.random.randint(len(far))]
    return np.exp2(a.ravel()).repeat(32)


def f64(x):
    return np.asarray(x).astype(np.float64)


def striped(idx):
    return np.tile(idx.reshape(-1, 16).T, (8, 1)).astype(np.uint16)


def unstriped(offs):
    return offs[:16].T.reshape(-1).astype(np.int64)


E2M1 = np.array([0.0, 0.5, 1.0, 1.5, 2.0, 3.0, 4.0, 6.0, -0.0, -0.5, -1.0, -1.5, -2.0, -3.0, -4.0, -6.0])


def pack_weight(w, fmt):
    k, n = w.shape
    w = f64(np.asarray(w, np.float32).astype(ml_dtypes.bfloat16)).reshape(k // 32, 32, n)
    amax = np.abs(w).max(1)
    if fmt == "e4m3":
        byte = np.frexp(amax)[1] - 1 + 127 - 7
    else:
        mant, ex = np.frexp(amax / 6.0)
        byte = np.where(mant > 0.5, ex, ex - 1) + 127
    byte = np.clip(np.where(amax > 0, byte, 1), 1, 254)
    scaled = (w * np.exp2(127.0 - byte)[:, None, :]).reshape(k, n).astype(np.float32)
    by_word = np.ascontiguousarray(scaled.reshape(k // 512, 128, 4, n).transpose(0, 1, 3, 2))
    if fmt == "e4m3":
        words = by_word.astype(ml_dtypes.float8_e4m3fn).view(np.uint8)
    else:
        c = by_word.astype(ml_dtypes.float4_e2m1fn).view(np.uint8) & 0xF
        words = (c[..., 0::2] | (c[..., 1::2] << 4)).reshape(k // 512, 128, 2 * n)
    return np.ascontiguousarray(words), np.ascontiguousarray(byte.astype(np.uint8).reshape(k // 512, 16, n))


def unpack_weight(words, scales, fmt):
    g, _, n = scales.shape
    words = np.ascontiguousarray(words).reshape(g, 128, n, -1)
    if fmt == "e4m3":
        vals = words.view(ml_dtypes.float8_e4m3fn).astype(np.float64)
    else:
        nib = np.empty((g, 128, n, 4), np.uint8)
        nib[..., 0::2] = words & 0xF
        nib[..., 1::2] = words >> 4
        vals = E2M1[nib]
    vals = vals * np.repeat(np.exp2(scales.astype(np.float64) - 127.0), 8, axis=1)[..., None]
    return vals.transpose(0, 1, 3, 2).reshape(g * 512, n)


def gelu(v):
    return 0.5 * v * (1.0 + np.tanh(np.sqrt(2.0 / np.pi) * (v + 0.044715 * v**3)))


def striped8(idx):
    return np.concatenate([v.reshape(-1, 16).T for v in idx]).astype(np.uint16)


def unstriped8(offs):
    return np.stack([offs[16 * g:16 * g + 16].T.reshape(-1) for g in range(8)]).astype(np.int64)


def heads(h, wgt, idx8):
    r = np.arange(h.shape[0])
    return wgt[r // 4 % 128] * h[r[:, None], idx8[r % 512 // 64]]


K, H, N, T, S, P = 512, 1024, 512, 4096, 2048, 1024

def setup_inputs():
    n = np.random.standard_normal
    s = mx_kscale(K)[:, None]
    s2 = mx_kscale(N)[:, None]
    u = mx_kscale(H)[:, None]
    tab_words, tab_scales = pack_weight(n((K, T)) * s, "e4m3")
    wl_words, wl_scales = pack_weight(n((K, H)) / np.sqrt(K) / s * u.T, "e2m1")
    w2_words, w2_scales = pack_weight(n((H, N)) / np.sqrt(H) / u, "e4m3")
    wgt = np.repeat(np.random.uniform(0.5, 2.0, (8, P)), 16, axis=0)
    return {
        "tab_words": tab_words, "tab_scales": tab_scales,
        "offs": striped(np.random.permutation(T)[:S]),
        "offs2": striped8(np.stack([np.random.permutation(S)[:P] for _ in range(8)])),
        "wl_words": wl_words, "wl_scales": wl_scales,
        "bl": (0.4 * n(H) * u[:, 0]).astype(np.float32),
        "wgt": wgt.astype(np.float32),
        "cs": n((N, P)).astype(np.float32),
        "gc": (np.exp(0.3 * n(N)) * s2[:, 0]).astype(np.float32),
        "wc": (n((N, H)) / np.sqrt(N) / s2 * u.T).astype(np.float32),
        "w2_words": w2_words, "w2_scales": w2_scales,
    }

def reference(tab_words, tab_scales, offs, offs2, wl_words, wl_scales, bl, wgt, cs, gc, wc, w2_words, w2_scales):
    v = unpack_weight(tab_words, tab_scales, "e4m3")[:, unstriped(offs)]
    wl = unpack_weight(wl_words, wl_scales, "e2m1")
    h = (wl.T @ v) + f64(bl)[:, None]
    x = heads(h, f64(wgt), unstriped8(offs2))
    clause = f64(cs)
    cq = mxq(clause * f64(gc)[:, None], 0, "e4m3")
    c = mxq(f64(wc), 0, "e4m3").T @ cq
    z = np.maximum(x, c)
    w2 = unpack_weight(w2_words, w2_scales, "e4m3")
    y = w2.T @ mxq(z, 0, "e4m3")
    return clause + y

@@ -1,0 +1,250 @@
+from contextlib import ExitStack
+
+import concourse.mybir as mybir
+
+K, H, N, T, S, M = 512, 1024, 512, 4096, 2048, 1024
+FLOPS = 2 * K * H * S + 2 * N * H * M + 2 * H * N * M
+
+F32 = mybir.dt.float32
+BF16 = mybir.dt.bfloat16
+I32 = mybir.dt.int32
+U32 = mybir.dt.uint32
+U16 = mybir.dt.uint16
+U8 = mybir.dt.uint8
+FP8X4 = mybir.dt.float8_e4m3fn_x4
+FP4X4 = mybir.dt.float4_e2m1fn_x4
+ALU = mybir.AluOpType
+ACT = mybir.ActivationFunctionType
+
+P = 128
+PACK = 4
+BANK = 512
+SUB = 128
+HALF = 512
+CHUNKS = ((0, 256), (256, 256), (512, 256), (768, 128), (896, 128))
+
+
+def tile_list_clause_state_round_kernel(
+    tc, tab_words, tab_scales, offs, offs2, wl_words, wl_scales, bl, wgt, cs, gc, wc, w2_words, w2_scales, out
+):
+    nc = tc.nc
+    with ExitStack() as ctx:
+        keep = ctx.enter_context(tc.tile_pool(name="keep", bufs=1))
+        ring = ctx.enter_context(tc.tile_pool(name="ring", bufs=2))
+        psum = ctx.enter_context(tc.psum_pool(name="psum", bufs=4))
+
+        def held(shape, dtype, name):
+            return keep.tile(shape, dtype, name=name, tag=name, align_bytes=64)
+
+        def load_scale_rows(queue, plane, rows):
+            for q in range(4):
+                queue.dma_start(plane[32 * q : 32 * q + 4].bitcast(I32), rows[4 * q : 4 * q + 4].bitcast(I32))
+
+        lit = held([P, S // 16], U16, "lit")
+        slot = held([P, M // 16], U16, "slot")
+        tabs = held([P, T], U8, "tabs")
+        tabw = held([P, T], I32, "tabw")
+        wlw_raw = held([P, 2 * H], U8, "wlw_raw")
+        wls_raw = held([P, H], U8, "wls_raw")
+        w2s = held([P, 2, N], U8, "w2s")
+        w2w = held([P, 2, N], I32, "w2w")
+        bias = held([P, 2, PACK], F32, "bias")
+        gain = held([P, PACK], F32, "gain")
+        weight = held([P, M], F32, "weight")
+        warm = held([P, 8], F32, "warm")
+        warm2 = held([P, 8], F32, "warm2")
+
+        nc.vector.memset(wls_raw[:].bitcast(I32), 0)
+        nc.vector.memset(tabs[:].bitcast(I32), 0)
+        nc.vector.memset(warm[:], 0.0)
+        nc.vector.memset(w2s[:].rearrange("p a n -> p (a n)").bitcast(I32), 0)
+        nc.scalar.activation(warm2[:], warm[:], ACT.Identity)
+
+        nc.sync.dma_start(lit[:], offs)
+        nc.sync.dma_start(wlw_raw[:].bitcast(I32), wl_words[0].bitcast(I32))
+        nc.sync.dma_start(wls_raw[0:16].bitcast(I32), wl_scales[0].bitcast(I32))
+        load_scale_rows(nc.sync, tabs[:], tab_scales[0])
+        nc.sync.dma_start(tabw[:], tab_words[0].rearrange("p t i -> p (t i)").bitcast(I32))
+
+        wlw = held([P, 2 * H], U8, "wlw")
+        wls = held([P, H], U8, "wls")
+        nc.vector.tensor_copy(
+            wlw[:].bitcast(U16).rearrange("p (b t m) -> p b t m", b=2, t=PACK),
+            wlw_raw[:].bitcast(U16).rearrange("p (b m t) -> p b t m", b=2, t=PACK),
+        )
+        nc.vector.tensor_copy(
+            wls[:].rearrange("p (b t m) -> p b t m", b=2, t=PACK),
+            wls_raw[:].rearrange("p (b m t) -> p b t m", b=2, t=PACK),
+        )
+
+        for q in range(1, 4):
+            nc.sync.dma_start(wls[32 * q : 32 * q + 4].bitcast(I32), wls[4 * q : 4 * q + 4].bitcast(I32))
+        vs = held([P, S], U8, "vs")
+        nc.vector.tensor_copy(vs[:], tabs[:].indirect(lit[:]))
+
+        wc_rows = wc.rearrange("(p j) r -> p j r", j=PACK)
+        cs_rows = cs.rearrange("(p j) m -> p j m", j=PACK)
+        wc_raw = [held([P, PACK, HALF], F32, "wc_raw%d" % b) for b in range(2)]
+        cs_raw = [held([P, PACK, HALF], F32, "cs_raw%d" % u) for u in range(2)]
+        nc.sync.dma_start(bias[:], bl.rearrange("(b p t) -> p b t", b=2, t=PACK))
+        nc.sync.dma_start(gain[:], gc.rearrange("(p j) -> p j", j=PACK))
+        nc.sync.dma_start(cs_raw[0][:], cs_rows[:, :, 0:HALF])
+        nc.sync.dma_start(slot[:], offs2)
+        nc.sync.dma_start(weight[:], wgt)
+        nc.sync.dma_start(wc_raw[0][:], wc_rows[:, :, 0:HALF])
+        nc.sync.dma_start(cs_raw[1][:], cs_rows[:, :, HALF:M])
+        nc.sync.dma_start(wc_raw[1][:], wc_rows[:, :, HALF:H])
+        nc.sync.dma_start(w2w[:], w2_words.rearrange("a p n i -> p a (n i)").bitcast(I32))
+        load_scale_rows(nc.sync, w2s[:], w2_scales.rearrange("a q n -> q a n"))
+
+        n_lit = S // BANK
+        vw = [held([P, BANK], U32, "vw%d" % j) for j in range(n_lit)]
+        h = [held([P, S], F32, "h%d" % e) for e in range(2 * PACK)]
+
+        def message(e, j):
+            acc = psum.tile([P, BANK], F32, name="acc", tag="wide")
+            nc.tensor.matmul_mx(
+                out=acc[:],
+                lhsT=wlw[:, 2 * P * e : 2 * P * (e + 1)].bitcast(FP4X4),
+                lhsT_scale=wls[:, P * e : P * (e + 1)],
+                rhs=vw[j][:].bitcast(FP8X4),
+                rhs_scale=vs[:, BANK * j : BANK * (j + 1)],
+                start=True,
+                stop=True,
+            )
+            b, t = divmod(e, PACK)
+            nc.scalar.activation(h[e][:, BANK * j : BANK * (j + 1)], acc[:], ACT.Identity, bias=bias[:, b, t : t + 1])
+
+        wcq = [held([P, HALF], U32, "wcq%d" % b) for b in range(2)]
+        wcs = [held([P, HALF], U8, "wcs%d" % b) for b in range(2)]
+        csq = [held([P, HALF], U32, "csq%d" % u) for u in range(2)]
+        css = [held([P, HALF], U8, "css%d" % u) for u in range(2)]
+
+        def quantise(codes, scales, values):
+            nc.vector.quantize_mx(out=codes.bitcast(FP8X4), scales=scales, in_=values)
+
+        def prepare_wc(b):
+            g = ring.tile([P, HALF * PACK], BF16, name="wc_g", tag="grouped", align_bytes=64)
+            nc.scalar.copy(
+                g[:].rearrange("p (t m j) -> p m t j", t=PACK, j=PACK),
+                wc_raw[b][:].rearrange("p j (m t) -> p m t j", t=PACK),
+            )
+            quantise(wcq[b][:], wcs[b][:], g[:])
+
+        def scale_cs(u):
+            scaled = ring.tile([P, PACK, HALF], BF16, name="scaled", tag="scaled", align_bytes=64)
+            for j in range(PACK):
+                nc.vector.tensor_scalar(scaled[:, j, :], cs_raw[u][:, j, :], gain[:, j : j + 1], None, ALU.mult)
+            return scaled
+
+        def prepare_cs(u, scaled):
+            g = ring.tile([P, HALF * PACK], BF16, name="cs_g", tag="grouped", align_bytes=64)
+            nc.scalar.copy(
+                g[:].rearrange("p (c i j) -> p c j i", i=4, j=PACK),
+                scaled[:].rearrange("p j (c i) -> p c j i", i=4),
+            )
+            quantise(csq[u][:], css[u][:], g[:])
+
+        x = [held([P, PACK, M], F32, "x%d" % b) for b in range(2)]
+
+        def pick(e):
+            b, t = divmod(e, PACK)
+            nc.vector.tensor_tensor(x[b][:, t, :], h[e][:].indirect(slot[:]), weight[:], ALU.mult)
+
+        zq = {}
+        zs = {}
+
+        def strongest(b, m0, width):
+            z = ring.tile([P, width * PACK], BF16, name="z", tag="z", align_bytes=64, bufs=3)
+            for s0 in range(0, width, SUB):
+                u, c0 = divmod(m0 + s0, HALF)
+                c = psum.tile([P, PACK, SUB], F32, name="c", tag="proj")
+                for t in range(PACK):
+                    nc.tensor.matmul_mx(
+                        out=c[:, t, :],
+                        lhsT=wcq[b][:, P * t : P * (t + 1)].bitcast(FP8X4),
+                        lhsT_scale=wcs[b][:, P * t : P * (t + 1)],
+                        rhs=csq[u][:, c0 : c0 + SUB].bitcast(FP8X4),
+                        rhs_scale=css[u][:, c0 : c0 + SUB],
+                        start=True,
+                        stop=True,
+                    )
+                nc.vector.tensor_tensor(
+                    z[:, PACK * s0 : PACK * (s0 + SUB)].rearrange("p (c i t) -> p c t i", i=2, t=PACK),
+                    c[:].rearrange("p t (c i) -> p c t i", i=2),
+                    x[b][:, :, m0 + s0 : m0 + s0 + SUB].rearrange("p t (c i) -> p c t i", i=2),
+                    ALU.max,
+                )
+            zq[b, m0] = held([P, width], U32, "zq%d_%d" % (b, m0))
+            zs[b, m0] = held([P, width], U8, "zs%d_%d" % (b, m0))
+            quantise(zq[b, m0][:], zs[b, m0][:], z[:])
+
+        out_rows = out.rearrange("(j p) m -> p j m", p=P)
+
+        resid = []
+
+        def update(m0, width):
+            per_bank = BANK // width
+            u, c0 = divmod(m0, HALF)
+            res = ring.tile([P, N // P, width], F32, name="res", tag="res", bufs=3)
+            for j0 in range(0, N // P, per_bank):
+                y = psum.tile([P, per_bank, width], F32, name="y", tag="wide")
+                for j in range(j0, j0 + per_bank):
+                    for b in range(2):
+                        nc.tensor.matmul_mx(
+                            out=y[:, j - j0, :],
+                            lhsT=w2w[:, b, P * j : P * (j + 1)].bitcast(FP8X4),
+                            lhsT_scale=w2s[:, b, P * j : P * (j + 1)],
+                            rhs=zq[b, m0][:].bitcast(FP8X4),
+                            rhs_scale=zs[b, m0][:],
+                            start=(b == 0),
+                            stop=(b == 1),
+                        )
+                nc.vector.tensor_tensor(
+                    res[:, j0 : j0 + per_bank, :], y[:], resid[u][:, j0 : j0 + per_bank, c0 : c0 + width], ALU.add
+                )
+            nc.sync.dma_start(out_rows[:, :, m0 : m0 + width], res[:])
+
+        for j in range(n_lit):
+            nc.vector.tensor_copy(
+                vw[j][:], tabw[:].bitcast(U32).indirect(lit[:, j * BANK // 16 : (j + 1) * BANK // 16])
+            )
+            message(0, j)
+            message(1, j)
+        scaled = scale_cs(0)
+        pick(0)
+        pick(1)
+        for j in range(n_lit):
+            message(2, j)
+        pick(2)
+        prepare_cs(0, scaled)
+        for j in range(n_lit):
+            message(3, j)
+        scaled = scale_cs(1)
+        pick(3)
+        prepare_wc(0)
+        for j in range(n_lit):
+            message(4, j)
+        for m0, width in CHUNKS[:2]:
+            strongest(0, m0, width)
+        pick(4)
+        prepare_cs(1, scaled)
+        for j in range(n_lit):
+            message(5, j)
+        for m0, width in CHUNKS[2:]:
+            strongest(0, m0, width)
+        pick(5)
+        prepare_wc(1)
+        cs_plain = cs.rearrange("(j p) m -> p j m", p=P)
+        for u, tenant in enumerate(("wc_raw0", "cs_raw0")):
+            resid.append(keep.tile([P, N // P, HALF], F32, name="resid%d" % u, tag=tenant, align_bytes=64))
+            nc.sync.dma_start(resid[u][:], cs_plain[:, :, u * HALF : (u + 1) * HALF])
+        for e in (6, 7):
+            for j in range(n_lit):
+                message(e, j)
+            pick(e)
+        for i, (m0, width) in enumerate(CHUNKS):
+            strongest(1, m0, width)
+            if i > 0:
+                update(*CHUNKS[i - 1])
+        update(*CHUNKS[-1])

@@ -54,7 +54,7 @@ def tile_list_clause_state_round_kernel(
         warm = held([P, 8], F32, "warm")
         warm2 = held([P, 8], F32, "warm2")
 
-        nc.vector.memset(wls_raw[:].bitcast(I32), 0)
+        nc.gpsimd.memset(wls_raw[:].bitcast(I32), 0)
         nc.vector.memset(tabs[:].bitcast(I32), 0)
         nc.vector.memset(warm[:], 0.0)
         nc.vector.memset(w2s[:].rearrange("p a n -> p (a n)").bitcast(I32), 0)
@@ -134,7 +134,10 @@ def tile_list_clause_state_round_kernel(
         def scale_cs(u):
             scaled = ring.tile([P, PACK, HALF], BF16, name="scaled", tag="scaled", align_bytes=64)
             for j in range(PACK):
-                nc.vector.tensor_scalar(scaled[:, j, :], cs_raw[u][:, j, :], gain[:, j : j + 1], None, ALU.mult)
+                if u == 0:
+                    nc.vector.tensor_scalar(scaled[:, j, :], cs_raw[u][:, j, :], gain[:, j : j + 1], None, ALU.mult)
+                else:
+                    nc.scalar.activation(scaled[:, j, :], cs_raw[u][:, j, :], ACT.Copy, scale=gain[:, j : j + 1])
             return scaled
 
         def prepare_cs(u, scaled):
@@ -152,58 +155,59 @@ def tile_list_clause_state_round_kernel(
             nc.vector.tensor_tensor(x[b][:, t, :], h[e][:].indirect(slot[:]), weight[:], ALU.mult)
 
         zq = {}
-        zs = {}
 
-        def strongest(b, m0, width):
-            z = ring.tile([P, width * PACK], BF16, name="z", tag="z", align_bytes=64, bufs=3)
-            for s0 in range(0, width, SUB):
-                u, c0 = divmod(m0 + s0, HALF)
-                c = psum.tile([P, PACK, SUB], F32, name="c", tag="proj")
-                for t in range(PACK):
-                    nc.tensor.matmul_mx(
-                        out=c[:, t, :],
-                        lhsT=wcq[b][:, P * t : P * (t + 1)].bitcast(FP8X4),
-                        lhsT_scale=wcs[b][:, P * t : P * (t + 1)],
-                        rhs=csq[u][:, c0 : c0 + SUB].bitcast(FP8X4),
-                        rhs_scale=css[u][:, c0 : c0 + SUB],
-                        start=True,
-                        stop=True,
+        def strongest(passes, m0, width):
+            z = ring.tile([P, len(passes), width * PACK], BF16, name="z", tag="z", align_bytes=64, bufs=3)
+            for a, b in enumerate(passes):
+                for s0 in range(0, width, SUB):
+                    u, c0 = divmod(m0 + s0, HALF)
+                    c = psum.tile([P, PACK, SUB], F32, name="c", tag="proj")
+                    for t in range(PACK):
+                        nc.tensor.matmul_mx(
+                            out=c[:, t, :],
+                            lhsT=wcq[b][:, P * t : P * (t + 1)].bitcast(FP8X4),
+                            lhsT_scale=wcs[b][:, P * t : P * (t + 1)],
+                            rhs=csq[u][:, c0 : c0 + SUB].bitcast(FP8X4),
+                            rhs_scale=css[u][:, c0 : c0 + SUB],
+                            start=True,
+                            stop=True,
+                        )
+                    nc.vector.tensor_tensor(
+                        z[:, a, PACK * s0 : PACK * (s0 + SUB)].rearrange("p (c i t) -> p c t i", i=2, t=PACK),
+                        c[:].rearrange("p t (c i) -> p c t i", i=2),
+                        x[b][:, :, m0 + s0 : m0 + s0 + SUB].rearrange("p t (c i) -> p c t i", i=2),
+                        ALU.max,
                     )
-                nc.vector.tensor_tensor(
-                    z[:, PACK * s0 : PACK * (s0 + SUB)].rearrange("p (c i t) -> p c t i", i=2, t=PACK),
-                    c[:].rearrange("p t (c i) -> p c t i", i=2),
-                    x[b][:, :, m0 + s0 : m0 + s0 + SUB].rearrange("p t (c i) -> p c t i", i=2),
-                    ALU.max,
-                )
-            zq[b, m0] = held([P, width], U32, "zq%d_%d" % (b, m0))
-            zs[b, m0] = held([P, width], U8, "zs%d_%d" % (b, m0))
-            quantise(zq[b, m0][:], zs[b, m0][:], z[:])
+            name = "%d_%d" % (passes[0], m0)
+            codes = held([P, len(passes) * width], U32, "zq" + name)
+            scales = held([P, len(passes) * width], U8, "zs" + name)
+            quantise(codes[:], scales[:], z[:].rearrange("p a w -> p (a w)"))
+            for a, b in enumerate(passes):
+                for s0 in range(0, width, SUB):
+                    zq[b, m0 + s0] = (codes, scales, a * width + s0)
 
         out_rows = out.rearrange("(j p) m -> p j m", p=P)
-
         resid = []
 
-        def update(m0, width):
-            per_bank = BANK // width
+        def update(m0, width, per_bank):
             u, c0 = divmod(m0, HALF)
-            res = ring.tile([P, N // P, width], F32, name="res", tag="res", bufs=3)
             for j0 in range(0, N // P, per_bank):
                 y = psum.tile([P, per_bank, width], F32, name="y", tag="wide")
                 for j in range(j0, j0 + per_bank):
                     for b in range(2):
+                        codes, scales, z0 = zq[b, m0]
                         nc.tensor.matmul_mx(
                             out=y[:, j - j0, :],
                             lhsT=w2w[:, b, P * j : P * (j + 1)].bitcast(FP8X4),
                             lhsT_scale=w2s[:, b, P * j : P * (j + 1)],
-                            rhs=zq[b, m0][:].bitcast(FP8X4),
-                            rhs_scale=zs[b, m0][:],
+                            rhs=codes[:, z0 : z0 + width].bitcast(FP8X4),
+                            rhs_scale=scales[:, z0 : z0 + width],
                             start=(b == 0),
                             stop=(b == 1),
                         )
-                nc.vector.tensor_tensor(
-                    res[:, j0 : j0 + per_bank, :], y[:], resid[u][:, j0 : j0 + per_bank, c0 : c0 + width], ALU.add
-                )
-            nc.sync.dma_start(out_rows[:, :, m0 : m0 + width], res[:])
+                res = ring.tile([P, per_bank, width], F32, name="res", tag="res", bufs=5)
+                nc.vector.tensor_tensor(res[:], y[:], resid[u][:, j0 : j0 + per_bank, c0 : c0 + width], ALU.add)
+                nc.sync.dma_start(out_rows[:, j0 : j0 + per_bank, m0 : m0 + width], res[:])
 
         for j in range(n_lit):
             nc.vector.tensor_copy(
@@ -211,40 +215,41 @@ def tile_list_clause_state_round_kernel(
             )
             message(0, j)
             message(1, j)
+        def messages(e):
+            for j in range(n_lit):
+                message(e, j)
+
         scaled = scale_cs(0)
         pick(0)
         pick(1)
-        for j in range(n_lit):
-            message(2, j)
+        messages(2)
         pick(2)
         prepare_cs(0, scaled)
-        for j in range(n_lit):
-            message(3, j)
-        scaled = scale_cs(1)
+        messages(3)
         pick(3)
-        prepare_wc(0)
-        for j in range(n_lit):
-            message(4, j)
-        for m0, width in CHUNKS[:2]:
-            strongest(0, m0, width)
+        messages(4)
         pick(4)
-        prepare_cs(1, scaled)
-        for j in range(n_lit):
-            message(5, j)
-        for m0, width in CHUNKS[2:]:
-            strongest(0, m0, width)
-        pick(5)
-        prepare_wc(1)
+        prepare_wc(0)
         cs_plain = cs.rearrange("(j p) m -> p j m", p=P)
-        for u, tenant in enumerate(("wc_raw0", "cs_raw0")):
+        for u, tenant in enumerate(("cs_raw0", "wc_raw0")):
             resid.append(keep.tile([P, N // P, HALF], F32, name="resid%d" % u, tag=tenant, align_bytes=64))
             nc.sync.dma_start(resid[u][:], cs_plain[:, :, u * HALF : (u + 1) * HALF])
-        for e in (6, 7):
-            for j in range(n_lit):
-                message(e, j)
-            pick(e)
-        for i, (m0, width) in enumerate(CHUNKS):
-            strongest(1, m0, width)
-            if i > 0:
-                update(*CHUNKS[i - 1])
-        update(*CHUNKS[-1])
+        messages(5)
+        strongest((0,), 0, HALF)
+        pick(5)
+        messages(6)
+        pick(6)
+        messages(7)
+        pick(7)
+        prepare_wc(1)
+        prepare_cs(1, scale_cs(1))
+        strongest((1,), 0, 256)
+        strongest((1,), 256, 256)
+        update(0, 256, 2)
+        update(256, 256, 2)
+        strongest((0, 1), 512, 256)
+        strongest((0, 1), 768, 128)
+        update(512, 256, 2)
+        strongest((0, 1), 896, 128)
+        update(768, 128, 4)
+        update(896, 128, 2)

@@ -126,8 +126,8 @@ def tile_list_clause_state_round_kernel(
         def prepare_wc(b):
             g = ring.tile([P, HALF * PACK], BF16, name="wc_g", tag="grouped", align_bytes=64)
             nc.scalar.copy(
-                g[:].rearrange("p (t m j) -> p m t j", t=PACK, j=PACK),
-                wc_raw[b][:].rearrange("p j (m t) -> p m t j", t=PACK),
+                g[:].rearrange("p (t m j) -> p m j t", t=PACK, j=PACK),
+                wc_raw[b][:].rearrange("p j (m t) -> p m j t", t=PACK),
             )
             quantise(wcq[b][:], wcs[b][:], g[:])
 

@@ -86,8 +86,8 @@ def tile_list_clause_state_round_kernel(
         cs_rows = cs.rearrange("(p j) m -> p j m", j=PACK)
         wc_raw = [held([P, PACK, HALF], F32, "wc_raw%d" % b) for b in range(2)]
         cs_raw = [held([P, PACK, HALF], F32, "cs_raw%d" % u) for u in range(2)]
-        nc.sync.dma_start(bias[:], bl.rearrange("(b p t) -> p b t", b=2, t=PACK))
-        nc.sync.dma_start(gain[:], gc.rearrange("(p j) -> p j", j=PACK))
+        nc.gpsimd.dma_start(bias[:], bl.rearrange("(b p t) -> p b t", b=2, t=PACK))
+        nc.gpsimd.dma_start(gain[:], gc.rearrange("(p j) -> p j", j=PACK))
         nc.sync.dma_start(cs_raw[0][:], cs_rows[:, :, 0:HALF])
         nc.sync.dma_start(slot[:], offs2)
         nc.sync.dma_start(weight[:], wgt)
@@ -229,27 +229,32 @@ def tile_list_clause_state_round_kernel(
         pick(3)
         messages(4)
         pick(4)
+        for j in range(n_lit - 1):
+            message(5, j)
         prepare_wc(0)
+        message(5, n_lit - 1)
+        pick(5)
         cs_plain = cs.rearrange("(j p) m -> p j m", p=P)
         for u, tenant in enumerate(("cs_raw0", "wc_raw0")):
             resid.append(keep.tile([P, N // P, HALF], F32, name="resid%d" % u, tag=tenant, align_bytes=64))
             nc.sync.dma_start(resid[u][:], cs_plain[:, :, u * HALF : (u + 1) * HALF])
-        messages(5)
-        strongest((0,), 0, HALF)
-        pick(5)
         messages(6)
+        strongest((0,), 0, HALF)
         pick(6)
-        messages(7)
-        pick(7)
+        for j in range(n_lit - 1):
+            message(7, j)
         prepare_wc(1)
+        message(7, n_lit - 1)
+        pick(7)
         prepare_cs(1, scale_cs(1))
         strongest((1,), 0, 256)
         strongest((1,), 256, 256)
         update(0, 256, 2)
         update(256, 256, 2)
         strongest((0, 1), 512, 256)
-        strongest((0, 1), 768, 128)
+        strongest((0,), 768, 256)
+        strongest((1,), 768, 128)
         update(512, 256, 2)
-        strongest((0, 1), 896, 128)
+        strongest((1,), 896, 128)
         update(768, 128, 4)
         update(896, 128, 2)

@@ -18,10 +18,16 @@ ACT = mybir.ActivationFunctionType
 
 P = 128
 PACK = 4
+QUADRANTS = 4
+PASSES = H // (P * PACK)
 BANK = 512
-SUB = 128
-HALF = 512
-CHUNKS = ((0, 256), (256, 256), (512, 256), (768, 128), (896, 128))
+LIST_ROWS = 16
+LITERAL_CHUNKS = S // BANK
+OUT_TILES = N // P
+SUB = BANK // PACK
+HALF = M // 2
+QUARTER = M // 4
+RESULT_BANKS = 9
 
 
 def tile_list_clause_state_round_kernel(
@@ -36,225 +42,236 @@ def tile_list_clause_state_round_kernel(
         def held(shape, dtype, name):
             return keep.tile(shape, dtype, name=name, tag=name, align_bytes=64)
 
-        def load_scale_rows(queue, plane, rows):
-            for q in range(4):
-                queue.dma_start(plane[32 * q : 32 * q + 4].bitcast(I32), rows[4 * q : 4 * q + 4].bitcast(I32))
-
-        lit = held([P, S // 16], U16, "lit")
-        slot = held([P, M // 16], U16, "slot")
-        tabs = held([P, T], U8, "tabs")
-        tabw = held([P, T], I32, "tabw")
-        wlw_raw = held([P, 2 * H], U8, "wlw_raw")
-        wls_raw = held([P, H], U8, "wls_raw")
-        w2s = held([P, 2, N], U8, "w2s")
-        w2w = held([P, 2, N], I32, "w2w")
-        bias = held([P, 2, PACK], F32, "bias")
-        gain = held([P, PACK], F32, "gain")
-        weight = held([P, M], F32, "weight")
-        warm = held([P, 8], F32, "warm")
-        warm2 = held([P, 8], F32, "warm2")
-
-        nc.gpsimd.memset(wls_raw[:].bitcast(I32), 0)
-        nc.vector.memset(tabs[:].bitcast(I32), 0)
-        nc.vector.memset(warm[:], 0.0)
-        nc.vector.memset(w2s[:].rearrange("p a n -> p (a n)").bitcast(I32), 0)
-        nc.scalar.activation(warm2[:], warm[:], ACT.Identity)
-
-        nc.sync.dma_start(lit[:], offs)
-        nc.sync.dma_start(wlw_raw[:].bitcast(I32), wl_words[0].bitcast(I32))
-        nc.sync.dma_start(wls_raw[0:16].bitcast(I32), wl_scales[0].bitcast(I32))
-        load_scale_rows(nc.sync, tabs[:], tab_scales[0])
-        nc.sync.dma_start(tabw[:], tab_words[0].rearrange("p t i -> p (t i)").bitcast(I32))
-
-        wlw = held([P, 2 * H], U8, "wlw")
-        wls = held([P, H], U8, "wls")
-        nc.vector.tensor_copy(
-            wlw[:].bitcast(U16).rearrange("p (b t m) -> p b t m", b=2, t=PACK),
-            wlw_raw[:].bitcast(U16).rearrange("p (b m t) -> p b t m", b=2, t=PACK),
-        )
-        nc.vector.tensor_copy(
-            wls[:].rearrange("p (b t m) -> p b t m", b=2, t=PACK),
-            wls_raw[:].rearrange("p (b m t) -> p b t m", b=2, t=PACK),
-        )
-
-        for q in range(1, 4):
-            nc.sync.dma_start(wls[32 * q : 32 * q + 4].bitcast(I32), wls[4 * q : 4 * q + 4].bitcast(I32))
-        vs = held([P, S], U8, "vs")
-        nc.vector.tensor_copy(vs[:], tabs[:].indirect(lit[:]))
-
-        wc_rows = wc.rearrange("(p j) r -> p j r", j=PACK)
-        cs_rows = cs.rearrange("(p j) m -> p j m", j=PACK)
-        wc_raw = [held([P, PACK, HALF], F32, "wc_raw%d" % b) for b in range(2)]
-        cs_raw = [held([P, PACK, HALF], F32, "cs_raw%d" % u) for u in range(2)]
-        nc.gpsimd.dma_start(bias[:], bl.rearrange("(b p t) -> p b t", b=2, t=PACK))
-        nc.gpsimd.dma_start(gain[:], gc.rearrange("(p j) -> p j", j=PACK))
-        nc.sync.dma_start(cs_raw[0][:], cs_rows[:, :, 0:HALF])
-        nc.sync.dma_start(slot[:], offs2)
-        nc.sync.dma_start(weight[:], wgt)
-        nc.sync.dma_start(wc_raw[0][:], wc_rows[:, :, 0:HALF])
-        nc.sync.dma_start(cs_raw[1][:], cs_rows[:, :, HALF:M])
-        nc.sync.dma_start(wc_raw[1][:], wc_rows[:, :, HALF:H])
-        nc.sync.dma_start(w2w[:], w2_words.rearrange("a p n i -> p a (n i)").bitcast(I32))
-        load_scale_rows(nc.sync, w2s[:], w2_scales.rearrange("a q n -> q a n"))
-
-        n_lit = S // BANK
-        vw = [held([P, BANK], U32, "vw%d" % j) for j in range(n_lit)]
-        h = [held([P, S], F32, "h%d" % e) for e in range(2 * PACK)]
-
-        def message(e, j):
-            acc = psum.tile([P, BANK], F32, name="acc", tag="wide")
-            nc.tensor.matmul_mx(
-                out=acc[:],
-                lhsT=wlw[:, 2 * P * e : 2 * P * (e + 1)].bitcast(FP4X4),
-                lhsT_scale=wls[:, P * e : P * (e + 1)],
-                rhs=vw[j][:].bitcast(FP8X4),
-                rhs_scale=vs[:, BANK * j : BANK * (j + 1)],
-                start=True,
-                stop=True,
-            )
-            b, t = divmod(e, PACK)
-            nc.scalar.activation(h[e][:, BANK * j : BANK * (j + 1)], acc[:], ACT.Identity, bias=bias[:, b, t : t + 1])
-
-        wcq = [held([P, HALF], U32, "wcq%d" % b) for b in range(2)]
-        wcs = [held([P, HALF], U8, "wcs%d" % b) for b in range(2)]
-        csq = [held([P, HALF], U32, "csq%d" % u) for u in range(2)]
-        css = [held([P, HALF], U8, "css%d" % u) for u in range(2)]
+        def load_scale_rows(tile, rows):
+            for q in range(QUADRANTS):
+                nc.sync.dma_start(tile[32 * q : 32 * q + 4].bitcast(I32), rows[4 * q : 4 * q + 4].bitcast(I32))
 
         def quantise(codes, scales, values):
             nc.vector.quantize_mx(out=codes.bitcast(FP8X4), scales=scales, in_=values)
 
-        def prepare_wc(b):
-            g = ring.tile([P, HALF * PACK], BF16, name="wc_g", tag="grouped", align_bytes=64)
-            nc.scalar.copy(
-                g[:].rearrange("p (t m j) -> p m j t", t=PACK, j=PACK),
-                wc_raw[b][:].rearrange("p j (m t) -> p m j t", t=PACK),
-            )
-            quantise(wcq[b][:], wcs[b][:], g[:])
+        literal_list = held([P, S // LIST_ROWS], U16, "literal_list")
+        slot_lists = held([P, M // LIST_ROWS], U16, "slot_lists")
+        table_scales = held([P, T], U8, "table_scales")
+        table_words = held([P, T], I32, "table_words")
+        wl_words_raw = held([P, 2 * H], U8, "wl_words_raw")
+        wl_scales_raw = held([P, H], U8, "wl_scales_raw")
+        w2_scale_tile = held([P, PASSES, N], U8, "w2_scale_tile")
+        w2_word_tile = held([P, PASSES, N], I32, "w2_word_tile")
+        bias = held([P, PASSES, PACK], F32, "bias")
+        gain = held([P, PACK], F32, "gain")
+        weight = held([P, M], F32, "weight")
 
-        def scale_cs(u):
-            scaled = ring.tile([P, PACK, HALF], BF16, name="scaled", tag="scaled", align_bytes=64)
+        nc.gpsimd.memset(wl_scales_raw[:].bitcast(I32), 0)
+        nc.vector.memset(table_scales[:].bitcast(I32), 0)
+        nc.vector.memset(w2_scale_tile[:].rearrange("p a n -> p (a n)").bitcast(I32), 0)
+
+        nc.sync.dma_start(literal_list[:], offs)
+        nc.sync.dma_start(wl_words_raw[:].bitcast(I32), wl_words[0].bitcast(I32))
+        nc.sync.dma_start(wl_scales_raw[0 : 4 * QUADRANTS].bitcast(I32), wl_scales[0].bitcast(I32))
+        load_scale_rows(table_scales[:], tab_scales[0])
+        nc.sync.dma_start(table_words[:], tab_words[0].rearrange("p t i -> p (t i)").bitcast(I32))
+
+        wl_word_tile = held([P, 2 * H], U8, "wl_word_tile")
+        wl_scale_tile = held([P, H], U8, "wl_scale_tile")
+        nc.vector.tensor_copy(
+            wl_word_tile[:].bitcast(U16).rearrange("k (b t p) -> k b t p", b=PASSES, t=PACK),
+            wl_words_raw[:].bitcast(U16).rearrange("k (b p t) -> k b t p", b=PASSES, t=PACK),
+        )
+        nc.vector.tensor_copy(
+            wl_scale_tile[:].rearrange("k (b t p) -> k b t p", b=PASSES, t=PACK),
+            wl_scales_raw[:].rearrange("k (b p t) -> k b t p", b=PASSES, t=PACK),
+        )
+        for q in range(1, QUADRANTS):
+            nc.sync.dma_start(
+                wl_scale_tile[32 * q : 32 * q + 4].bitcast(I32), wl_scale_tile[4 * q : 4 * q + 4].bitcast(I32)
+            )
+
+        v_scales = held([P, S], U8, "v_scales")
+        nc.vector.tensor_copy(v_scales[:], table_scales[:].indirect(literal_list[:]))
+
+        wc_rows = wc.rearrange("(p j) r -> p j r", j=PACK)
+        cs_rows = cs.rearrange("(p j) m -> p j m", j=PACK)
+        wc_raw = [held([P, PACK, HALF], F32, "wc_raw%d" % b) for b in range(PASSES)]
+        cs_raw = [held([P, PACK, HALF], F32, "cs_raw%d" % half) for half in range(2)]
+        nc.gpsimd.dma_start(bias[:], bl.rearrange("(b p t) -> p b t", b=PASSES, t=PACK))
+        nc.gpsimd.dma_start(gain[:], gc.rearrange("(p j) -> p j", j=PACK))
+        nc.sync.dma_start(cs_raw[0][:], cs_rows[:, :, 0:HALF])
+        nc.sync.dma_start(slot_lists[:], offs2)
+        nc.sync.dma_start(weight[:], wgt)
+        nc.sync.dma_start(wc_raw[0][:], wc_rows[:, :, 0:HALF])
+        nc.sync.dma_start(cs_raw[1][:], cs_rows[:, :, HALF:M])
+        nc.sync.dma_start(wc_raw[1][:], wc_rows[:, :, HALF:H])
+        nc.sync.dma_start(w2_word_tile[:], w2_words.rearrange("a p n i -> p a (n i)").bitcast(I32))
+        load_scale_rows(w2_scale_tile[:], w2_scales.rearrange("a q n -> q a n"))
+
+        v_words = [held([P, BANK], U32, "v_words%d" % chunk) for chunk in range(LITERAL_CHUNKS)]
+        h = [held([P, S], F32, "h%d" % row_tile) for row_tile in range(PASSES * PACK)]
+
+        def messages(row_tile, chunks):
+            b, t = divmod(row_tile, PACK)
+            for chunk in chunks:
+                literals = slice(BANK * chunk, BANK * (chunk + 1))
+                acc = psum.tile([P, BANK], F32, name="acc", tag="wide")
+                nc.tensor.matmul_mx(
+                    out=acc[:],
+                    lhsT=wl_word_tile[:, 2 * P * row_tile : 2 * P * (row_tile + 1)].bitcast(FP4X4),
+                    lhsT_scale=wl_scale_tile[:, P * row_tile : P * (row_tile + 1)],
+                    rhs=v_words[chunk][:].bitcast(FP8X4),
+                    rhs_scale=v_scales[:, literals],
+                    start=True,
+                    stop=True,
+                )
+                nc.scalar.activation(h[row_tile][:, literals], acc[:], ACT.Identity, bias=bias[:, b, t : t + 1])
+
+        wc_codes = [held([P, HALF], U32, "wc_codes%d" % b) for b in range(PASSES)]
+        wc_scales = [held([P, HALF], U8, "wc_scales%d" % b) for b in range(PASSES)]
+
+        def quantise_wc(b):
+            interleaved = ring.tile([P, HALF * PACK], BF16, name="wc_interleaved", tag="interleaved", align_bytes=64)
+            nc.scalar.copy(
+                interleaved[:].rearrange("k (t p j) -> k p j t", t=PACK, j=PACK),
+                wc_raw[b][:].rearrange("k j (p t) -> k p j t", t=PACK),
+            )
+            quantise(wc_codes[b][:], wc_scales[b][:], interleaved[:])
+
+        def apply_gain(m0, width):
+            half, c0 = divmod(m0, HALF)
+            gained = ring.tile([P, PACK, width], BF16, name="gained", tag="gained", align_bytes=64)
             for j in range(PACK):
-                if u == 0:
-                    nc.vector.tensor_scalar(scaled[:, j, :], cs_raw[u][:, j, :], gain[:, j : j + 1], None, ALU.mult)
+                rows = cs_raw[half][:, j, c0 : c0 + width]
+                if half == 0:
+                    nc.vector.tensor_scalar(gained[:, j, :], rows, gain[:, j : j + 1], None, ALU.mult)
                 else:
-                    nc.scalar.activation(scaled[:, j, :], cs_raw[u][:, j, :], ACT.Copy, scale=gain[:, j : j + 1])
-            return scaled
+                    nc.scalar.activation(gained[:, j, :], rows, ACT.Copy, scale=gain[:, j : j + 1])
+            return gained
 
-        def prepare_cs(u, scaled):
-            g = ring.tile([P, HALF * PACK], BF16, name="cs_g", tag="grouped", align_bytes=64)
+        cs_operand = {}
+
+        def quantise_cs(m0, width, gained):
+            interleaved = ring.tile([P, width * PACK], BF16, name="cs_interleaved", tag="interleaved", align_bytes=64)
             nc.scalar.copy(
-                g[:].rearrange("p (c i j) -> p c j i", i=4, j=PACK),
-                scaled[:].rearrange("p j (c i) -> p c j i", i=4),
+                interleaved[:].rearrange("p (g i j) -> p g j i", i=4, j=PACK),
+                gained[:].rearrange("p j (g i) -> p g j i", i=4),
             )
-            quantise(csq[u][:], css[u][:], g[:])
+            codes = held([P, width], U32, "cs_codes%d" % m0)
+            scales = held([P, width], U8, "cs_scales%d" % m0)
+            quantise(codes[:], scales[:], interleaved[:])
+            for s0 in range(0, width, SUB):
+                cs_operand[m0 + s0] = (codes[:, s0 : s0 + SUB], scales[:, s0 : s0 + SUB])
 
-        x = [held([P, PACK, M], F32, "x%d" % b) for b in range(2)]
+        x = [held([P, PACK, M], F32, "x%d" % b) for b in range(PASSES)]
 
-        def pick(e):
-            b, t = divmod(e, PACK)
-            nc.vector.tensor_tensor(x[b][:, t, :], h[e][:].indirect(slot[:]), weight[:], ALU.mult)
+        def pick(row_tile):
+            b, t = divmod(row_tile, PACK)
+            nc.vector.tensor_tensor(x[b][:, t, :], h[row_tile][:].indirect(slot_lists[:]), weight[:], ALU.mult)
 
-        zq = {}
+        z_operand = {}
 
         def strongest(passes, m0, width):
-            z = ring.tile([P, len(passes), width * PACK], BF16, name="z", tag="z", align_bytes=64, bufs=3)
-            for a, b in enumerate(passes):
+            z = ring.tile([P, len(passes), width * PACK], BF16, name="z", tag="z", align_bytes=64)
+            for place, b in enumerate(passes):
                 for s0 in range(0, width, SUB):
-                    u, c0 = divmod(m0 + s0, HALF)
+                    cs_codes, cs_scales = cs_operand[m0 + s0]
                     c = psum.tile([P, PACK, SUB], F32, name="c", tag="proj")
                     for t in range(PACK):
                         nc.tensor.matmul_mx(
                             out=c[:, t, :],
-                            lhsT=wcq[b][:, P * t : P * (t + 1)].bitcast(FP8X4),
-                            lhsT_scale=wcs[b][:, P * t : P * (t + 1)],
-                            rhs=csq[u][:, c0 : c0 + SUB].bitcast(FP8X4),
-                            rhs_scale=css[u][:, c0 : c0 + SUB],
+                            lhsT=wc_codes[b][:, P * t : P * (t + 1)].bitcast(FP8X4),
+                            lhsT_scale=wc_scales[b][:, P * t : P * (t + 1)],
+                            rhs=cs_codes.bitcast(FP8X4),
+                            rhs_scale=cs_scales,
                             start=True,
                             stop=True,
                         )
                     nc.vector.tensor_tensor(
-                        z[:, a, PACK * s0 : PACK * (s0 + SUB)].rearrange("p (c i t) -> p c t i", i=2, t=PACK),
-                        c[:].rearrange("p t (c i) -> p c t i", i=2),
-                        x[b][:, :, m0 + s0 : m0 + s0 + SUB].rearrange("p t (c i) -> p c t i", i=2),
+                        z[:, place, PACK * s0 : PACK * (s0 + SUB)].rearrange("p (g i t) -> p g t i", i=2, t=PACK),
+                        c[:].rearrange("p t (g i) -> p g t i", i=2),
+                        x[b][:, :, m0 + s0 : m0 + s0 + SUB].rearrange("p t (g i) -> p g t i", i=2),
                         ALU.max,
                     )
-            name = "%d_%d" % (passes[0], m0)
-            codes = held([P, len(passes) * width], U32, "zq" + name)
-            scales = held([P, len(passes) * width], U8, "zs" + name)
+            codes = held([P, len(passes) * width], U32, "z_codes%d_%d" % (passes[0], m0))
+            scales = held([P, len(passes) * width], U8, "z_scales%d_%d" % (passes[0], m0))
             quantise(codes[:], scales[:], z[:].rearrange("p a w -> p (a w)"))
-            for a, b in enumerate(passes):
+            for place, b in enumerate(passes):
                 for s0 in range(0, width, SUB):
-                    zq[b, m0 + s0] = (codes, scales, a * width + s0)
+                    z_operand[b, m0 + s0] = (codes, scales, place * width + s0)
 
-        out_rows = out.rearrange("(j p) m -> p j m", p=P)
-        resid = []
+        out_rows = out.rearrange("(o p) m -> p o m", p=P)
+        residual = []
 
-        def update(m0, width, per_bank):
-            u, c0 = divmod(m0, HALF)
-            for j0 in range(0, N // P, per_bank):
-                y = psum.tile([P, per_bank, width], F32, name="y", tag="wide")
-                for j in range(j0, j0 + per_bank):
-                    for b in range(2):
-                        codes, scales, z0 = zq[b, m0]
+        def update(m0, width, tiles_per_bank):
+            half, c0 = divmod(m0, HALF)
+            for o0 in range(0, OUT_TILES, tiles_per_bank):
+                y = psum.tile([P, tiles_per_bank, width], F32, name="y", tag="wide")
+                for o in range(o0, o0 + tiles_per_bank):
+                    for b in range(PASSES):
+                        codes, scales, z0 = z_operand[b, m0]
                         nc.tensor.matmul_mx(
-                            out=y[:, j - j0, :],
-                            lhsT=w2w[:, b, P * j : P * (j + 1)].bitcast(FP8X4),
-                            lhsT_scale=w2s[:, b, P * j : P * (j + 1)],
+                            out=y[:, o - o0, :],
+                            lhsT=w2_word_tile[:, b, P * o : P * (o + 1)].bitcast(FP8X4),
+                            lhsT_scale=w2_scale_tile[:, b, P * o : P * (o + 1)],
                             rhs=codes[:, z0 : z0 + width].bitcast(FP8X4),
                             rhs_scale=scales[:, z0 : z0 + width],
                             start=(b == 0),
-                            stop=(b == 1),
+                            stop=(b == PASSES - 1),
                         )
-                res = ring.tile([P, per_bank, width], F32, name="res", tag="res", bufs=5)
-                nc.vector.tensor_tensor(res[:], y[:], resid[u][:, j0 : j0 + per_bank, c0 : c0 + width], ALU.add)
-                nc.sync.dma_start(out_rows[:, j0 : j0 + per_bank, m0 : m0 + width], res[:])
+                result = ring.tile([P, tiles_per_bank, width], F32, name="result", tag="result", bufs=RESULT_BANKS)
+                states = residual[half][:, o0 : o0 + tiles_per_bank, c0 : c0 + width]
+                target = out_rows[:, o0 : o0 + tiles_per_bank, m0 : m0 + width]
+                if half == 0:
+                    nc.scalar.copy(result[:], y[:])
+                    for o in range(tiles_per_bank):
+                        nc.gpsimd.tensor_tensor(result[:, o, :], result[:, o, :], states[:, o, :], ALU.add)
+                    nc.sync.dma_start(target, result[:])
+                else:
+                    nc.vector.tensor_tensor(result[:], y[:], states, ALU.add)
+                    nc.scalar.dma_start(target, result[:])
 
-        for j in range(n_lit):
-            nc.vector.tensor_copy(
-                vw[j][:], tabw[:].bitcast(U32).indirect(lit[:, j * BANK // 16 : (j + 1) * BANK // 16])
-            )
-            message(0, j)
-            message(1, j)
-        def messages(e):
-            for j in range(n_lit):
-                message(e, j)
+        for chunk in range(LITERAL_CHUNKS):
+            entries = literal_list[:, chunk * BANK // LIST_ROWS : (chunk + 1) * BANK // LIST_ROWS]
+            nc.vector.tensor_copy(v_words[chunk][:], table_words[:].bitcast(U32).indirect(entries))
+            messages(0, [chunk])
+            messages(1, [chunk])
 
-        scaled = scale_cs(0)
+        all_chunks = range(LITERAL_CHUNKS)
+        gained = apply_gain(0, HALF)
         pick(0)
         pick(1)
-        messages(2)
+        messages(2, all_chunks)
         pick(2)
-        prepare_cs(0, scaled)
-        messages(3)
-        pick(3)
-        messages(4)
-        pick(4)
-        for j in range(n_lit - 1):
-            message(5, j)
-        prepare_wc(0)
-        message(5, n_lit - 1)
+        quantise_cs(0, HALF, gained)
+        for row_tile in (3, 4):
+            messages(row_tile, all_chunks)
+            pick(row_tile)
+
+        messages(5, all_chunks[:-1])
+        quantise_wc(0)
+        messages(5, all_chunks[-1:])
         pick(5)
-        cs_plain = cs.rearrange("(j p) m -> p j m", p=P)
-        for u, tenant in enumerate(("cs_raw0", "wc_raw0")):
-            resid.append(keep.tile([P, N // P, HALF], F32, name="resid%d" % u, tag=tenant, align_bytes=64))
-            nc.sync.dma_start(resid[u][:], cs_plain[:, :, u * HALF : (u + 1) * HALF])
-        messages(6)
+
+        cs_plain = cs.rearrange("(o p) m -> p o m", p=P)
+        for half, used_up in enumerate(("cs_raw0", "wc_raw0")):
+            residual.append(keep.tile([P, OUT_TILES, HALF], F32, name="residual", tag=used_up, align_bytes=64))
+            nc.sync.dma_start(residual[half][:], cs_plain[:, :, half * HALF : (half + 1) * HALF])
+
+        messages(6, all_chunks)
         strongest((0,), 0, HALF)
         pick(6)
-        for j in range(n_lit - 1):
-            message(7, j)
-        prepare_wc(1)
-        message(7, n_lit - 1)
+        messages(7, all_chunks[:-1])
+        quantise_wc(1)
+        messages(7, all_chunks[-1:])
         pick(7)
-        prepare_cs(1, scale_cs(1))
-        strongest((1,), 0, 256)
-        strongest((1,), 256, 256)
-        update(0, 256, 2)
-        update(256, 256, 2)
-        strongest((0, 1), 512, 256)
-        strongest((0,), 768, 256)
-        strongest((1,), 768, 128)
-        update(512, 256, 2)
-        strongest((1,), 896, 128)
-        update(768, 128, 4)
-        update(896, 128, 2)
+
+        for m0 in (HALF, HALF + QUARTER):
+            quantise_cs(m0, QUARTER, apply_gain(m0, QUARTER))
+        for m0 in (0, QUARTER):
+            strongest((1,), m0, QUARTER)
+        for m0 in (0, QUARTER):
+            update(m0, QUARTER, 2)
+        strongest((0, 1), HALF, QUARTER)
+        strongest((0,), HALF + QUARTER, QUARTER)
+        strongest((1,), M - 2 * SUB, SUB)
+        update(HALF, QUARTER, 2)
+        strongest((1,), M - SUB, SUB)
+        update(M - 2 * SUB, SUB, 4)
+        update(M - SUB, SUB, 2)

@@ -63,7 +63,10 @@ def tile_list_clause_state_round_kernel(
 
         nc.gpsimd.memset(wl_scales_raw[:].bitcast(I32), 0)
         nc.vector.memset(table_scales[:].bitcast(I32), 0)
-        nc.vector.memset(w2_scale_tile[:].rearrange("p a n -> p (a n)").bitcast(I32), 0)
+        v_scales = held([P, S], U8, "v_scales")
+        nc.gpsimd.dma_start(bias[:], bl.rearrange("(b p t) -> p b t", b=PASSES, t=PACK))
+        nc.gpsimd.dma_start(gain[:], gc.rearrange("(p j) -> p j", j=PACK))
+        nc.gpsimd.memset(w2_scale_tile[:].rearrange("p a n -> p (a n)").bitcast(I32), 0)
 
         nc.sync.dma_start(literal_list[:], offs)
         nc.sync.dma_start(wl_words_raw[:].bitcast(I32), wl_words[0].bitcast(I32))
@@ -77,7 +80,7 @@ def tile_list_clause_state_round_kernel(
             wl_word_tile[:].bitcast(U16).rearrange("k (b t p) -> k b t p", b=PASSES, t=PACK),
             wl_words_raw[:].bitcast(U16).rearrange("k (b p t) -> k b t p", b=PASSES, t=PACK),
         )
-        nc.vector.tensor_copy(
+        nc.gpsimd.tensor_copy(
             wl_scale_tile[:].rearrange("k (b t p) -> k b t p", b=PASSES, t=PACK),
             wl_scales_raw[:].rearrange("k (b p t) -> k b t p", b=PASSES, t=PACK),
         )
@@ -86,20 +89,19 @@ def tile_list_clause_state_round_kernel(
                 wl_scale_tile[32 * q : 32 * q + 4].bitcast(I32), wl_scale_tile[4 * q : 4 * q + 4].bitcast(I32)
             )
 
-        v_scales = held([P, S], U8, "v_scales")
         nc.vector.tensor_copy(v_scales[:], table_scales[:].indirect(literal_list[:]))
 
         wc_rows = wc.rearrange("(p j) r -> p j r", j=PACK)
         cs_rows = cs.rearrange("(p j) m -> p j m", j=PACK)
         wc_raw = [held([P, PACK, HALF], F32, "wc_raw%d" % b) for b in range(PASSES)]
-        cs_raw = [held([P, PACK, HALF], F32, "cs_raw%d" % half) for half in range(2)]
-        nc.gpsimd.dma_start(bias[:], bl.rearrange("(b p t) -> p b t", b=PASSES, t=PACK))
-        nc.gpsimd.dma_start(gain[:], gc.rearrange("(p j) -> p j", j=PACK))
-        nc.sync.dma_start(cs_raw[0][:], cs_rows[:, :, 0:HALF])
+        cs_raw = [held([P, PACK, QUARTER], F32, "cs_raw%d" % quarter) for quarter in range(4)]
+        nc.sync.dma_start(cs_raw[0][:], cs_rows[:, :, 0:QUARTER])
+        nc.sync.dma_start(cs_raw[1][:], cs_rows[:, :, QUARTER:HALF])
         nc.sync.dma_start(slot_lists[:], offs2)
         nc.sync.dma_start(weight[:], wgt)
         nc.sync.dma_start(wc_raw[0][:], wc_rows[:, :, 0:HALF])
-        nc.sync.dma_start(cs_raw[1][:], cs_rows[:, :, HALF:M])
+        for quarter in (2, 3):
+            nc.sync.dma_start(cs_raw[quarter][:], cs_rows[:, :, quarter * QUARTER : (quarter + 1) * QUARTER])
         nc.sync.dma_start(wc_raw[1][:], wc_rows[:, :, HALF:H])
         nc.sync.dma_start(w2_word_tile[:], w2_words.rearrange("a p n i -> p a (n i)").bitcast(I32))
         load_scale_rows(w2_scale_tile[:], w2_scales.rearrange("a q n -> q a n"))
@@ -134,22 +136,21 @@ def tile_list_clause_state_round_kernel(
             )
             quantise(wc_codes[b][:], wc_scales[b][:], interleaved[:])
 
-        def apply_gain(m0, width):
-            half, c0 = divmod(m0, HALF)
-            gained = ring.tile([P, PACK, width], BF16, name="gained", tag="gained", align_bytes=64)
+        def apply_gain(m0, after):
+            gained = keep.tile([P, PACK, QUARTER], BF16, name="gained", tag=after, align_bytes=64)
             for j in range(PACK):
-                rows = cs_raw[half][:, j, c0 : c0 + width]
-                if half == 0:
-                    nc.vector.tensor_scalar(gained[:, j, :], rows, gain[:, j : j + 1], None, ALU.mult)
+                rows = cs_raw[m0 // QUARTER][:, j, :]
+                if m0 < M - QUARTER:
+                    nc.gpsimd.tensor_scalar(gained[:, j, :], rows, gain[:, j : j + 1], 0.0, ALU.mult, ALU.add)
                 else:
                     nc.scalar.activation(gained[:, j, :], rows, ACT.Copy, scale=gain[:, j : j + 1])
             return gained
 
         cs_operand = {}
 
-        def quantise_cs(m0, width, gained):
-            interleaved = ring.tile([P, width * PACK], BF16, name="cs_interleaved", tag="interleaved", align_bytes=64)
-            nc.scalar.copy(
+        def quantise_cs(m0, width, gained, after):
+            interleaved = keep.tile([P, width * PACK], BF16, name="cs_interleaved", tag=after, align_bytes=64)
+            (nc.vector.tensor_copy if m0 == 0 else nc.scalar.copy)(
                 interleaved[:].rearrange("p (g i j) -> p g j i", i=4, j=PACK),
                 gained[:].rearrange("p j (g i) -> p g j i", i=4),
             )
@@ -184,9 +185,9 @@ def tile_list_clause_state_round_kernel(
                             stop=True,
                         )
                     nc.vector.tensor_tensor(
-                        z[:, place, PACK * s0 : PACK * (s0 + SUB)].rearrange("p (g i t) -> p g t i", i=2, t=PACK),
-                        c[:].rearrange("p t (g i) -> p g t i", i=2),
-                        x[b][:, :, m0 + s0 : m0 + s0 + SUB].rearrange("p t (g i) -> p g t i", i=2),
+                        z[:, place, PACK * s0 : PACK * (s0 + SUB)].rearrange("p (g i t) -> p g t i", i=4, t=PACK),
+                        c[:].rearrange("p t (g i) -> p g t i", i=4),
+                        x[b][:, :, m0 + s0 : m0 + s0 + SUB].rearrange("p t (g i) -> p g t i", i=4),
                         ALU.max,
                     )
             codes = held([P, len(passes) * width], U32, "z_codes%d_%d" % (passes[0], m0))
@@ -203,8 +204,8 @@ def tile_list_clause_state_round_kernel(
             half, c0 = divmod(m0, HALF)
             for o0 in range(0, OUT_TILES, tiles_per_bank):
                 y = psum.tile([P, tiles_per_bank, width], F32, name="y", tag="wide")
-                for o in range(o0, o0 + tiles_per_bank):
-                    for b in range(PASSES):
+                for b in range(PASSES):
+                    for o in range(o0, o0 + tiles_per_bank):
                         codes, scales, z0 = z_operand[b, m0]
                         nc.tensor.matmul_mx(
                             out=y[:, o - o0, :],
@@ -212,13 +213,13 @@ def tile_list_clause_state_round_kernel(
                             lhsT_scale=w2_scale_tile[:, b, P * o : P * (o + 1)],
                             rhs=codes[:, z0 : z0 + width].bitcast(FP8X4),
                             rhs_scale=scales[:, z0 : z0 + width],
-                            start=(b == 0),
-                            stop=(b == PASSES - 1),
+                            start=(b == 0 and o == o0),
+                            stop=(b == PASSES - 1 and o == o0 + tiles_per_bank - 1),
                         )
                 result = ring.tile([P, tiles_per_bank, width], F32, name="result", tag="result", bufs=RESULT_BANKS)
                 states = residual[half][:, o0 : o0 + tiles_per_bank, c0 : c0 + width]
                 target = out_rows[:, o0 : o0 + tiles_per_bank, m0 : m0 + width]
-                if half == 0:
+                if m0 < HALF or (m0 == HALF and o0 == 0):
                     nc.scalar.copy(result[:], y[:])
                     for o in range(tiles_per_bank):
                         nc.gpsimd.tensor_tensor(result[:, o, :], result[:, o, :], states[:, o, :], ALU.add)
@@ -234,12 +235,13 @@ def tile_list_clause_state_round_kernel(
             messages(1, [chunk])
 
         all_chunks = range(LITERAL_CHUNKS)
-        gained = apply_gain(0, HALF)
+        quantise_cs(0, QUARTER, apply_gain(0, "gained0"), "interleaved0")
+        gained = apply_gain(QUARTER, "gained1")
         pick(0)
         pick(1)
         messages(2, all_chunks)
         pick(2)
-        quantise_cs(0, HALF, gained)
+        quantise_cs(QUARTER, QUARTER, gained, "h0")
         for row_tile in (3, 4):
             messages(row_tile, all_chunks)
             pick(row_tile)
@@ -250,10 +252,11 @@ def tile_list_clause_state_round_kernel(
         pick(5)
 
         cs_plain = cs.rearrange("(o p) m -> p o m", p=P)
-        for half, used_up in enumerate(("cs_raw0", "wc_raw0")):
+        for half, used_up in enumerate(("table_words", "wc_raw0")):
             residual.append(keep.tile([P, OUT_TILES, HALF], F32, name="residual", tag=used_up, align_bytes=64))
             nc.sync.dma_start(residual[half][:], cs_plain[:, :, half * HALF : (half + 1) * HALF])
 
+        gained = apply_gain(HALF, "h5")
         messages(6, all_chunks)
         strongest((0,), 0, HALF)
         pick(6)
@@ -262,12 +265,12 @@ def tile_list_clause_state_round_kernel(
         messages(7, all_chunks[-1:])
         pick(7)
 
-        for m0 in (HALF, HALF + QUARTER):
-            quantise_cs(m0, QUARTER, apply_gain(m0, QUARTER))
-        for m0 in (0, QUARTER):
-            strongest((1,), m0, QUARTER)
-        for m0 in (0, QUARTER):
-            update(m0, QUARTER, 2)
+        strongest((1,), 0, QUARTER)
+        update(0, QUARTER, 2)
+        quantise_cs(HALF, QUARTER, gained, "h6")
+        strongest((1,), QUARTER, QUARTER)
+        update(QUARTER, QUARTER, 2)
+        quantise_cs(HALF + QUARTER, QUARTER, apply_gain(HALF + QUARTER, "h2"), "h1")
         strongest((0, 1), HALF, QUARTER)
         strongest((0,), HALF + QUARTER, QUARTER)
         strongest((1,), M - 2 * SUB, SUB)

@@ -27,6 +27,7 @@ OUT_TILES = N // P
 SUB = BANK // PACK
 HALF = M // 2
 QUARTER = M // 4
+CS_RANGES = ((0, QUARTER), (QUARTER, QUARTER), (HALF, HALF))
 RESULT_BANKS = 9
 
 
@@ -94,14 +95,13 @@ def tile_list_clause_state_round_kernel(
         wc_rows = wc.rearrange("(p j) r -> p j r", j=PACK)
         cs_rows = cs.rearrange("(p j) m -> p j m", j=PACK)
         wc_raw = [held([P, PACK, HALF], F32, "wc_raw%d" % b) for b in range(PASSES)]
-        cs_raw = [held([P, PACK, QUARTER], F32, "cs_raw%d" % quarter) for quarter in range(4)]
+        cs_raw = {m0: held([P, PACK, width], F32, "cs_raw%d" % m0) for m0, width in CS_RANGES}
         nc.sync.dma_start(cs_raw[0][:], cs_rows[:, :, 0:QUARTER])
-        nc.sync.dma_start(cs_raw[1][:], cs_rows[:, :, QUARTER:HALF])
+        nc.sync.dma_start(cs_raw[QUARTER][:], cs_rows[:, :, QUARTER:HALF])
         nc.sync.dma_start(slot_lists[:], offs2)
         nc.sync.dma_start(weight[:], wgt)
         nc.sync.dma_start(wc_raw[0][:], wc_rows[:, :, 0:HALF])
-        for quarter in (2, 3):
-            nc.sync.dma_start(cs_raw[quarter][:], cs_rows[:, :, quarter * QUARTER : (quarter + 1) * QUARTER])
+        nc.sync.dma_start(cs_raw[HALF][:], cs_rows[:, :, HALF:M])
         nc.sync.dma_start(wc_raw[1][:], wc_rows[:, :, HALF:H])
         nc.sync.dma_start(w2_word_tile[:], w2_words.rearrange("a p n i -> p a (n i)").bitcast(I32))
         load_scale_rows(w2_scale_tile[:], w2_scales.rearrange("a q n -> q a n"))
@@ -136,14 +136,11 @@ def tile_list_clause_state_round_kernel(
             )
             quantise(wc_codes[b][:], wc_scales[b][:], interleaved[:])
 
-        def apply_gain(m0, after):
-            gained = keep.tile([P, PACK, QUARTER], BF16, name="gained", tag=after, align_bytes=64)
+        def apply_gain(m0, width, after):
+            gained = keep.tile([P, PACK, width], BF16, name="gained", tag=after, align_bytes=64)
             for j in range(PACK):
-                rows = cs_raw[m0 // QUARTER][:, j, :]
-                if m0 < M - QUARTER:
-                    nc.gpsimd.tensor_scalar(gained[:, j, :], rows, gain[:, j : j + 1], 0.0, ALU.mult, ALU.add)
-                else:
-                    nc.scalar.activation(gained[:, j, :], rows, ACT.Copy, scale=gain[:, j : j + 1])
+                rows = cs_raw[m0][:, j, :]
+                nc.gpsimd.tensor_scalar(gained[:, j, :], rows, gain[:, j : j + 1], 0.0, ALU.mult, ALU.add)
             return gained
 
         cs_operand = {}
@@ -168,8 +165,11 @@ def tile_list_clause_state_round_kernel(
 
         z_operand = {}
 
-        def strongest(passes, m0, width):
-            z = ring.tile([P, len(passes), width * PACK], BF16, name="z", tag="z", align_bytes=64)
+        def strongest(passes, m0, width, after=None):
+            if after is None:
+                z = ring.tile([P, len(passes), width * PACK], BF16, name="z", tag="z", align_bytes=64)
+            else:
+                z = keep.tile([P, len(passes), width * PACK], BF16, name="z", tag=after, align_bytes=64)
             for place, b in enumerate(passes):
                 for s0 in range(0, width, SUB):
                     cs_codes, cs_scales = cs_operand[m0 + s0]
@@ -223,7 +223,7 @@ def tile_list_clause_state_round_kernel(
                     nc.scalar.copy(result[:], y[:])
                     for o in range(tiles_per_bank):
                         nc.gpsimd.tensor_tensor(result[:, o, :], result[:, o, :], states[:, o, :], ALU.add)
-                    nc.sync.dma_start(target, result[:])
+                        nc.sync.dma_start(target[:, o, :], result[:, o, :])
                 else:
                     nc.vector.tensor_tensor(result[:], y[:], states, ALU.add)
                     nc.scalar.dma_start(target, result[:])
@@ -235,14 +235,11 @@ def tile_list_clause_state_round_kernel(
             messages(1, [chunk])
 
         all_chunks = range(LITERAL_CHUNKS)
-        quantise_cs(0, QUARTER, apply_gain(0, "gained0"), "interleaved0")
-        gained = apply_gain(QUARTER, "gained1")
+        quantise_cs(0, QUARTER, apply_gain(0, QUARTER, "gained0"), "interleaved0")
+        gained = apply_gain(QUARTER, QUARTER, "gained1")
         pick(0)
         pick(1)
-        messages(2, all_chunks)
-        pick(2)
-        quantise_cs(QUARTER, QUARTER, gained, "h0")
-        for row_tile in (3, 4):
+        for row_tile in (2, 3, 4):
             messages(row_tile, all_chunks)
             pick(row_tile)
 
@@ -250,27 +247,27 @@ def tile_list_clause_state_round_kernel(
         quantise_wc(0)
         messages(5, all_chunks[-1:])
         pick(5)
+        quantise_cs(QUARTER, QUARTER, gained, "h3")
 
         cs_plain = cs.rearrange("(o p) m -> p o m", p=P)
         for half, used_up in enumerate(("table_words", "wc_raw0")):
             residual.append(keep.tile([P, OUT_TILES, HALF], F32, name="residual", tag=used_up, align_bytes=64))
             nc.sync.dma_start(residual[half][:], cs_plain[:, :, half * HALF : (half + 1) * HALF])
 
-        gained = apply_gain(HALF, "h5")
+        gained = apply_gain(HALF, HALF, "h5")
         messages(6, all_chunks)
-        strongest((0,), 0, HALF)
+        strongest((0,), 0, HALF, "h3")
         pick(6)
         messages(7, all_chunks[:-1])
         quantise_wc(1)
         messages(7, all_chunks[-1:])
         pick(7)
 
+        quantise_cs(HALF, HALF, gained, "h6")
         strongest((1,), 0, QUARTER)
         update(0, QUARTER, 2)
-        quantise_cs(HALF, QUARTER, gained, "h6")
         strongest((1,), QUARTER, QUARTER)
         update(QUARTER, QUARTER, 2)
-        quantise_cs(HALF + QUARTER, QUARTER, apply_gain(HALF + QUARTER, "h2"), "h1")
         strongest((0, 1), HALF, QUARTER)
         strongest((0,), HALF + QUARTER, QUARTER)
         strongest((1,), M - 2 * SUB, SUB)

@@ -44,8 +44,8 @@ def tile_list_clause_state_round_kernel(
             return keep.tile(shape, dtype, name=name, tag=name, align_bytes=64)
 
         def load_scale_rows(tile, rows):
-            for q in range(QUADRANTS):
-                nc.sync.dma_start(tile[32 * q : 32 * q + 4].bitcast(I32), rows[4 * q : 4 * q + 4].bitcast(I32))
+            for r in range(4):
+                nc.sync.dma_start(tile[r:P:32].bitcast(I32), rows[r : 4 * QUADRANTS : 4].bitcast(I32))
 
         def quantise(codes, scales, values):
             nc.vector.quantize_mx(out=codes.bitcast(FP8X4), scales=scales, in_=values)
@@ -81,7 +81,7 @@ def tile_list_clause_state_round_kernel(
             wl_word_tile[:].bitcast(U16).rearrange("k (b t p) -> k b t p", b=PASSES, t=PACK),
             wl_words_raw[:].bitcast(U16).rearrange("k (b p t) -> k b t p", b=PASSES, t=PACK),
         )
-        nc.gpsimd.tensor_copy(
+        nc.vector.tensor_copy(
             wl_scale_tile[:].rearrange("k (b t p) -> k b t p", b=PASSES, t=PACK),
             wl_scales_raw[:].rearrange("k (b p t) -> k b t p", b=PASSES, t=PACK),
         )
@@ -167,7 +167,7 @@ def tile_list_clause_state_round_kernel(
 
         def strongest(passes, m0, width, after=None):
             if after is None:
-                z = ring.tile([P, len(passes), width * PACK], BF16, name="z", tag="z", align_bytes=64)
+                z = ring.tile([P, len(passes), width * PACK], BF16, name="z", tag="z", bufs=3, align_bytes=64)
             else:
                 z = keep.tile([P, len(passes), width * PACK], BF16, name="z", tag=after, align_bytes=64)
             for place, b in enumerate(passes):
@@ -190,6 +190,9 @@ def tile_list_clause_state_round_kernel(
                         x[b][:, :, m0 + s0 : m0 + s0 + SUB].rearrange("p t (g i) -> p g t i", i=4),
                         ALU.max,
                     )
+            return z, passes, m0, width
+
+        def quantise_z(z, passes, m0, width):
             codes = held([P, len(passes) * width], U32, "z_codes%d_%d" % (passes[0], m0))
             scales = held([P, len(passes) * width], U8, "z_scales%d_%d" % (passes[0], m0))
             quantise(codes[:], scales[:], z[:].rearrange("p a w -> p (a w)"))
@@ -219,14 +222,18 @@ def tile_list_clause_state_round_kernel(
                 result = ring.tile([P, tiles_per_bank, width], F32, name="result", tag="result", bufs=RESULT_BANKS)
                 states = residual[half][:, o0 : o0 + tiles_per_bank, c0 : c0 + width]
                 target = out_rows[:, o0 : o0 + tiles_per_bank, m0 : m0 + width]
-                if m0 < HALF or (m0 == HALF and o0 == 0):
+                if m0 < HALF:
                     nc.scalar.copy(result[:], y[:])
                     for o in range(tiles_per_bank):
                         nc.gpsimd.tensor_tensor(result[:, o, :], result[:, o, :], states[:, o, :], ALU.add)
                         nc.sync.dma_start(target[:, o, :], result[:, o, :])
-                else:
+                elif m0 == HALF:
                     nc.vector.tensor_tensor(result[:], y[:], states, ALU.add)
                     nc.scalar.dma_start(target, result[:])
+                else:
+                    for o in range(tiles_per_bank):
+                        nc.vector.tensor_tensor(result[:, o, :], y[:, o, :], states[:, o, :], ALU.add)
+                        nc.scalar.dma_start(target[:, o, :], result[:, o, :])
 
         for chunk in range(LITERAL_CHUNKS):
             entries = literal_list[:, chunk * BANK // LIST_ROWS : (chunk + 1) * BANK // LIST_ROWS]
@@ -256,7 +263,7 @@ def tile_list_clause_state_round_kernel(
 
         gained = apply_gain(HALF, HALF, "h5")
         messages(6, all_chunks)
-        strongest((0,), 0, HALF, "h3")
+        quantise_z(*strongest((0,), 0, HALF, "h3"))
         pick(6)
         messages(7, all_chunks[:-1])
         quantise_wc(1)
@@ -264,14 +271,14 @@ def tile_list_clause_state_round_kernel(
         pick(7)
 
         quantise_cs(HALF, HALF, gained, "h6")
-        strongest((1,), 0, QUARTER)
-        update(0, QUARTER, 2)
-        strongest((1,), QUARTER, QUARTER)
-        update(QUARTER, QUARTER, 2)
-        strongest((0, 1), HALF, QUARTER)
-        strongest((0,), HALF + QUARTER, QUARTER)
-        strongest((1,), M - 2 * SUB, SUB)
+        for m0 in (0, QUARTER):
+            quantise_z(*strongest((1,), m0, QUARTER))
+            update(m0, QUARTER, 2)
+        third = strongest((0, 1), HALF, QUARTER)
+        fourth = strongest((0,), HALF + QUARTER, QUARTER)
+        quantise_z(*third)
+        quantise_z(*fourth)
+        fourth = strongest((1,), HALF + QUARTER, QUARTER)
         update(HALF, QUARTER, 2)
-        strongest((1,), M - SUB, SUB)
-        update(M - 2 * SUB, SUB, 4)
-        update(M - SUB, SUB, 2)
+        quantise_z(*fourth)
+        update(HALF + QUARTER, QUARTER, 2)

@@ -28,7 +28,7 @@ SUB = BANK // PACK
 HALF = M // 2
 QUARTER = M // 4
 CS_RANGES = ((0, QUARTER), (QUARTER, QUARTER), (HALF, HALF))
-RESULT_BANKS = 9
+RESULT_BANKS = 8
 
 
 def tile_list_clause_state_round_kernel(
@@ -125,32 +125,38 @@ def tile_list_clause_state_round_kernel(
                 )
                 nc.scalar.activation(h[row_tile][:, literals], acc[:], ACT.Identity, bias=bias[:, b, t : t + 1])
 
+        def reuse(shape, dtype, name, used_up):
+            return keep.tile(shape, dtype, name=name, tag=used_up, align_bytes=64)
+
         wc_codes = [held([P, HALF], U32, "wc_codes%d" % b) for b in range(PASSES)]
         wc_scales = [held([P, HALF], U8, "wc_scales%d" % b) for b in range(PASSES)]
 
-        def quantise_wc(b):
+        def interleave_wc(b):
             interleaved = ring.tile([P, HALF * PACK], BF16, name="wc_interleaved", tag="interleaved", align_bytes=64)
             nc.scalar.copy(
                 interleaved[:].rearrange("k (t p j) -> k p j t", t=PACK, j=PACK),
                 wc_raw[b][:].rearrange("k j (p t) -> k p j t", t=PACK),
             )
-            quantise(wc_codes[b][:], wc_scales[b][:], interleaved[:])
+            return interleaved
 
-        def apply_gain(m0, width, after):
-            gained = keep.tile([P, PACK, width], BF16, name="gained", tag=after, align_bytes=64)
+        def gain_on_gpsimd(m0, name):
+            gained = held([P, PACK, QUARTER], BF16, name)
             for j in range(PACK):
-                rows = cs_raw[m0][:, j, :]
-                nc.gpsimd.tensor_scalar(gained[:, j, :], rows, gain[:, j : j + 1], 0.0, ALU.mult, ALU.add)
+                nc.gpsimd.tensor_scalar(gained[:, j, :], cs_raw[m0][:, j, :], gain[:, j : j + 1], 0.0, ALU.mult, ALU.add)
             return gained
+
+        def interleave_cs(copy, gained, used_up):
+            interleaved = reuse([P, gained.shape[2] * PACK], BF16, "cs_interleaved", used_up)
+            copy(
+                interleaved[:].rearrange("p (g i j) -> p g j i", i=4, j=PACK),
+                gained.rearrange("p j (g i) -> p g j i", i=4),
+            )
+            return interleaved
 
         cs_operand = {}
 
-        def quantise_cs(m0, width, gained, after):
-            interleaved = keep.tile([P, width * PACK], BF16, name="cs_interleaved", tag=after, align_bytes=64)
-            (nc.vector.tensor_copy if m0 == 0 else nc.scalar.copy)(
-                interleaved[:].rearrange("p (g i j) -> p g j i", i=4, j=PACK),
-                gained[:].rearrange("p j (g i) -> p g j i", i=4),
-            )
+        def quantise_cs(m0, interleaved):
+            width = interleaved.shape[1] // PACK
             codes = held([P, width], U32, "cs_codes%d" % m0)
             scales = held([P, width], U8, "cs_scales%d" % m0)
             quantise(codes[:], scales[:], interleaved[:])
@@ -163,77 +169,100 @@ def tile_list_clause_state_round_kernel(
             b, t = divmod(row_tile, PACK)
             nc.vector.tensor_tensor(x[b][:, t, :], h[row_tile][:].indirect(slot_lists[:]), weight[:], ALU.mult)
 
+        def strongest(z, b, m0):
+            for s0 in range(0, z.shape[1] // PACK, SUB):
+                cs_codes, cs_scales = cs_operand[m0 + s0]
+                c = psum.tile([P, PACK, SUB], F32, name="c", tag="proj")
+                for t in range(PACK):
+                    nc.tensor.matmul_mx(
+                        out=c[:, t, :],
+                        lhsT=wc_codes[b][:, P * t : P * (t + 1)].bitcast(FP8X4),
+                        lhsT_scale=wc_scales[b][:, P * t : P * (t + 1)],
+                        rhs=cs_codes.bitcast(FP8X4),
+                        rhs_scale=cs_scales,
+                        start=True,
+                        stop=True,
+                    )
+                nc.vector.tensor_tensor(
+                    z[:, PACK * s0 : PACK * (s0 + SUB)].rearrange("p (g i t) -> p g t i", i=4, t=PACK),
+                    c[:].rearrange("p t (g i) -> p g t i", i=4),
+                    x[b][:, :, m0 + s0 : m0 + s0 + SUB].rearrange("p t (g i) -> p g t i", i=4),
+                    ALU.max,
+                )
+
         z_operand = {}
 
-        def strongest(passes, m0, width, after=None):
-            if after is None:
-                z = ring.tile([P, len(passes), width * PACK], BF16, name="z", tag="z", bufs=3, align_bytes=64)
-            else:
-                z = keep.tile([P, len(passes), width * PACK], BF16, name="z", tag=after, align_bytes=64)
-            for place, b in enumerate(passes):
-                for s0 in range(0, width, SUB):
-                    cs_codes, cs_scales = cs_operand[m0 + s0]
-                    c = psum.tile([P, PACK, SUB], F32, name="c", tag="proj")
-                    for t in range(PACK):
-                        nc.tensor.matmul_mx(
-                            out=c[:, t, :],
-                            lhsT=wc_codes[b][:, P * t : P * (t + 1)].bitcast(FP8X4),
-                            lhsT_scale=wc_scales[b][:, P * t : P * (t + 1)],
-                            rhs=cs_codes.bitcast(FP8X4),
-                            rhs_scale=cs_scales,
-                            start=True,
-                            stop=True,
-                        )
-                    nc.vector.tensor_tensor(
-                        z[:, place, PACK * s0 : PACK * (s0 + SUB)].rearrange("p (g i t) -> p g t i", i=4, t=PACK),
-                        c[:].rearrange("p t (g i) -> p g t i", i=4),
-                        x[b][:, :, m0 + s0 : m0 + s0 + SUB].rearrange("p t (g i) -> p g t i", i=4),
-                        ALU.max,
-                    )
-            return z, passes, m0, width
+        def z_tile(pieces, used_up):
+            tile = reuse([P, PACK * sum(width for b, m0, width in pieces)], BF16, "z", used_up)
+            places, column = {}, 0
+            for b, m0, width in pieces:
+                places[b, m0] = (column, width)
+                column = column + width
+            return tile, places
 
-        def quantise_z(z, passes, m0, width):
-            codes = held([P, len(passes) * width], U32, "z_codes%d_%d" % (passes[0], m0))
-            scales = held([P, len(passes) * width], U8, "z_scales%d_%d" % (passes[0], m0))
-            quantise(codes[:], scales[:], z[:].rearrange("p a w -> p (a w)"))
-            for place, b in enumerate(passes):
+        def maxima(z, b, m0):
+            tile, places = z
+            column, width = places[b, m0]
+            strongest(tile[:, PACK * column : PACK * (column + width)], b, m0)
+
+        def quantise_z(z, used_up=None):
+            tile, places = z
+            columns = tile.shape[1] // PACK
+            name = "z%d_%d" % min(places)
+            codes = reuse([P, columns], U32, name + "_codes", used_up or name + "_codes")
+            scales = held([P, columns], U8, name + "_scales")
+            quantise(codes[:], scales[:], tile[:])
+            for b, m0 in places:
+                column, width = places[b, m0]
                 for s0 in range(0, width, SUB):
-                    z_operand[b, m0 + s0] = (codes, scales, place * width + s0)
+                    z_operand[b, m0 + s0] = (codes, scales, column + s0)
 
         out_rows = out.rearrange("(o p) m -> p o m", p=P)
         residual = []
 
-        def update(m0, width, tiles_per_bank):
-            half, c0 = divmod(m0, HALF)
-            for o0 in range(0, OUT_TILES, tiles_per_bank):
-                y = psum.tile([P, tiles_per_bank, width], F32, name="y", tag="wide")
-                for b in range(PASSES):
-                    for o in range(o0, o0 + tiles_per_bank):
-                        codes, scales, z0 = z_operand[b, m0]
-                        nc.tensor.matmul_mx(
-                            out=y[:, o - o0, :],
-                            lhsT=w2_word_tile[:, b, P * o : P * (o + 1)].bitcast(FP8X4),
-                            lhsT_scale=w2_scale_tile[:, b, P * o : P * (o + 1)],
-                            rhs=codes[:, z0 : z0 + width].bitcast(FP8X4),
-                            rhs_scale=scales[:, z0 : z0 + width],
-                            start=(b == 0 and o == o0),
-                            stop=(b == PASSES - 1 and o == o0 + tiles_per_bank - 1),
-                        )
-                result = ring.tile([P, tiles_per_bank, width], F32, name="result", tag="result", bufs=RESULT_BANKS)
-                states = residual[half][:, o0 : o0 + tiles_per_bank, c0 : c0 + width]
-                target = out_rows[:, o0 : o0 + tiles_per_bank, m0 : m0 + width]
-                if m0 < HALF:
-                    nc.scalar.copy(result[:], y[:])
-                    for o in range(tiles_per_bank):
-                        nc.gpsimd.tensor_tensor(result[:, o, :], result[:, o, :], states[:, o, :], ALU.add)
-                        nc.sync.dma_start(target[:, o, :], result[:, o, :])
-                elif m0 == HALF:
-                    nc.vector.tensor_tensor(result[:], y[:], states, ALU.add)
-                    nc.scalar.dma_start(target, result[:])
-                else:
-                    for o in range(tiles_per_bank):
-                        nc.vector.tensor_tensor(result[:, o, :], y[:, o, :], states[:, o, :], ALU.add)
-                        nc.scalar.dma_start(target[:, o, :], result[:, o, :])
+        def product(m0, width, o0):
+            tiles = BANK // width
+            y = psum.tile([P, tiles, width], F32, name="y", tag="wide")
+            for b in range(PASSES):
+                for o in range(o0, o0 + tiles):
+                    codes, scales, z0 = z_operand[b, m0]
+                    nc.tensor.matmul_mx(
+                        out=y[:, o - o0, :],
+                        lhsT=w2_word_tile[:, b, P * o : P * (o + 1)].bitcast(FP8X4),
+                        lhsT_scale=w2_scale_tile[:, b, P * o : P * (o + 1)],
+                        rhs=codes[:, z0 : z0 + width].bitcast(FP8X4),
+                        rhs_scale=scales[:, z0 : z0 + width],
+                        start=(b == 0 and o == o0),
+                        stop=(b == PASSES - 1 and o == o0 + tiles - 1),
+                    )
+            return y
+
+        def result_tile(shape):
+            return ring.tile(shape, F32, name="result", tag="result", bufs=RESULT_BANKS)
+
+        def update_on_gpsimd(m0, width):
+            tiles = BANK // width
+            for o0 in range(0, OUT_TILES, tiles):
+                y = product(m0, width, o0)
+                result = result_tile([P, tiles, width])
+                nc.scalar.copy(result[:], y[:])
+                for r0 in range(0, tiles, tiles // 2):
+                    rows = slice(r0, r0 + tiles // 2)
+                    out_tiles = slice(o0 + r0, o0 + r0 + tiles // 2)
+                    states = residual[m0 // HALF][:, out_tiles, m0 % HALF : m0 % HALF + width]
+                    nc.gpsimd.tensor_tensor(result[:, rows, :], result[:, rows, :], states, ALU.add)
+                    nc.sync.dma_start(out_rows[:, out_tiles, m0 : m0 + width], result[:, rows, :])
+
+        def update_on_vector(m0, width, o0, y, pieces):
+            tiles = BANK // width
+            result = result_tile([P, tiles, width])
+            step = tiles // pieces
+            for r0 in range(0, tiles, step):
+                rows = slice(r0, r0 + step)
+                out_tiles = slice(o0 + r0, o0 + r0 + step)
+                states = residual[m0 // HALF][:, out_tiles, m0 % HALF : m0 % HALF + width]
+                nc.vector.tensor_tensor(result[:, rows, :], y[:, rows, :], states, ALU.add)
+                nc.scalar.dma_start(out_rows[:, out_tiles, m0 : m0 + width], result[:, rows, :])
 
         for chunk in range(LITERAL_CHUNKS):
             entries = literal_list[:, chunk * BANK // LIST_ROWS : (chunk + 1) * BANK // LIST_ROWS]
@@ -242,43 +271,60 @@ def tile_list_clause_state_round_kernel(
             messages(1, [chunk])
 
         all_chunks = range(LITERAL_CHUNKS)
-        quantise_cs(0, QUARTER, apply_gain(0, QUARTER, "gained0"), "interleaved0")
-        gained = apply_gain(QUARTER, QUARTER, "gained1")
+        q0, q1, q2, q3 = range(0, M, QUARTER)
+        run = QUARTER * PACK
+        quantise_cs(q0, interleave_cs(nc.vector.tensor_copy, gain_on_gpsimd(q0, "gained0")[:], "interleaved0"))
+        gained1 = gain_on_gpsimd(q1, "gained1")
         pick(0)
         pick(1)
-        for row_tile in (2, 3, 4):
+        cs_plain = cs.rearrange("(o p) m -> p o m", p=P)
+        for half, used_up in enumerate(("table_words", "h0")):
+            residual.append(reuse([P, OUT_TILES, HALF], F32, "residual", used_up))
+            nc.sync.dma_start(residual[half][:], cs_plain[:, :, half * HALF : (half + 1) * HALF])
+        for row_tile in range(2, 7):
             messages(row_tile, all_chunks)
             pick(row_tile)
-
-        messages(5, all_chunks[:-1])
-        quantise_wc(0)
-        messages(5, all_chunks[-1:])
-        pick(5)
-        quantise_cs(QUARTER, QUARTER, gained, "h3")
-
-        cs_plain = cs.rearrange("(o p) m -> p o m", p=P)
-        for half, used_up in enumerate(("table_words", "wc_raw0")):
-            residual.append(keep.tile([P, OUT_TILES, HALF], F32, name="residual", tag=used_up, align_bytes=64))
-            nc.sync.dma_start(residual[half][:], cs_plain[:, :, half * HALF : (half + 1) * HALF])
-
-        gained = apply_gain(HALF, HALF, "h5")
-        messages(6, all_chunks)
-        quantise_z(*strongest((0,), 0, HALF, "h3"))
-        pick(6)
         messages(7, all_chunks[:-1])
-        quantise_wc(1)
+        quantise(wc_codes[0][:], wc_scales[0][:], interleave_wc(0)[:])
         messages(7, all_chunks[-1:])
         pick(7)
 
-        quantise_cs(HALF, HALF, gained, "h6")
-        for m0 in (0, QUARTER):
-            quantise_z(*strongest((1,), m0, QUARTER))
-            update(m0, QUARTER, 2)
-        third = strongest((0, 1), HALF, QUARTER)
-        fourth = strongest((0,), HALF + QUARTER, QUARTER)
-        quantise_z(*third)
-        quantise_z(*fourth)
-        fourth = strongest((1,), HALF + QUARTER, QUARTER)
-        update(HALF, QUARTER, 2)
-        quantise_z(*fourth)
-        update(HALF + QUARTER, QUARTER, 2)
+        e4, e5, e6, e7 = range(HALF, M, SUB)
+        wc_interleaved = interleave_wc(1)
+        z = z_tile([(0, q0, QUARTER)], "h1")
+        maxima(z, 0, q0)
+        quantise(wc_codes[1][:], wc_scales[1][:], wc_interleaved[:])
+        quantise_z(z, "wc_raw1")
+        quantise_cs(q1, interleave_cs(nc.scalar.copy, gained1[:], "h2"))
+        gained = reuse([P, PACK, HALF], BF16, "gained", "h5")
+        for j in range(PACK):
+            nc.scalar.activation(gained[:, j, :], cs_raw[HALF][:, j, :], ACT.Copy, scale=gain[:, j : j + 1])
+        second_half = interleave_cs(nc.scalar.copy, gained[:], "h3")
+
+        z = z_tile([(1, q0, QUARTER), (0, q1, QUARTER)], "gained1")
+        maxima(z, 1, q0)
+        maxima(z, 0, q1)
+        quantise_cs(q2, second_half)
+        quantise_z(z)
+
+        z = z_tile([(1, q1, QUARTER), (0, q2, QUARTER)], "h4")
+        following = z_tile([(1, e4, SUB), (1, e5, SUB), (0, q3, QUARTER)], "h6")
+        maxima(z, 1, q1)
+        maxima(z, 0, q2)
+        maxima(following, 1, e4)
+        update_on_gpsimd(q0, QUARTER)
+        quantise_z(z)
+
+        z = following
+        last = z_tile([(1, e6, SUB), (1, e7, SUB)], "h7")
+        maxima(z, 1, e5)
+        maxima(z, 0, q3)
+        maxima(last, 1, e6)
+        quantise_z(z)
+        maxima(last, 1, e7)
+        update_on_gpsimd(q1, QUARTER)
+        update_on_vector(q2, QUARTER, 0, product(q2, QUARTER, 0), 1)
+        quantise_z(last)
+        update_on_vector(q2, QUARTER, 2, product(q2, QUARTER, 2), 1)
+        update_on_vector(q3, QUARTER, 0, product(q3, QUARTER, 0), 2)
+        update_on_vector(q3, QUARTER, 2, product(q3, QUARTER, 2), 2)

@@ -62,8 +62,9 @@ def tile_list_clause_state_round_kernel(
         gain = held([P, PACK], F32, "gain")
         weight = held([P, M], F32, "weight")
 
-        nc.gpsimd.memset(wl_scales_raw[:].bitcast(I32), 0)
-        nc.vector.memset(table_scales[:].bitcast(I32), 0)
+        nc.gpsimd.memset(table_scales[:, 0 : T // 2].bitcast(I32), 0)
+        nc.vector.memset(wl_scales_raw[:].bitcast(I32), 0)
+        nc.vector.memset(table_scales[:, T // 2 : T].bitcast(I32), 0)
         v_scales = held([P, S], U8, "v_scales")
         nc.gpsimd.dma_start(bias[:], bl.rearrange("(b p t) -> p b t", b=PASSES, t=PACK))
         nc.gpsimd.dma_start(gain[:], gc.rearrange("(p j) -> p j", j=PACK))
@@ -289,40 +290,37 @@ def tile_list_clause_state_round_kernel(
         messages(7, all_chunks[-1:])
         pick(7)
 
-        e4, e5, e6, e7 = range(HALF, M, SUB)
-        wc_interleaved = interleave_wc(1)
-        z = z_tile([(0, q0, QUARTER)], "h1")
+        e6, e7 = range(q3, M, SUB)
+        quantise(wc_codes[1][:], wc_scales[1][:], interleave_wc(1)[:])
+        z = z_tile([(0, q0, QUARTER), (1, q0, QUARTER)], "wc_raw1")
         maxima(z, 0, q0)
-        quantise(wc_codes[1][:], wc_scales[1][:], wc_interleaved[:])
-        quantise_z(z, "wc_raw1")
+        maxima(z, 1, q0)
         quantise_cs(q1, interleave_cs(nc.scalar.copy, gained1[:], "h2"))
+        quantise_z(z)
         gained = reuse([P, PACK, HALF], BF16, "gained", "h5")
         for j in range(PACK):
             nc.scalar.activation(gained[:, j, :], cs_raw[HALF][:, j, :], ACT.Copy, scale=gain[:, j : j + 1])
         second_half = interleave_cs(nc.scalar.copy, gained[:], "h3")
 
-        z = z_tile([(1, q0, QUARTER), (0, q1, QUARTER)], "gained1")
-        maxima(z, 1, q0)
+        z = z_tile([(0, q1, QUARTER), (1, q1, QUARTER)], "h4")
         maxima(z, 0, q1)
+        maxima(z, 1, q1)
+        update_on_gpsimd(q0, QUARTER)
         quantise_cs(q2, second_half)
         quantise_z(z)
 
-        z = z_tile([(1, q1, QUARTER), (0, q2, QUARTER)], "h4")
-        following = z_tile([(1, e4, SUB), (1, e5, SUB), (0, q3, QUARTER)], "h6")
-        maxima(z, 1, q1)
-        maxima(z, 0, q2)
-        maxima(following, 1, e4)
-        update_on_gpsimd(q0, QUARTER)
-        quantise_z(z)
-
-        z = following
+        z = z_tile([(0, q2, QUARTER), (1, q2, QUARTER)], "h6")
+        following = z_tile([(0, e6, SUB), (0, e7, SUB)], "h1")
         last = z_tile([(1, e6, SUB), (1, e7, SUB)], "h7")
-        maxima(z, 1, e5)
-        maxima(z, 0, q3)
-        maxima(last, 1, e6)
-        quantise_z(z)
-        maxima(last, 1, e7)
+        maxima(z, 0, q2)
+        maxima(z, 1, q2)
+        maxima(following, 0, e6)
         update_on_gpsimd(q1, QUARTER)
+        quantise_z(z)
+        maxima(following, 0, e7)
+        maxima(last, 1, e6)
+        quantise_z(following)
+        maxima(last, 1, e7)
         update_on_vector(q2, QUARTER, 0, product(q2, QUARTER, 0), 1)
         quantise_z(last)
         update_on_vector(q2, QUARTER, 2, product(q2, QUARTER, 2), 1)

@@ -241,9 +241,9 @@ def tile_list_clause_state_round_kernel(
         def result_tile(shape):
             return ring.tile(shape, F32, name="result", tag="result", bufs=RESULT_BANKS)
 
-        def update_on_gpsimd(m0, width):
+        def update_on_gpsimd(m0, width, out_end=OUT_TILES):
             tiles = BANK // width
-            for o0 in range(0, OUT_TILES, tiles):
+            for o0 in range(0, out_end, tiles):
                 y = product(m0, width, o0)
                 result = result_tile([P, tiles, width])
                 nc.scalar.copy(result[:], y[:])
@@ -290,20 +290,23 @@ def tile_list_clause_state_round_kernel(
         messages(7, all_chunks[-1:])
         pick(7)
 
+        e2, e3 = range(q1, q2, SUB)
         e6, e7 = range(q3, M, SUB)
         quantise(wc_codes[1][:], wc_scales[1][:], interleave_wc(1)[:])
         z = z_tile([(0, q0, QUARTER), (1, q0, QUARTER)], "wc_raw1")
         maxima(z, 0, q0)
-        maxima(z, 1, q0)
         quantise_cs(q1, interleave_cs(nc.scalar.copy, gained1[:], "h2"))
+        maxima(z, 1, q0)
+        following = z_tile([(0, e2, SUB), (0, e3, SUB), (1, q1, QUARTER)], "h4")
+        maxima(following, 0, e2)
         quantise_z(z)
         gained = reuse([P, PACK, HALF], BF16, "gained", "h5")
         for j in range(PACK):
             nc.scalar.activation(gained[:, j, :], cs_raw[HALF][:, j, :], ACT.Copy, scale=gain[:, j : j + 1])
         second_half = interleave_cs(nc.scalar.copy, gained[:], "h3")
 
-        z = z_tile([(0, q1, QUARTER), (1, q1, QUARTER)], "h4")
-        maxima(z, 0, q1)
+        z = following
+        maxima(z, 0, e3)
         maxima(z, 1, q1)
         update_on_gpsimd(q0, QUARTER)
         quantise_cs(q2, second_half)
@@ -319,9 +322,9 @@ def tile_list_clause_state_round_kernel(
         quantise_z(z)
         maxima(following, 0, e7)
         maxima(last, 1, e6)
-        quantise_z(following)
         maxima(last, 1, e7)
-        update_on_vector(q2, QUARTER, 0, product(q2, QUARTER, 0), 1)
+        update_on_gpsimd(q2, QUARTER, 2)
+        quantise_z(following)
         quantise_z(last)
         update_on_vector(q2, QUARTER, 2, product(q2, QUARTER, 2), 1)
         update_on_vector(q3, QUARTER, 0, product(q3, QUARTER, 0), 2)

@@ -62,18 +62,20 @@ def tile_list_clause_state_round_kernel(
         gain = held([P, PACK], F32, "gain")
         weight = held([P, M], F32, "weight")
 
+        nc.gpsimd.memset(wl_scales_raw[:].bitcast(I32), 0)
         nc.gpsimd.memset(table_scales[:, 0 : T // 2].bitcast(I32), 0)
-        nc.vector.memset(wl_scales_raw[:].bitcast(I32), 0)
         nc.vector.memset(table_scales[:, T // 2 : T].bitcast(I32), 0)
-        v_scales = held([P, S], U8, "v_scales")
+        v_scales = [held([P, S // 2], U8, "v_scales%d" % half) for half in range(2)]
         nc.gpsimd.dma_start(bias[:], bl.rearrange("(b p t) -> p b t", b=PASSES, t=PACK))
         nc.gpsimd.dma_start(gain[:], gc.rearrange("(p j) -> p j", j=PACK))
+        for half in range(2):
+            nc.gpsimd.memset(v_scales[half][:].bitcast(I32), 0)
         nc.gpsimd.memset(w2_scale_tile[:].rearrange("p a n -> p (a n)").bitcast(I32), 0)
 
         nc.sync.dma_start(literal_list[:], offs)
         nc.sync.dma_start(wl_words_raw[:].bitcast(I32), wl_words[0].bitcast(I32))
-        nc.sync.dma_start(wl_scales_raw[0 : 4 * QUADRANTS].bitcast(I32), wl_scales[0].bitcast(I32))
-        load_scale_rows(table_scales[:], tab_scales[0])
+        load_scale_rows(wl_scales_raw[:], wl_scales[0])
+        nc.sync.dma_start(table_scales[0:P:8].bitcast(I32), tab_scales[0].bitcast(I32))
         nc.sync.dma_start(table_words[:], tab_words[0].rearrange("p t i -> p (t i)").bitcast(I32))
 
         wl_word_tile = held([P, 2 * H], U8, "wl_word_tile")
@@ -86,12 +88,17 @@ def tile_list_clause_state_round_kernel(
             wl_scale_tile[:].rearrange("k (b t p) -> k b t p", b=PASSES, t=PACK),
             wl_scales_raw[:].rearrange("k (b p t) -> k b t p", b=PASSES, t=PACK),
         )
-        for q in range(1, QUADRANTS):
-            nc.sync.dma_start(
-                wl_scale_tile[32 * q : 32 * q + 4].bitcast(I32), wl_scale_tile[4 * q : 4 * q + 4].bitcast(I32)
-            )
 
-        nc.vector.tensor_copy(v_scales[:], table_scales[:].indirect(literal_list[:]))
+        gathered = [held([P, S // 2], U8, "gathered_scales%d" % half) for half in range(2)]
+        for half in range(2):
+            entries = literal_list[:, half * S // 2 // LIST_ROWS : (half + 1) * S // 2 // LIST_ROWS]
+            nc.vector.tensor_copy(gathered[half][:], table_scales[:].indirect(entries))
+
+        def carry_scale_rows(queue, half):
+            for r in range(4):
+                queue.dma_start(v_scales[half][r:P:32].bitcast(I32), gathered[half][8 * r : P : 32].bitcast(I32))
+
+        carry_scale_rows(nc.scalar, 0)
 
         wc_rows = wc.rearrange("(p j) r -> p j r", j=PACK)
         cs_rows = cs.rearrange("(p j) m -> p j m", j=PACK)
@@ -99,6 +106,7 @@ def tile_list_clause_state_round_kernel(
         cs_raw = {m0: held([P, PACK, width], F32, "cs_raw%d" % m0) for m0, width in CS_RANGES}
         nc.sync.dma_start(cs_raw[0][:], cs_rows[:, :, 0:QUARTER])
         nc.sync.dma_start(cs_raw[QUARTER][:], cs_rows[:, :, QUARTER:HALF])
+        carry_scale_rows(nc.sync, 1)
         nc.sync.dma_start(slot_lists[:], offs2)
         nc.sync.dma_start(weight[:], wgt)
         nc.sync.dma_start(wc_raw[0][:], wc_rows[:, :, 0:HALF])
@@ -120,7 +128,7 @@ def tile_list_clause_state_round_kernel(
                     lhsT=wl_word_tile[:, 2 * P * row_tile : 2 * P * (row_tile + 1)].bitcast(FP4X4),
                     lhsT_scale=wl_scale_tile[:, P * row_tile : P * (row_tile + 1)],
                     rhs=v_words[chunk][:].bitcast(FP8X4),
-                    rhs_scale=v_scales[:, literals],
+                    rhs_scale=v_scales[chunk // 2][:, BANK * (chunk % 2) : BANK * (chunk % 2 + 1)],
                     start=True,
                     stop=True,
                 )

@@ -28,6 +28,7 @@ SUB = BANK // PACK
 HALF = M // 2
 QUARTER = M // 4
 CS_RANGES = ((0, QUARTER), (QUARTER, QUARTER), (HALF, HALF))
+SPARE = P - 4 * QUADRANTS
 RESULT_BANKS = 8
 
 
@@ -43,9 +44,12 @@ def tile_list_clause_state_round_kernel(
         def held(shape, dtype, name):
             return keep.tile(shape, dtype, name=name, tag=name, align_bytes=64)
 
-        def load_scale_rows(tile, rows):
+        def reuse(shape, dtype, name, used_up):
+            return keep.tile(shape, dtype, name=name, tag=used_up, align_bytes=64)
+
+        def load_scale_rows(queue, tile, rows):
             for r in range(4):
-                nc.sync.dma_start(tile[r:P:32].bitcast(I32), rows[r : 4 * QUADRANTS : 4].bitcast(I32))
+                queue.dma_start(tile[r:P:32].bitcast(I32), rows[r : 4 * QUADRANTS : 4].bitcast(I32))
 
         def quantise(codes, scales, values):
             nc.vector.quantize_mx(out=codes.bitcast(FP8X4), scales=scales, in_=values)
@@ -56,38 +60,31 @@ def tile_list_clause_state_round_kernel(
         table_words = held([P, T], I32, "table_words")
         wl_words_raw = held([P, 2 * H], U8, "wl_words_raw")
         wl_scales_raw = held([P, H], U8, "wl_scales_raw")
-        w2_scale_tile = held([P, PASSES, N], U8, "w2_scale_tile")
-        w2_word_tile = held([P, PASSES, N], I32, "w2_word_tile")
         bias = held([P, PASSES, PACK], F32, "bias")
         gain = held([P, PACK], F32, "gain")
-        weight = held([P, M], F32, "weight")
 
-        nc.gpsimd.memset(wl_scales_raw[:].bitcast(I32), 0)
-        nc.gpsimd.memset(table_scales[:, 0 : T // 2].bitcast(I32), 0)
-        nc.vector.memset(table_scales[:, T // 2 : T].bitcast(I32), 0)
+        nc.vector.memset(wl_scales_raw[:].bitcast(I32), 0)
+        nc.gpsimd.memset(table_scales[0:SPARE, 0 : T // 2].bitcast(I32), 0)
+        nc.vector.memset(table_scales[0:SPARE, T // 2 : T].bitcast(I32), 0)
         v_scales = [held([P, S // 2], U8, "v_scales%d" % half) for half in range(2)]
         nc.gpsimd.dma_start(bias[:], bl.rearrange("(b p t) -> p b t", b=PASSES, t=PACK))
         nc.gpsimd.dma_start(gain[:], gc.rearrange("(p j) -> p j", j=PACK))
         for half in range(2):
-            nc.gpsimd.memset(v_scales[half][:].bitcast(I32), 0)
-        nc.gpsimd.memset(w2_scale_tile[:].rearrange("p a n -> p (a n)").bitcast(I32), 0)
+            nc.vector.memset(v_scales[half][:].bitcast(I32), 0)
 
         nc.sync.dma_start(literal_list[:], offs)
+        nc.sync.dma_start(table_scales[SPARE:P].bitcast(I32), tab_scales[0].bitcast(I32))
         nc.sync.dma_start(wl_words_raw[:].bitcast(I32), wl_words[0].bitcast(I32))
-        load_scale_rows(wl_scales_raw[:], wl_scales[0])
-        nc.sync.dma_start(table_scales[0:P:8].bitcast(I32), tab_scales[0].bitcast(I32))
+        load_scale_rows(nc.scalar, wl_scales_raw[:], wl_scales[0])
         nc.sync.dma_start(table_words[:], tab_words[0].rearrange("p t i -> p (t i)").bitcast(I32))
 
-        wl_word_tile = held([P, 2 * H], U8, "wl_word_tile")
-        wl_scale_tile = held([P, H], U8, "wl_scale_tile")
-        nc.vector.tensor_copy(
-            wl_word_tile[:].bitcast(U16).rearrange("k (b t p) -> k b t p", b=PASSES, t=PACK),
-            wl_words_raw[:].bitcast(U16).rearrange("k (b p t) -> k b t p", b=PASSES, t=PACK),
-        )
-        nc.vector.tensor_copy(
-            wl_scale_tile[:].rearrange("k (b t p) -> k b t p", b=PASSES, t=PACK),
-            wl_scales_raw[:].rearrange("k (b p t) -> k b t p", b=PASSES, t=PACK),
-        )
+        wl_word_tile = [held([P, PACK, P, 2], U8, "wl_word_tile%d" % b) for b in range(PASSES)]
+        wl_scale_tile = [held([P, PACK, P], U8, "wl_scale_tile%d" % b) for b in range(PASSES)]
+        wl_words_dealt = wl_words_raw[:].rearrange("k (b p t e) -> k b t e p", b=PASSES, t=PACK, e=2)
+        wl_scales_dealt = wl_scales_raw[:].rearrange("k (b p t) -> k b t p", b=PASSES, t=PACK)
+        for b in range(PASSES):
+            nc.gpsimd.tensor_copy(wl_word_tile[b][:].rearrange("k t p e -> k t e p"), wl_words_dealt[:, b])
+            nc.gpsimd.tensor_copy(wl_scale_tile[b][:], wl_scales_dealt[:, b])
 
         gathered = [held([P, S // 2], U8, "gathered_scales%d" % half) for half in range(2)]
         for half in range(2):
@@ -96,24 +93,23 @@ def tile_list_clause_state_round_kernel(
 
         def carry_scale_rows(queue, half):
             for r in range(4):
-                queue.dma_start(v_scales[half][r:P:32].bitcast(I32), gathered[half][8 * r : P : 32].bitcast(I32))
+                queue.dma_start(v_scales[half][r:P:32].bitcast(I32), gathered[half][SPARE + r : P : 4].bitcast(I32))
 
-        carry_scale_rows(nc.scalar, 0)
 
         wc_rows = wc.rearrange("(p j) r -> p j r", j=PACK)
         cs_rows = cs.rearrange("(p j) m -> p j m", j=PACK)
-        wc_raw = [held([P, PACK, HALF], F32, "wc_raw%d" % b) for b in range(PASSES)]
-        cs_raw = {m0: held([P, PACK, width], F32, "cs_raw%d" % m0) for m0, width in CS_RANGES}
-        nc.sync.dma_start(cs_raw[0][:], cs_rows[:, :, 0:QUARTER])
-        nc.sync.dma_start(cs_raw[QUARTER][:], cs_rows[:, :, QUARTER:HALF])
-        carry_scale_rows(nc.sync, 1)
+        cs_raw = {0: held([P, PACK, QUARTER], F32, "cs_raw0")[:]}
+        nc.sync.dma_start(cs_raw[0], cs_rows[:, :, 0:QUARTER])
         nc.sync.dma_start(slot_lists[:], offs2)
-        nc.sync.dma_start(weight[:], wgt)
+        carry_scale_rows(nc.sync, 0)
+        carry_scale_rows(nc.sync, 1)
+        states_and_weight = reuse([P, 2, M], F32, "states_and_weight", "table_scales")
+        cs_raw[QUARTER] = states_and_weight[:, 0, :].rearrange("p (j m) -> p j m", j=PACK)
+        weight = states_and_weight[:, 1, :]
+        nc.sync.dma_start(cs_raw[QUARTER], cs_rows[:, :, QUARTER:HALF])
+        nc.sync.dma_start(weight, wgt)
+        wc_raw = [reuse([P, PACK, HALF], F32, "wc_raw0", "gathered_scales0")]
         nc.sync.dma_start(wc_raw[0][:], wc_rows[:, :, 0:HALF])
-        nc.sync.dma_start(cs_raw[HALF][:], cs_rows[:, :, HALF:M])
-        nc.sync.dma_start(wc_raw[1][:], wc_rows[:, :, HALF:H])
-        nc.sync.dma_start(w2_word_tile[:], w2_words.rearrange("a p n i -> p a (n i)").bitcast(I32))
-        load_scale_rows(w2_scale_tile[:], w2_scales.rearrange("a q n -> q a n"))
 
         v_words = [held([P, BANK], U32, "v_words%d" % chunk) for chunk in range(LITERAL_CHUNKS)]
         h = [held([P, S], F32, "h%d" % row_tile) for row_tile in range(PASSES * PACK)]
@@ -125,17 +121,14 @@ def tile_list_clause_state_round_kernel(
                 acc = psum.tile([P, BANK], F32, name="acc", tag="wide")
                 nc.tensor.matmul_mx(
                     out=acc[:],
-                    lhsT=wl_word_tile[:, 2 * P * row_tile : 2 * P * (row_tile + 1)].bitcast(FP4X4),
-                    lhsT_scale=wl_scale_tile[:, P * row_tile : P * (row_tile + 1)],
+                    lhsT=wl_word_tile[b][:, t].rearrange("k p e -> k (p e)").bitcast(FP4X4),
+                    lhsT_scale=wl_scale_tile[b][:, t],
                     rhs=v_words[chunk][:].bitcast(FP8X4),
                     rhs_scale=v_scales[chunk // 2][:, BANK * (chunk % 2) : BANK * (chunk % 2 + 1)],
                     start=True,
                     stop=True,
                 )
                 nc.scalar.activation(h[row_tile][:, literals], acc[:], ACT.Identity, bias=bias[:, b, t : t + 1])
-
-        def reuse(shape, dtype, name, used_up):
-            return keep.tile(shape, dtype, name=name, tag=used_up, align_bytes=64)
 
         wc_codes = [held([P, HALF], U32, "wc_codes%d" % b) for b in range(PASSES)]
         wc_scales = [held([P, HALF], U8, "wc_scales%d" % b) for b in range(PASSES)]
@@ -176,7 +169,7 @@ def tile_list_clause_state_round_kernel(
 
         def pick(row_tile):
             b, t = divmod(row_tile, PACK)
-            nc.vector.tensor_tensor(x[b][:, t, :], h[row_tile][:].indirect(slot_lists[:]), weight[:], ALU.mult)
+            nc.vector.tensor_tensor(x[b][:, t, :], h[row_tile][:].indirect(slot_lists[:]), weight, ALU.mult)
 
         def strongest(z, b, m0):
             for s0 in range(0, z.shape[1] // PACK, SUB):
@@ -284,6 +277,15 @@ def tile_list_clause_state_round_kernel(
         run = QUARTER * PACK
         quantise_cs(q0, interleave_cs(nc.vector.tensor_copy, gain_on_gpsimd(q0, "gained0")[:], "interleaved0"))
         gained1 = gain_on_gpsimd(q1, "gained1")
+        wc_raw.append(reuse([P, PACK, HALF], F32, "wc_raw1", "gathered_scales1"))
+        nc.sync.dma_start(wc_raw[1][:], wc_rows[:, :, HALF:H])
+        cs_raw[HALF] = reuse([P, PACK, HALF], F32, "cs_raw2", "gained0")
+        nc.sync.dma_start(cs_raw[HALF][:], cs_rows[:, :, HALF:M])
+        w2_word_tile = reuse([P, PASSES, N], I32, "w2_word_tile", "interleaved0")
+        nc.sync.dma_start(w2_word_tile[:], w2_words.rearrange("a p n i -> p a (n i)").bitcast(I32))
+        w2_scale_tile = reuse([P, PASSES, N], U8, "w2_scale_tile", "cs_raw0")
+        nc.gpsimd.memset(w2_scale_tile[:].rearrange("p a n -> p (a n)").bitcast(I32), 0)
+        load_scale_rows(nc.sync, w2_scale_tile[:], w2_scales.rearrange("a q n -> q a n"))
         pick(0)
         pick(1)
         cs_plain = cs.rearrange("(o p) m -> p o m", p=P)
@@ -301,7 +303,7 @@ def tile_list_clause_state_round_kernel(
         e2, e3 = range(q1, q2, SUB)
         e6, e7 = range(q3, M, SUB)
         quantise(wc_codes[1][:], wc_scales[1][:], interleave_wc(1)[:])
-        z = z_tile([(0, q0, QUARTER), (1, q0, QUARTER)], "wc_raw1")
+        z = z_tile([(0, q0, QUARTER), (1, q0, QUARTER)], "gathered_scales1")
         maxima(z, 0, q0)
         quantise_cs(q1, interleave_cs(nc.scalar.copy, gained1[:], "h2"))
         maxima(z, 1, q0)

@@ -47,8 +47,8 @@ def tile_list_clause_state_round_kernel(
         def reuse(shape, dtype, name, used_up):
             return keep.tile(shape, dtype, name=name, tag=used_up, align_bytes=64)
 
-        def load_scale_rows(queue, tile, rows):
-            for r in range(4):
+        def load_scale_rows(queue, tile, rows, which=range(4)):
+            for r in which:
                 queue.dma_start(tile[r:P:32].bitcast(I32), rows[r : 4 * QUADRANTS : 4].bitcast(I32))
 
         def quantise(codes, scales, values):
@@ -63,11 +63,11 @@ def tile_list_clause_state_round_kernel(
         bias = held([P, PASSES, PACK], F32, "bias")
         gain = held([P, PACK], F32, "gain")
 
+        nc.gpsimd.dma_start(bias[:], bl.rearrange("(b p t) -> p b t", b=PASSES, t=PACK))
         nc.vector.memset(wl_scales_raw[:].bitcast(I32), 0)
         nc.gpsimd.memset(table_scales[0:SPARE, 0 : T // 2].bitcast(I32), 0)
         nc.vector.memset(table_scales[0:SPARE, T // 2 : T].bitcast(I32), 0)
         v_scales = [held([P, S // 2], U8, "v_scales%d" % half) for half in range(2)]
-        nc.gpsimd.dma_start(bias[:], bl.rearrange("(b p t) -> p b t", b=PASSES, t=PACK))
         nc.gpsimd.dma_start(gain[:], gc.rearrange("(p j) -> p j", j=PACK))
         for half in range(2):
             nc.vector.memset(v_scales[half][:].bitcast(I32), 0)
@@ -75,21 +75,30 @@ def tile_list_clause_state_round_kernel(
         nc.sync.dma_start(literal_list[:], offs)
         nc.sync.dma_start(table_scales[SPARE:P].bitcast(I32), tab_scales[0].bitcast(I32))
         nc.sync.dma_start(wl_words_raw[:].bitcast(I32), wl_words[0].bitcast(I32))
-        load_scale_rows(nc.scalar, wl_scales_raw[:], wl_scales[0])
+        load_scale_rows(nc.sync, wl_scales_raw[:], wl_scales[0], range(2))
+        load_scale_rows(nc.scalar, wl_scales_raw[:], wl_scales[0], range(2, 4))
         nc.sync.dma_start(table_words[:], tab_words[0].rearrange("p t i -> p (t i)").bitcast(I32))
 
-        wl_word_tile = [held([P, PACK, P, 2], U8, "wl_word_tile%d" % b) for b in range(PASSES)]
-        wl_scale_tile = [held([P, PACK, P], U8, "wl_scale_tile%d" % b) for b in range(PASSES)]
-        wl_words_dealt = wl_words_raw[:].rearrange("k (b p t e) -> k b t e p", b=PASSES, t=PACK, e=2)
-        wl_scales_dealt = wl_scales_raw[:].rearrange("k (b p t) -> k b t p", b=PASSES, t=PACK)
-        for b in range(PASSES):
-            nc.gpsimd.tensor_copy(wl_word_tile[b][:].rearrange("k t p e -> k t e p"), wl_words_dealt[:, b])
-            nc.gpsimd.tensor_copy(wl_scale_tile[b][:], wl_scales_dealt[:, b])
+        wl_dealt = []
+
+        def deal_wl(b, tile):
+            words, scales = tile[:, 0 : 2 * HALF], tile[:, 2 * HALF : 3 * HALF]
+            nc.vector.tensor_copy(
+                words.bitcast(U16).rearrange("k (t p) -> k t p", t=PACK),
+                wl_words_raw[:, 2 * HALF * b : 2 * HALF * (b + 1)].bitcast(U16).rearrange("k (p t) -> k t p", t=PACK),
+            )
+            nc.vector.tensor_copy(
+                scales.rearrange("k (t p) -> k t p", t=PACK),
+                wl_scales_raw[:, HALF * b : HALF * (b + 1)].rearrange("k (p t) -> k t p", t=PACK),
+            )
+            wl_dealt.append((words, scales))
 
         gathered = [held([P, S // 2], U8, "gathered_scales%d" % half) for half in range(2)]
         for half in range(2):
             entries = literal_list[:, half * S // 2 // LIST_ROWS : (half + 1) * S // 2 // LIST_ROWS]
             nc.vector.tensor_copy(gathered[half][:], table_scales[:].indirect(entries))
+
+        deal_wl(0, held([P, 3 * HALF], U8, "wl_dealt0"))
 
         def carry_scale_rows(queue, half):
             for r in range(4):
@@ -121,8 +130,8 @@ def tile_list_clause_state_round_kernel(
                 acc = psum.tile([P, BANK], F32, name="acc", tag="wide")
                 nc.tensor.matmul_mx(
                     out=acc[:],
-                    lhsT=wl_word_tile[b][:, t].rearrange("k p e -> k (p e)").bitcast(FP4X4),
-                    lhsT_scale=wl_scale_tile[b][:, t],
+                    lhsT=wl_dealt[b][0][:, 2 * P * t : 2 * P * (t + 1)].bitcast(FP4X4),
+                    lhsT_scale=wl_dealt[b][1][:, P * t : P * (t + 1)],
                     rhs=v_words[chunk][:].bitcast(FP8X4),
                     rhs_scale=v_scales[chunk // 2][:, BANK * (chunk % 2) : BANK * (chunk % 2 + 1)],
                     start=True,
@@ -270,8 +279,11 @@ def tile_list_clause_state_round_kernel(
             entries = literal_list[:, chunk * BANK // LIST_ROWS : (chunk + 1) * BANK // LIST_ROWS]
             nc.vector.tensor_copy(v_words[chunk][:], table_words[:].bitcast(U32).indirect(entries))
             messages(0, [chunk])
-            messages(1, [chunk])
+            if chunk < LITERAL_CHUNKS // 2:
+                messages(1, [chunk])
+        messages(1, range(LITERAL_CHUNKS // 2, LITERAL_CHUNKS))
 
+        deal_wl(1, reuse([P, 3 * HALF], U8, "wl_dealt1", "table_words"))
         all_chunks = range(LITERAL_CHUNKS)
         q0, q1, q2, q3 = range(0, M, QUARTER)
         run = QUARTER * PACK
@@ -289,7 +301,7 @@ def tile_list_clause_state_round_kernel(
         pick(0)
         pick(1)
         cs_plain = cs.rearrange("(o p) m -> p o m", p=P)
-        for half, used_up in enumerate(("table_words", "h0")):
+        for half, used_up in enumerate(("wl_words_raw", "h0")):
             residual.append(reuse([P, OUT_TILES, HALF], F32, "residual", used_up))
             nc.sync.dma_start(residual[half][:], cs_plain[:, :, half * HALF : (half + 1) * HALF])
         for row_tile in range(2, 7):

@@ -111,11 +111,11 @@ def tile_list_clause_state_round_kernel(
         nc.sync.dma_start(cs_raw[0], cs_rows[:, :, 0:QUARTER])
         nc.sync.dma_start(slot_lists[:], offs2)
         carry_scale_rows(nc.sync, 0)
-        carry_scale_rows(nc.sync, 1)
         states_and_weight = reuse([P, 2, M], F32, "states_and_weight", "table_scales")
         cs_raw[QUARTER] = states_and_weight[:, 0, :].rearrange("p (j m) -> p j m", j=PACK)
         weight = states_and_weight[:, 1, :]
         nc.sync.dma_start(cs_raw[QUARTER], cs_rows[:, :, QUARTER:HALF])
+        carry_scale_rows(nc.sync, 1)
         nc.sync.dma_start(weight, wgt)
         wc_raw = [reuse([P, PACK, HALF], F32, "wc_raw0", "gathered_scales0")]
         nc.sync.dma_start(wc_raw[0][:], wc_rows[:, :, 0:HALF])

@@ -27,8 +27,10 @@ OUT_TILES = N // P
 SUB = BANK // PACK
 HALF = M // 2
 QUARTER = M // 4
-CS_RANGES = ((0, QUARTER), (QUARTER, QUARTER), (HALF, HALF))
-SPARE = P - 4 * QUADRANTS
+ROW_TILES = PASSES * PACK
+QUADRANT_ROWS = 4
+SPARE = P - QUADRANT_ROWS * QUADRANTS
+RUN = 4
 RESULT_BANKS = 8
 
 
@@ -38,7 +40,7 @@ def tile_list_clause_state_round_kernel(
     nc = tc.nc
     with ExitStack() as ctx:
         keep = ctx.enter_context(tc.tile_pool(name="keep", bufs=1))
-        ring = ctx.enter_context(tc.tile_pool(name="ring", bufs=2))
+        ring = ctx.enter_context(tc.tile_pool(name="ring", bufs=PASSES))
         psum = ctx.enter_context(tc.psum_pool(name="psum", bufs=4))
 
         def held(shape, dtype, name):
@@ -47,9 +49,9 @@ def tile_list_clause_state_round_kernel(
         def reuse(shape, dtype, name, used_up):
             return keep.tile(shape, dtype, name=name, tag=used_up, align_bytes=64)
 
-        def load_scale_rows(queue, tile, rows, which=range(4)):
-            for r in which:
-                queue.dma_start(tile[r:P:32].bitcast(I32), rows[r : 4 * QUADRANTS : 4].bitcast(I32))
+        def load_scale_rows(queue, tile, rows, places=range(QUADRANT_ROWS)):
+            for r in places:
+                queue.dma_start(tile[r:P:32].bitcast(I32), rows[r : QUADRANT_ROWS * QUADRANTS : QUADRANT_ROWS].bitcast(I32))
 
         def quantise(codes, scales, values):
             nc.vector.quantize_mx(out=codes.bitcast(FP8X4), scales=scales, in_=values)
@@ -75,8 +77,8 @@ def tile_list_clause_state_round_kernel(
         nc.sync.dma_start(literal_list[:], offs)
         nc.sync.dma_start(table_scales[SPARE:P].bitcast(I32), tab_scales[0].bitcast(I32))
         nc.sync.dma_start(wl_words_raw[:].bitcast(I32), wl_words[0].bitcast(I32))
-        load_scale_rows(nc.sync, wl_scales_raw[:], wl_scales[0], range(2))
-        load_scale_rows(nc.scalar, wl_scales_raw[:], wl_scales[0], range(2, 4))
+        load_scale_rows(nc.sync, wl_scales_raw[:], wl_scales[0], range(QUADRANT_ROWS // 2))
+        load_scale_rows(nc.scalar, wl_scales_raw[:], wl_scales[0], range(QUADRANT_ROWS // 2, QUADRANT_ROWS))
         nc.sync.dma_start(table_words[:], tab_words[0].rearrange("p t i -> p (t i)").bitcast(I32))
 
         wl_dealt = []
@@ -101,16 +103,16 @@ def tile_list_clause_state_round_kernel(
         deal_wl(0, held([P, 3 * HALF], U8, "wl_dealt0"))
 
         def carry_scale_rows(queue, half):
-            for r in range(4):
-                queue.dma_start(v_scales[half][r:P:32].bitcast(I32), gathered[half][SPARE + r : P : 4].bitcast(I32))
-
+            for r in range(QUADRANT_ROWS):
+                rows = gathered[half][SPARE + r : P : QUADRANT_ROWS]
+                queue.dma_start(v_scales[half][r:P:32].bitcast(I32), rows.bitcast(I32))
 
         wc_rows = wc.rearrange("(p j) r -> p j r", j=PACK)
         cs_rows = cs.rearrange("(p j) m -> p j m", j=PACK)
         cs_raw = {0: held([P, PACK, QUARTER], F32, "cs_raw0")[:]}
         nc.sync.dma_start(cs_raw[0], cs_rows[:, :, 0:QUARTER])
         nc.sync.dma_start(slot_lists[:], offs2)
-        carry_scale_rows(nc.sync, 0)
+        carry_scale_rows(nc.scalar, 0)
         states_and_weight = reuse([P, 2, M], F32, "states_and_weight", "table_scales")
         cs_raw[QUARTER] = states_and_weight[:, 0, :].rearrange("p (j m) -> p j m", j=PACK)
         weight = states_and_weight[:, 1, :]
@@ -121,7 +123,7 @@ def tile_list_clause_state_round_kernel(
         nc.sync.dma_start(wc_raw[0][:], wc_rows[:, :, 0:HALF])
 
         v_words = [held([P, BANK], U32, "v_words%d" % chunk) for chunk in range(LITERAL_CHUNKS)]
-        h = [held([P, S], F32, "h%d" % row_tile) for row_tile in range(PASSES * PACK)]
+        h = [held([P, S], F32, "h%d" % row_tile) for row_tile in range(ROW_TILES)]
 
         def messages(row_tile, chunks):
             b, t = divmod(row_tile, PACK)
@@ -159,8 +161,8 @@ def tile_list_clause_state_round_kernel(
         def interleave_cs(copy, gained, used_up):
             interleaved = reuse([P, gained.shape[2] * PACK], BF16, "cs_interleaved", used_up)
             copy(
-                interleaved[:].rearrange("p (g i j) -> p g j i", i=4, j=PACK),
-                gained.rearrange("p j (g i) -> p g j i", i=4),
+                interleaved[:].rearrange("p (g i j) -> p g j i", i=RUN, j=PACK),
+                gained.rearrange("p j (g i) -> p g j i", i=RUN),
             )
             return interleaved
 
@@ -195,9 +197,9 @@ def tile_list_clause_state_round_kernel(
                         stop=True,
                     )
                 nc.vector.tensor_tensor(
-                    z[:, PACK * s0 : PACK * (s0 + SUB)].rearrange("p (g i t) -> p g t i", i=4, t=PACK),
-                    c[:].rearrange("p t (g i) -> p g t i", i=4),
-                    x[b][:, :, m0 + s0 : m0 + s0 + SUB].rearrange("p t (g i) -> p g t i", i=4),
+                    z[:, PACK * s0 : PACK * (s0 + SUB)].rearrange("p (g i t) -> p g t i", i=RUN, t=PACK),
+                    c[:].rearrange("p t (g i) -> p g t i", i=RUN),
+                    x[b][:, :, m0 + s0 : m0 + s0 + SUB].rearrange("p t (g i) -> p g t i", i=RUN),
                     ALU.max,
                 )
 
@@ -216,11 +218,11 @@ def tile_list_clause_state_round_kernel(
             column, width = places[b, m0]
             strongest(tile[:, PACK * column : PACK * (column + width)], b, m0)
 
-        def quantise_z(z, used_up=None):
+        def quantise_z(z):
             tile, places = z
             columns = tile.shape[1] // PACK
             name = "z%d_%d" % min(places)
-            codes = reuse([P, columns], U32, name + "_codes", used_up or name + "_codes")
+            codes = held([P, columns], U32, name + "_codes")
             scales = held([P, columns], U8, name + "_scales")
             quantise(codes[:], scales[:], tile[:])
             for b, m0 in places:
@@ -275,20 +277,20 @@ def tile_list_clause_state_round_kernel(
                 nc.vector.tensor_tensor(result[:, rows, :], y[:, rows, :], states, ALU.add)
                 nc.scalar.dma_start(out_rows[:, out_tiles, m0 : m0 + width], result[:, rows, :])
 
-        for chunk in range(LITERAL_CHUNKS):
+        all_chunks = range(LITERAL_CHUNKS)
+        for chunk in all_chunks:
             entries = literal_list[:, chunk * BANK // LIST_ROWS : (chunk + 1) * BANK // LIST_ROWS]
             nc.vector.tensor_copy(v_words[chunk][:], table_words[:].bitcast(U32).indirect(entries))
             messages(0, [chunk])
             if chunk < LITERAL_CHUNKS // 2:
                 messages(1, [chunk])
-        messages(1, range(LITERAL_CHUNKS // 2, LITERAL_CHUNKS))
+        messages(1, all_chunks[LITERAL_CHUNKS // 2 :])
 
         deal_wl(1, reuse([P, 3 * HALF], U8, "wl_dealt1", "table_words"))
-        all_chunks = range(LITERAL_CHUNKS)
         q0, q1, q2, q3 = range(0, M, QUARTER)
-        run = QUARTER * PACK
         quantise_cs(q0, interleave_cs(nc.vector.tensor_copy, gain_on_gpsimd(q0, "gained0")[:], "interleaved0"))
         gained1 = gain_on_gpsimd(q1, "gained1")
+
         wc_raw.append(reuse([P, PACK, HALF], F32, "wc_raw1", "gathered_scales1"))
         nc.sync.dma_start(wc_raw[1][:], wc_rows[:, :, HALF:H])
         cs_raw[HALF] = reuse([P, PACK, HALF], F32, "cs_raw2", "gained0")
@@ -304,50 +306,51 @@ def tile_list_clause_state_round_kernel(
         for half, used_up in enumerate(("wl_words_raw", "h0")):
             residual.append(reuse([P, OUT_TILES, HALF], F32, "residual", used_up))
             nc.sync.dma_start(residual[half][:], cs_plain[:, :, half * HALF : (half + 1) * HALF])
-        for row_tile in range(2, 7):
+
+        last_tile = ROW_TILES - 1
+        for row_tile in range(2, last_tile):
             messages(row_tile, all_chunks)
             pick(row_tile)
-        messages(7, all_chunks[:-1])
+        messages(last_tile, all_chunks[:-1])
         quantise(wc_codes[0][:], wc_scales[0][:], interleave_wc(0)[:])
-        messages(7, all_chunks[-1:])
-        pick(7)
+        messages(last_tile, all_chunks[-1:])
+        pick(last_tile)
 
         e2, e3 = range(q1, q2, SUB)
         e6, e7 = range(q3, M, SUB)
         quantise(wc_codes[1][:], wc_scales[1][:], interleave_wc(1)[:])
-        z = z_tile([(0, q0, QUARTER), (1, q0, QUARTER)], "gathered_scales1")
-        maxima(z, 0, q0)
+        z_first = z_tile([(0, q0, QUARTER), (1, q0, QUARTER)], "gathered_scales1")
+        maxima(z_first, 0, q0)
         quantise_cs(q1, interleave_cs(nc.scalar.copy, gained1[:], "h2"))
-        maxima(z, 1, q0)
-        following = z_tile([(0, e2, SUB), (0, e3, SUB), (1, q1, QUARTER)], "h4")
-        maxima(following, 0, e2)
-        quantise_z(z)
-        gained = reuse([P, PACK, HALF], BF16, "gained", "h5")
+        maxima(z_first, 1, q0)
+        z_second = z_tile([(0, e2, SUB), (0, e3, SUB), (1, q1, QUARTER)], "h4")
+        maxima(z_second, 0, e2)
+        quantise_z(z_first)
+        gained2 = reuse([P, PACK, HALF], BF16, "gained", "h5")
         for j in range(PACK):
-            nc.scalar.activation(gained[:, j, :], cs_raw[HALF][:, j, :], ACT.Copy, scale=gain[:, j : j + 1])
-        second_half = interleave_cs(nc.scalar.copy, gained[:], "h3")
+            nc.scalar.activation(gained2[:, j, :], cs_raw[HALF][:, j, :], ACT.Copy, scale=gain[:, j : j + 1])
+        second_half = interleave_cs(nc.scalar.copy, gained2[:], "h3")
 
-        z = following
-        maxima(z, 0, e3)
-        maxima(z, 1, q1)
+        maxima(z_second, 0, e3)
+        maxima(z_second, 1, q1)
         update_on_gpsimd(q0, QUARTER)
         quantise_cs(q2, second_half)
-        quantise_z(z)
+        quantise_z(z_second)
 
-        z = z_tile([(0, q2, QUARTER), (1, q2, QUARTER)], "h6")
-        following = z_tile([(0, e6, SUB), (0, e7, SUB)], "h1")
-        last = z_tile([(1, e6, SUB), (1, e7, SUB)], "h7")
-        maxima(z, 0, q2)
-        maxima(z, 1, q2)
-        maxima(following, 0, e6)
+        z_third = z_tile([(0, q2, QUARTER), (1, q2, QUARTER)], "h6")
+        z_fourth = [z_tile([(b, e6, SUB), (b, e7, SUB)], used_up) for b, used_up in enumerate(("h1", "h7"))]
+        maxima(z_third, 0, q2)
+        maxima(z_third, 1, q2)
+        maxima(z_fourth[0], 0, e6)
         update_on_gpsimd(q1, QUARTER)
-        quantise_z(z)
-        maxima(following, 0, e7)
-        maxima(last, 1, e6)
-        maxima(last, 1, e7)
-        update_on_gpsimd(q2, QUARTER, 2)
-        quantise_z(following)
-        quantise_z(last)
-        update_on_vector(q2, QUARTER, 2, product(q2, QUARTER, 2), 1)
+        quantise_z(z_third)
+        maxima(z_fourth[0], 0, e7)
+        maxima(z_fourth[1], 1, e6)
+        maxima(z_fourth[1], 1, e7)
+        middle = OUT_TILES // 2
+        update_on_gpsimd(q2, QUARTER, middle)
+        quantise_z(z_fourth[0])
+        quantise_z(z_fourth[1])
+        update_on_vector(q2, QUARTER, middle, product(q2, QUARTER, middle), 1)
         update_on_vector(q3, QUARTER, 0, product(q3, QUARTER, 0), 2)
-        update_on_vector(q3, QUARTER, 2, product(q3, QUARTER, 2), 2)
+        update_on_vector(q3, QUARTER, middle, product(q3, QUARTER, middle), 2)

@@ -19,16 +19,16 @@ ACT = mybir.ActivationFunctionType
 P = 128
 PACK = 4
 QUADRANTS = 4
-PASSES = H // (P * PACK)
-BANK = 512
-LIST_ROWS = 16
-LITERAL_CHUNKS = S // BANK
-OUT_TILES = N // P
-SUB = BANK // PACK
-HALF = M // 2
-QUARTER = M // 4
-ROW_TILES = PASSES * PACK
 QUADRANT_ROWS = 4
+PASSES = H // (P * PACK)
+ROW_TILES = PASSES * PACK
+BANK = 512
+SHORT = BANK // 2
+LIST_ROWS = 16
+OUT_TILES = N // P
+EIGHTH = BANK // PACK
+QUARTER = M // 4
+HALF = M // 2
 SPARE = P - QUADRANT_ROWS * QUADRANTS
 RUN = 4
 RESULT_BANKS = 8
@@ -49,7 +49,7 @@ def tile_list_clause_state_round_kernel(
         def reuse(shape, dtype, name, used_up):
             return keep.tile(shape, dtype, name=name, tag=used_up, align_bytes=64)
 
-        def load_scale_rows(queue, tile, rows, places=range(QUADRANT_ROWS)):
+        def load_scale_rows(queue, tile, rows, places):
             for r in places:
                 queue.dma_start(tile[r:P:32].bitcast(I32), rows[r : QUADRANT_ROWS * QUADRANTS : QUADRANT_ROWS].bitcast(I32))
 
@@ -64,13 +64,12 @@ def tile_list_clause_state_round_kernel(
         wl_scales_raw = held([P, H], U8, "wl_scales_raw")
         bias = held([P, PASSES, PACK], F32, "bias")
         gain = held([P, PACK], F32, "gain")
+        v_scales = [held([P, S // 2], U8, "v_scales%d" % half) for half in range(2)]
 
         nc.gpsimd.dma_start(bias[:], bl.rearrange("(b p t) -> p b t", b=PASSES, t=PACK))
-        nc.vector.memset(wl_scales_raw[:].bitcast(I32), 0)
-        nc.gpsimd.memset(table_scales[0:SPARE, 0 : T // 2].bitcast(I32), 0)
-        nc.vector.memset(table_scales[0:SPARE, T // 2 : T].bitcast(I32), 0)
-        v_scales = [held([P, S // 2], U8, "v_scales%d" % half) for half in range(2)]
         nc.gpsimd.dma_start(gain[:], gc.rearrange("(p j) -> p j", j=PACK))
+        nc.vector.memset(wl_scales_raw[:].bitcast(I32), 0)
+        nc.vector.memset(table_scales[0:SPARE].bitcast(I32), 0)
         for half in range(2):
             nc.vector.memset(v_scales[half][:].bitcast(I32), 0)
 
@@ -81,26 +80,24 @@ def tile_list_clause_state_round_kernel(
         load_scale_rows(nc.scalar, wl_scales_raw[:], wl_scales[0], range(QUADRANT_ROWS // 2, QUADRANT_ROWS))
         nc.sync.dma_start(table_words[:], tab_words[0].rearrange("p t i -> p (t i)").bitcast(I32))
 
-        wl_dealt = []
-
-        def deal_wl(b, tile):
-            words, scales = tile[:, 0 : 2 * HALF], tile[:, 2 * HALF : 3 * HALF]
-            nc.vector.tensor_copy(
-                words.bitcast(U16).rearrange("k (t p) -> k t p", t=PACK),
+        wl_dealt_words = [held([P, 2 * HALF], U8, "wl_dealt_words%d" % b) for b in range(PASSES)]
+        wl_dealt_scales = [held([P, HALF], U8, "wl_dealt_scales%d" % b) for b in range(PASSES)]
+        for b in range(PASSES):
+            nc.scalar.copy(
+                wl_dealt_words[b][:].bitcast(U16).rearrange("k (t p) -> k t p", t=PACK),
                 wl_words_raw[:, 2 * HALF * b : 2 * HALF * (b + 1)].bitcast(U16).rearrange("k (p t) -> k t p", t=PACK),
             )
-            nc.vector.tensor_copy(
-                scales.rearrange("k (t p) -> k t p", t=PACK),
+            nc.gpsimd.tensor_copy(
+                wl_dealt_scales[b][:].rearrange("k (t p) -> k t p", t=PACK),
                 wl_scales_raw[:, HALF * b : HALF * (b + 1)].rearrange("k (p t) -> k t p", t=PACK),
             )
-            wl_dealt.append((words, scales))
+
+        def entries(first, end):
+            return literal_list[:, first // LIST_ROWS : end // LIST_ROWS]
 
         gathered = [held([P, S // 2], U8, "gathered_scales%d" % half) for half in range(2)]
         for half in range(2):
-            entries = literal_list[:, half * S // 2 // LIST_ROWS : (half + 1) * S // 2 // LIST_ROWS]
-            nc.vector.tensor_copy(gathered[half][:], table_scales[:].indirect(entries))
-
-        deal_wl(0, held([P, 3 * HALF], U8, "wl_dealt0"))
+            nc.vector.tensor_copy(gathered[half][:], table_scales[:].indirect(entries(half * S // 2, (half + 1) * S // 2)))
 
         def carry_scale_rows(queue, half):
             for r in range(QUADRANT_ROWS):
@@ -122,24 +119,28 @@ def tile_list_clause_state_round_kernel(
         wc_raw = [reuse([P, PACK, HALF], F32, "wc_raw0", "gathered_scales0")]
         nc.sync.dma_start(wc_raw[0][:], wc_rows[:, :, 0:HALF])
 
-        v_words = [held([P, BANK], U32, "v_words%d" % chunk) for chunk in range(LITERAL_CHUNKS)]
+        v_words = held([P, S], U32, "v_words")
         h = [held([P, S], F32, "h%d" % row_tile) for row_tile in range(ROW_TILES)]
 
-        def messages(row_tile, chunks):
+        def gather_words(first, end):
+            nc.vector.tensor_copy(v_words[:, first:end], table_words[:].bitcast(U32).indirect(entries(first, end)))
+
+        def messages(row_tile, first, end):
             b, t = divmod(row_tile, PACK)
-            for chunk in chunks:
-                literals = slice(BANK * chunk, BANK * (chunk + 1))
-                acc = psum.tile([P, BANK], F32, name="acc", tag="wide")
+            for j0 in range(first, end, BANK):
+                width = min(BANK, end - j0)
+                half, column = divmod(j0, S // 2)
+                acc = psum.tile([P, width], F32, name="acc", tag="wide")
                 nc.tensor.matmul_mx(
                     out=acc[:],
-                    lhsT=wl_dealt[b][0][:, 2 * P * t : 2 * P * (t + 1)].bitcast(FP4X4),
-                    lhsT_scale=wl_dealt[b][1][:, P * t : P * (t + 1)],
-                    rhs=v_words[chunk][:].bitcast(FP8X4),
-                    rhs_scale=v_scales[chunk // 2][:, BANK * (chunk % 2) : BANK * (chunk % 2 + 1)],
+                    lhsT=wl_dealt_words[b][:, 2 * P * t : 2 * P * (t + 1)].bitcast(FP4X4),
+                    lhsT_scale=wl_dealt_scales[b][:, P * t : P * (t + 1)],
+                    rhs=v_words[:, j0 : j0 + width].bitcast(FP8X4),
+                    rhs_scale=v_scales[half][:, column : column + width],
                     start=True,
                     stop=True,
                 )
-                nc.scalar.activation(h[row_tile][:, literals], acc[:], ACT.Identity, bias=bias[:, b, t : t + 1])
+                nc.scalar.activation(h[row_tile][:, j0 : j0 + width], acc[:], ACT.Identity, bias=bias[:, b, t : t + 1])
 
         wc_codes = [held([P, HALF], U32, "wc_codes%d" % b) for b in range(PASSES)]
         wc_scales = [held([P, HALF], U8, "wc_scales%d" % b) for b in range(PASSES)]
@@ -173,8 +174,8 @@ def tile_list_clause_state_round_kernel(
             codes = held([P, width], U32, "cs_codes%d" % m0)
             scales = held([P, width], U8, "cs_scales%d" % m0)
             quantise(codes[:], scales[:], interleaved[:])
-            for s0 in range(0, width, SUB):
-                cs_operand[m0 + s0] = (codes[:, s0 : s0 + SUB], scales[:, s0 : s0 + SUB])
+            for s0 in range(0, width, EIGHTH):
+                cs_operand[m0 + s0] = (codes[:, s0 : s0 + EIGHTH], scales[:, s0 : s0 + EIGHTH])
 
         x = [held([P, PACK, M], F32, "x%d" % b) for b in range(PASSES)]
 
@@ -183,9 +184,9 @@ def tile_list_clause_state_round_kernel(
             nc.vector.tensor_tensor(x[b][:, t, :], h[row_tile][:].indirect(slot_lists[:]), weight, ALU.mult)
 
         def strongest(z, b, m0):
-            for s0 in range(0, z.shape[1] // PACK, SUB):
+            for s0 in range(0, z.shape[1] // PACK, EIGHTH):
                 cs_codes, cs_scales = cs_operand[m0 + s0]
-                c = psum.tile([P, PACK, SUB], F32, name="c", tag="proj")
+                c = psum.tile([P, PACK, EIGHTH], F32, name="c", tag="proj")
                 for t in range(PACK):
                     nc.tensor.matmul_mx(
                         out=c[:, t, :],
@@ -197,9 +198,9 @@ def tile_list_clause_state_round_kernel(
                         stop=True,
                     )
                 nc.vector.tensor_tensor(
-                    z[:, PACK * s0 : PACK * (s0 + SUB)].rearrange("p (g i t) -> p g t i", i=RUN, t=PACK),
+                    z[:, PACK * s0 : PACK * (s0 + EIGHTH)].rearrange("p (g i t) -> p g t i", i=RUN, t=PACK),
                     c[:].rearrange("p t (g i) -> p g t i", i=RUN),
-                    x[b][:, :, m0 + s0 : m0 + s0 + SUB].rearrange("p t (g i) -> p g t i", i=RUN),
+                    x[b][:, :, m0 + s0 : m0 + s0 + EIGHTH].rearrange("p t (g i) -> p g t i", i=RUN),
                     ALU.max,
                 )
 
@@ -227,7 +228,7 @@ def tile_list_clause_state_round_kernel(
             quantise(codes[:], scales[:], tile[:])
             for b, m0 in places:
                 column, width = places[b, m0]
-                for s0 in range(0, width, SUB):
+                for s0 in range(0, width, EIGHTH):
                     z_operand[b, m0 + s0] = (codes, scales, column + s0)
 
         out_rows = out.rearrange("(o p) m -> p o m", p=P)
@@ -277,16 +278,24 @@ def tile_list_clause_state_round_kernel(
                 nc.vector.tensor_tensor(result[:, rows, :], y[:, rows, :], states, ALU.add)
                 nc.scalar.dma_start(out_rows[:, out_tiles, m0 : m0 + width], result[:, rows, :])
 
-        all_chunks = range(LITERAL_CHUNKS)
-        for chunk in all_chunks:
-            entries = literal_list[:, chunk * BANK // LIST_ROWS : (chunk + 1) * BANK // LIST_ROWS]
-            nc.vector.tensor_copy(v_words[chunk][:], table_words[:].bitcast(U32).indirect(entries))
-            messages(0, [chunk])
-            if chunk < LITERAL_CHUNKS // 2:
-                messages(1, [chunk])
-        messages(1, all_chunks[LITERAL_CHUNKS // 2 :])
+        gather_words(0, SHORT)
+        messages(0, 0, SHORT)
+        messages(1, 0, SHORT)
+        gather_words(SHORT, BANK)
+        messages(0, SHORT, BANK)
+        messages(1, SHORT, BANK)
+        messages(2, 0, BANK)
+        gather_words(BANK, 2 * BANK)
+        messages(0, BANK, 2 * BANK)
+        messages(1, BANK, 2 * BANK)
+        gather_words(2 * BANK, 3 * BANK)
+        messages(0, 2 * BANK, 3 * BANK)
+        gather_words(3 * BANK, S - SHORT)
+        messages(0, 3 * BANK, S - SHORT)
+        gather_words(S - SHORT, S)
+        messages(0, S - SHORT, S)
+        messages(1, 2 * BANK, S)
 
-        deal_wl(1, reuse([P, 3 * HALF], U8, "wl_dealt1", "table_words"))
         q0, q1, q2, q3 = range(0, M, QUARTER)
         quantise_cs(q0, interleave_cs(nc.vector.tensor_copy, gain_on_gpsimd(q0, "gained0")[:], "interleaved0"))
         gained1 = gain_on_gpsimd(q1, "gained1")
@@ -299,31 +308,33 @@ def tile_list_clause_state_round_kernel(
         nc.sync.dma_start(w2_word_tile[:], w2_words.rearrange("a p n i -> p a (n i)").bitcast(I32))
         w2_scale_tile = reuse([P, PASSES, N], U8, "w2_scale_tile", "cs_raw0")
         nc.gpsimd.memset(w2_scale_tile[:].rearrange("p a n -> p (a n)").bitcast(I32), 0)
-        load_scale_rows(nc.sync, w2_scale_tile[:], w2_scales.rearrange("a q n -> q a n"))
+        load_scale_rows(nc.sync, w2_scale_tile[:], w2_scales.rearrange("a q n -> q a n"), range(QUADRANT_ROWS))
         pick(0)
         pick(1)
         cs_plain = cs.rearrange("(o p) m -> p o m", p=P)
-        for half, used_up in enumerate(("wl_words_raw", "h0")):
+        for half, used_up in enumerate(("table_words", "h0")):
             residual.append(reuse([P, OUT_TILES, HALF], F32, "residual", used_up))
             nc.sync.dma_start(residual[half][:], cs_plain[:, :, half * HALF : (half + 1) * HALF])
 
         last_tile = ROW_TILES - 1
-        for row_tile in range(2, last_tile):
-            messages(row_tile, all_chunks)
+        messages(2, BANK, S)
+        pick(2)
+        for row_tile in range(3, last_tile):
+            messages(row_tile, 0, S)
             pick(row_tile)
-        messages(last_tile, all_chunks[:-1])
+        messages(last_tile, 0, S - BANK)
         quantise(wc_codes[0][:], wc_scales[0][:], interleave_wc(0)[:])
-        messages(last_tile, all_chunks[-1:])
+        messages(last_tile, S - BANK, S)
         pick(last_tile)
 
-        e2, e3 = range(q1, q2, SUB)
-        e6, e7 = range(q3, M, SUB)
+        e2, e3 = range(q1, q2, EIGHTH)
+        e6, e7 = range(q3, M, EIGHTH)
         quantise(wc_codes[1][:], wc_scales[1][:], interleave_wc(1)[:])
         z_first = z_tile([(0, q0, QUARTER), (1, q0, QUARTER)], "gathered_scales1")
         maxima(z_first, 0, q0)
         quantise_cs(q1, interleave_cs(nc.scalar.copy, gained1[:], "h2"))
         maxima(z_first, 1, q0)
-        z_second = z_tile([(0, e2, SUB), (0, e3, SUB), (1, q1, QUARTER)], "h4")
+        z_second = z_tile([(0, e2, EIGHTH), (0, e3, EIGHTH), (1, q1, QUARTER)], "h4")
         maxima(z_second, 0, e2)
         quantise_z(z_first)
         gained2 = reuse([P, PACK, HALF], BF16, "gained", "h5")
@@ -338,7 +349,7 @@ def tile_list_clause_state_round_kernel(
         quantise_z(z_second)
 
         z_third = z_tile([(0, q2, QUARTER), (1, q2, QUARTER)], "h6")
-        z_fourth = [z_tile([(b, e6, SUB), (b, e7, SUB)], used_up) for b, used_up in enumerate(("h1", "h7"))]
+        z_fourth = [z_tile([(b, e6, EIGHTH), (b, e7, EIGHTH)], used_up) for b, used_up in enumerate(("h1", "h7"))]
         maxima(z_third, 0, q2)
         maxima(z_third, 1, q2)
         maxima(z_fourth[0], 0, e6)

@@ -153,19 +153,23 @@ def tile_list_clause_state_round_kernel(
             )
             return interleaved
 
-        def gain_on_gpsimd(m0, name):
-            gained = held([P, PACK, QUARTER], BF16, name)
-            for j in range(PACK):
-                nc.gpsimd.tensor_scalar(gained[:, j, :], cs_raw[m0][:, j, :], gain[:, j : j + 1], 0.0, ALU.mult, ALU.add)
-            return gained
-
-        def interleave_cs(copy, gained, used_up):
-            interleaved = reuse([P, gained.shape[2] * PACK], BF16, "cs_interleaved", used_up)
-            copy(
-                interleaved[:].rearrange("p (g i j) -> p g j i", i=RUN, j=PACK),
-                gained.rearrange("p j (g i) -> p g j i", i=RUN),
+        def gain_interleaved(engine, target, states):
+            groups = states.shape[2] // RUN
+            engine.tensor_tensor(
+                target.rearrange("p (g i j) -> p g j i", i=RUN, j=PACK),
+                states.rearrange("p j (g i) -> p g j i", i=RUN),
+                gain[:].unsqueeze(1).unsqueeze(3).to_broadcast([P, groups, PACK, RUN]),
+                ALU.mult,
             )
-            return interleaved
+
+        def gain_on_scalar(target, states, used_up):
+            gained = reuse([P, PACK, states.shape[2]], BF16, "gained", used_up)
+            for j in range(PACK):
+                nc.scalar.activation(gained[:, j, :], states[:, j, :], ACT.Copy, scale=gain[:, j : j + 1])
+            nc.scalar.copy(
+                target.rearrange("p (g i j) -> p g j i", i=RUN, j=PACK),
+                gained[:].rearrange("p j (g i) -> p g j i", i=RUN),
+            )
 
         cs_operand = {}
 
@@ -297,16 +301,19 @@ def tile_list_clause_state_round_kernel(
         messages(1, 2 * BANK, S)
 
         q0, q1, q2, q3 = range(0, M, QUARTER)
-        quantise_cs(q0, interleave_cs(nc.vector.tensor_copy, gain_on_gpsimd(q0, "gained0")[:], "interleaved0"))
-        gained1 = gain_on_gpsimd(q1, "gained1")
+        first = held([P, QUARTER * PACK], BF16, "first")
+        gain_interleaved(nc.gpsimd, first[:], cs_raw[q0])
+        second = held([P, QUARTER * PACK], BF16, "second")
+        gain_interleaved(nc.vector, second[:, 0 : EIGHTH * PACK], cs_raw[q1][:, :, 0:EIGHTH])
+        quantise_cs(q0, first)
 
         wc_raw.append(reuse([P, PACK, HALF], F32, "wc_raw1", "gathered_scales1"))
         nc.sync.dma_start(wc_raw[1][:], wc_rows[:, :, HALF:H])
-        cs_raw[HALF] = reuse([P, PACK, HALF], F32, "cs_raw2", "gained0")
+        cs_raw[HALF] = reuse([P, PACK, HALF], F32, "cs_raw2", "cs_raw0")
         nc.sync.dma_start(cs_raw[HALF][:], cs_rows[:, :, HALF:M])
-        w2_word_tile = reuse([P, PASSES, N], I32, "w2_word_tile", "interleaved0")
+        w2_word_tile = reuse([P, PASSES, N], I32, "w2_word_tile", "first")
         nc.sync.dma_start(w2_word_tile[:], w2_words.rearrange("a p n i -> p a (n i)").bitcast(I32))
-        w2_scale_tile = reuse([P, PASSES, N], U8, "w2_scale_tile", "cs_raw0")
+        w2_scale_tile = reuse([P, PASSES, N], U8, "w2_scale_tile", "wl_scales_raw")
         nc.gpsimd.memset(w2_scale_tile[:].rearrange("p a n -> p (a n)").bitcast(I32), 0)
         load_scale_rows(nc.sync, w2_scale_tile[:], w2_scales.rearrange("a q n -> q a n"), range(QUADRANT_ROWS))
         pick(0)
@@ -332,15 +339,14 @@ def tile_list_clause_state_round_kernel(
         quantise(wc_codes[1][:], wc_scales[1][:], interleave_wc(1)[:])
         z_first = z_tile([(0, q0, QUARTER), (1, q0, QUARTER)], "gathered_scales1")
         maxima(z_first, 0, q0)
-        quantise_cs(q1, interleave_cs(nc.scalar.copy, gained1[:], "h2"))
+        gain_on_scalar(second[:, EIGHTH * PACK :], cs_raw[q1][:, :, EIGHTH:QUARTER], "h2")
+        quantise_cs(q1, second)
         maxima(z_first, 1, q0)
         z_second = z_tile([(0, e2, EIGHTH), (0, e3, EIGHTH), (1, q1, QUARTER)], "h4")
         maxima(z_second, 0, e2)
         quantise_z(z_first)
-        gained2 = reuse([P, PACK, HALF], BF16, "gained", "h5")
-        for j in range(PACK):
-            nc.scalar.activation(gained2[:, j, :], cs_raw[HALF][:, j, :], ACT.Copy, scale=gain[:, j : j + 1])
-        second_half = interleave_cs(nc.scalar.copy, gained2[:], "h3")
+        second_half = reuse([P, HALF * PACK], BF16, "second_half", "h3")
+        gain_on_scalar(second_half[:], cs_raw[HALF][:], "h5")
 
         maxima(z_second, 0, e3)
         maxima(z_second, 1, q1)

@@ -64,14 +64,15 @@ def tile_list_clause_state_round_kernel(
         wl_scales_raw = held([P, H], U8, "wl_scales_raw")
         bias = held([P, PASSES, PACK], F32, "bias")
         gain = held([P, PACK], F32, "gain")
-        v_scales = [held([P, S // 2], U8, "v_scales%d" % half) for half in range(2)]
+        scale_parts = [(0, BANK), (BANK, S)]
+        v_scales = [held([P, end - first], U8, "v_scales%d" % first) for first, end in scale_parts]
 
         nc.gpsimd.dma_start(bias[:], bl.rearrange("(b p t) -> p b t", b=PASSES, t=PACK))
         nc.gpsimd.dma_start(gain[:], gc.rearrange("(p j) -> p j", j=PACK))
         nc.vector.memset(wl_scales_raw[:].bitcast(I32), 0)
         nc.vector.memset(table_scales[0:SPARE].bitcast(I32), 0)
-        for half in range(2):
-            nc.vector.memset(v_scales[half][:].bitcast(I32), 0)
+        for part in v_scales:
+            nc.vector.memset(part[:].bitcast(I32), 0)
 
         nc.sync.dma_start(literal_list[:], offs)
         nc.sync.dma_start(table_scales[SPARE:P].bitcast(I32), tab_scales[0].bitcast(I32))
@@ -95,9 +96,9 @@ def tile_list_clause_state_round_kernel(
         def entries(first, end):
             return literal_list[:, first // LIST_ROWS : end // LIST_ROWS]
 
-        gathered = [held([P, S // 2], U8, "gathered_scales%d" % half) for half in range(2)]
-        for half in range(2):
-            nc.vector.tensor_copy(gathered[half][:], table_scales[:].indirect(entries(half * S // 2, (half + 1) * S // 2)))
+        gathered = [held([P, end - first], U8, "gathered_scales%d" % part) for part, (first, end) in enumerate(scale_parts)]
+        for part, (first, end) in enumerate(scale_parts):
+            nc.vector.tensor_copy(gathered[part][:], table_scales[:].indirect(entries(first, end)))
 
         def carry_scale_rows(queue, half):
             for r in range(QUADRANT_ROWS):
@@ -106,17 +107,17 @@ def tile_list_clause_state_round_kernel(
 
         wc_rows = wc.rearrange("(p j) r -> p j r", j=PACK)
         cs_rows = cs.rearrange("(p j) m -> p j m", j=PACK)
-        cs_raw = {0: held([P, PACK, QUARTER], F32, "cs_raw0")[:]}
-        nc.sync.dma_start(cs_raw[0], cs_rows[:, :, 0:QUARTER])
         nc.sync.dma_start(slot_lists[:], offs2)
         carry_scale_rows(nc.scalar, 0)
-        states_and_weight = reuse([P, 2, M], F32, "states_and_weight", "table_scales")
-        cs_raw[QUARTER] = states_and_weight[:, 0, :].rearrange("p (j m) -> p j m", j=PACK)
-        weight = states_and_weight[:, 1, :]
-        nc.sync.dma_start(cs_raw[QUARTER], cs_rows[:, :, QUARTER:HALF])
-        carry_scale_rows(nc.sync, 1)
+        carry_scale_rows(nc.scalar, 1)
+        cs_first = reuse([P, 2, M], F32, "cs_first", "wl_scales_raw")
+        cs_raw = {}
+        for piece, m0 in enumerate((0, QUARTER)):
+            cs_raw[m0] = cs_first[:, piece, :].rearrange("p (j m) -> p j m", j=PACK)
+            nc.sync.dma_start(cs_raw[m0], cs_rows[:, :, m0 : m0 + QUARTER])
+        weight = reuse([P, M], F32, "weight", "gathered_scales0")[:]
         nc.sync.dma_start(weight, wgt)
-        wc_raw = [reuse([P, PACK, HALF], F32, "wc_raw0", "gathered_scales0")]
+        wc_raw = [reuse([P, PACK, HALF], F32, "wc_raw0", "gathered_scales1")]
         nc.sync.dma_start(wc_raw[0][:], wc_rows[:, :, 0:HALF])
 
         v_words = held([P, S], U32, "v_words")
@@ -129,7 +130,8 @@ def tile_list_clause_state_round_kernel(
             b, t = divmod(row_tile, PACK)
             for j0 in range(first, end, BANK):
                 width = min(BANK, end - j0)
-                half, column = divmod(j0, S // 2)
+                half = 0 if j0 < BANK else 1
+                column = j0 - scale_parts[half][0]
                 acc = psum.tile([P, width], F32, name="acc", tag="wide")
                 nc.tensor.matmul_mx(
                     out=acc[:],
@@ -291,14 +293,13 @@ def tile_list_clause_state_round_kernel(
         messages(2, 0, BANK)
         gather_words(BANK, 2 * BANK)
         messages(0, BANK, 2 * BANK)
-        messages(1, BANK, 2 * BANK)
         gather_words(2 * BANK, 3 * BANK)
         messages(0, 2 * BANK, 3 * BANK)
         gather_words(3 * BANK, S - SHORT)
         messages(0, 3 * BANK, S - SHORT)
         gather_words(S - SHORT, S)
         messages(0, S - SHORT, S)
-        messages(1, 2 * BANK, S)
+        messages(1, BANK, S)
 
         q0, q1, q2, q3 = range(0, M, QUARTER)
         first = held([P, QUARTER * PACK], BF16, "first")
@@ -307,19 +308,19 @@ def tile_list_clause_state_round_kernel(
         gain_interleaved(nc.vector, second[:, 0 : EIGHTH * PACK], cs_raw[q1][:, :, 0:EIGHTH])
         quantise_cs(q0, first)
 
-        wc_raw.append(reuse([P, PACK, HALF], F32, "wc_raw1", "gathered_scales1"))
+        wc_raw.append(reuse([P, PACK, HALF], F32, "wc_raw1", "table_words"))
         nc.sync.dma_start(wc_raw[1][:], wc_rows[:, :, HALF:H])
-        cs_raw[HALF] = reuse([P, PACK, HALF], F32, "cs_raw2", "cs_raw0")
+        cs_raw[HALF] = reuse([P, PACK, HALF], F32, "cs_raw2", "first")
         nc.sync.dma_start(cs_raw[HALF][:], cs_rows[:, :, HALF:M])
-        w2_word_tile = reuse([P, PASSES, N], I32, "w2_word_tile", "first")
+        w2_word_tile = reuse([P, PASSES, N], I32, "w2_word_tile", "v_words")
         nc.sync.dma_start(w2_word_tile[:], w2_words.rearrange("a p n i -> p a (n i)").bitcast(I32))
-        w2_scale_tile = reuse([P, PASSES, N], U8, "w2_scale_tile", "wl_scales_raw")
+        w2_scale_tile = reuse([P, PASSES, N], U8, "w2_scale_tile", "wl_words_raw")
         nc.gpsimd.memset(w2_scale_tile[:].rearrange("p a n -> p (a n)").bitcast(I32), 0)
         load_scale_rows(nc.sync, w2_scale_tile[:], w2_scales.rearrange("a q n -> q a n"), range(QUADRANT_ROWS))
         pick(0)
         pick(1)
         cs_plain = cs.rearrange("(o p) m -> p o m", p=P)
-        for half, used_up in enumerate(("table_words", "h0")):
+        for half, used_up in enumerate(("h1", "h0")):
             residual.append(reuse([P, OUT_TILES, HALF], F32, "residual", used_up))
             nc.sync.dma_start(residual[half][:], cs_plain[:, :, half * HALF : (half + 1) * HALF])
 
@@ -337,7 +338,7 @@ def tile_list_clause_state_round_kernel(
         e2, e3 = range(q1, q2, EIGHTH)
         e6, e7 = range(q3, M, EIGHTH)
         quantise(wc_codes[1][:], wc_scales[1][:], interleave_wc(1)[:])
-        z_first = z_tile([(0, q0, QUARTER), (1, q0, QUARTER)], "gathered_scales1")
+        z_first = z_tile([(0, q0, QUARTER), (1, q0, QUARTER)], "table_words")
         maxima(z_first, 0, q0)
         gain_on_scalar(second[:, EIGHTH * PACK :], cs_raw[q1][:, :, EIGHTH:QUARTER], "h2")
         quantise_cs(q1, second)
@@ -355,7 +356,7 @@ def tile_list_clause_state_round_kernel(
         quantise_z(z_second)
 
         z_third = z_tile([(0, q2, QUARTER), (1, q2, QUARTER)], "h6")
-        z_fourth = [z_tile([(b, e6, EIGHTH), (b, e7, EIGHTH)], used_up) for b, used_up in enumerate(("h1", "h7"))]
+        z_fourth = [z_tile([(b, e6, EIGHTH), (b, e7, EIGHTH)], used_up) for b, used_up in enumerate(("h2", "h7"))]
         maxima(z_third, 0, q2)
         maxima(z_third, 1, q2)
         maxima(z_fourth[0], 0, e6)

@@ -31,6 +31,8 @@ QUARTER = M // 4
 HALF = M // 2
 SPARE = P - QUADRANT_ROWS * QUADRANTS
 RUN = 4
+PAIR = 2
+LATE = 2 * EIGHTH
 RESULT_BANKS = 8
 
 
@@ -117,8 +119,9 @@ def tile_list_clause_state_round_kernel(
             nc.sync.dma_start(cs_raw[m0], cs_rows[:, :, m0 : m0 + QUARTER])
         weight = reuse([P, M], F32, "weight", "gathered_scales0")[:]
         nc.sync.dma_start(weight, wgt)
-        wc_raw = [reuse([P, PACK, HALF], F32, "wc_raw0", "gathered_scales1")]
-        nc.sync.dma_start(wc_raw[0][:], wc_rows[:, :, 0:HALF])
+        shared = reuse([P, PACK * M - LATE + PACK * HALF], F32, "shared", "gathered_scales1")
+        wc_raw = [shared[:, PACK * M - LATE :].rearrange("p (j r) -> p j r", j=PACK)]
+        nc.sync.dma_start(wc_raw[0], wc_rows[:, :, 0:HALF])
 
         v_words = held([P, S], U32, "v_words")
         h = [held([P, S], F32, "h%d" % row_tile) for row_tile in range(ROW_TILES)]
@@ -144,16 +147,19 @@ def tile_list_clause_state_round_kernel(
                 )
                 nc.scalar.activation(h[row_tile][:, j0 : j0 + width], acc[:], ACT.Identity, bias=bias[:, b, t : t + 1])
 
-        wc_codes = [held([P, HALF], U32, "wc_codes%d" % b) for b in range(PASSES)]
-        wc_scales = [held([P, HALF], U8, "wc_scales%d" % b) for b in range(PASSES)]
+        wc_operand = {}
 
-        def interleave_wc(b):
-            interleaved = ring.tile([P, HALF * PACK], BF16, name="wc_interleaved", tag="interleaved", align_bytes=64)
+        def prepare_wc(b, t0):
+            interleaved = held([P, PAIR * P * PACK], BF16, "wc_interleaved%d_%d" % (b, t0))
             nc.scalar.copy(
-                interleaved[:].rearrange("k (t p j) -> k p j t", t=PACK, j=PACK),
-                wc_raw[b][:].rearrange("k j (p t) -> k p j t", t=PACK),
+                interleaved[:].rearrange("k (t p j) -> k p j t", t=PAIR, j=PACK),
+                wc_raw[b].rearrange("k j (p t) -> k p j t", t=PACK)[:, :, :, t0 : t0 + PAIR],
             )
-            return interleaved
+            codes = held([P, PAIR * P], U32, "wc_codes%d_%d" % (b, t0))
+            scales = held([P, PAIR * P], U8, "wc_scales%d_%d" % (b, t0))
+            quantise(codes[:], scales[:], interleaved[:])
+            for t in range(PAIR):
+                wc_operand[b, t0 + t] = (codes[:, P * t : P * (t + 1)], scales[:, P * t : P * (t + 1)])
 
         def gain_interleaved(engine, target, states):
             groups = states.shape[2] // RUN
@@ -183,11 +189,12 @@ def tile_list_clause_state_round_kernel(
             for s0 in range(0, width, EIGHTH):
                 cs_operand[m0 + s0] = (codes[:, s0 : s0 + EIGHTH], scales[:, s0 : s0 + EIGHTH])
 
-        x = [held([P, PACK, M], F32, "x%d" % b) for b in range(PASSES)]
+        x = [held([P, PACK, M], F32, "x0")[:], shared[:, 0 : PACK * M].rearrange("p (t m) -> p t m", t=PACK)]
 
-        def pick(row_tile):
+        def pick(row_tile, first=0, end=M):
             b, t = divmod(row_tile, PACK)
-            nc.vector.tensor_tensor(x[b][:, t, :], h[row_tile][:].indirect(slot_lists[:]), weight, ALU.mult)
+            clauses = slot_lists[:, first // LIST_ROWS : end // LIST_ROWS]
+            nc.vector.tensor_tensor(x[b][:, t, first:end], h[row_tile][:].indirect(clauses), weight[:, first:end], ALU.mult)
 
         def strongest(z, b, m0):
             for s0 in range(0, z.shape[1] // PACK, EIGHTH):
@@ -196,8 +203,8 @@ def tile_list_clause_state_round_kernel(
                 for t in range(PACK):
                     nc.tensor.matmul_mx(
                         out=c[:, t, :],
-                        lhsT=wc_codes[b][:, P * t : P * (t + 1)].bitcast(FP8X4),
-                        lhsT_scale=wc_scales[b][:, P * t : P * (t + 1)],
+                        lhsT=wc_operand[b, t][0].bitcast(FP8X4),
+                        lhsT_scale=wc_operand[b, t][1],
                         rhs=cs_codes.bitcast(FP8X4),
                         rhs_scale=cs_scales,
                         start=True,
@@ -225,11 +232,11 @@ def tile_list_clause_state_round_kernel(
             column, width = places[b, m0]
             strongest(tile[:, PACK * column : PACK * (column + width)], b, m0)
 
-        def quantise_z(z):
+        def quantise_z(z, used_up=None):
             tile, places = z
             columns = tile.shape[1] // PACK
             name = "z%d_%d" % min(places)
-            codes = held([P, columns], U32, name + "_codes")
+            codes = reuse([P, columns], U32, name + "_codes", used_up or name + "_codes")
             scales = held([P, columns], U8, name + "_scales")
             quantise(codes[:], scales[:], tile[:])
             for b, m0 in places:
@@ -304,12 +311,13 @@ def tile_list_clause_state_round_kernel(
         q0, q1, q2, q3 = range(0, M, QUARTER)
         first = held([P, QUARTER * PACK], BF16, "first")
         gain_interleaved(nc.gpsimd, first[:], cs_raw[q0])
-        second = held([P, QUARTER * PACK], BF16, "second")
-        gain_interleaved(nc.vector, second[:, 0 : EIGHTH * PACK], cs_raw[q1][:, :, 0:EIGHTH])
+        third_eighth = held([P, EIGHTH * PACK], BF16, "third_eighth")
+        gain_interleaved(nc.vector, third_eighth[:], cs_raw[q1][:, :, 0:EIGHTH])
         quantise_cs(q0, first)
+        quantise_cs(q1, third_eighth)
 
-        wc_raw.append(reuse([P, PACK, HALF], F32, "wc_raw1", "table_words"))
-        nc.sync.dma_start(wc_raw[1][:], wc_rows[:, :, HALF:H])
+        wc_raw.append(reuse([P, PACK, HALF], F32, "wc_raw1", "table_words")[:])
+        nc.sync.dma_start(wc_raw[1], wc_rows[:, :, HALF:H])
         cs_raw[HALF] = reuse([P, PACK, HALF], F32, "cs_raw2", "first")
         nc.sync.dma_start(cs_raw[HALF][:], cs_rows[:, :, HALF:M])
         w2_word_tile = reuse([P, PASSES, N], I32, "w2_word_tile", "v_words")
@@ -330,30 +338,36 @@ def tile_list_clause_state_round_kernel(
         for row_tile in range(3, last_tile):
             messages(row_tile, 0, S)
             pick(row_tile)
-        messages(last_tile, 0, S - BANK)
-        quantise(wc_codes[0][:], wc_scales[0][:], interleave_wc(0)[:])
-        messages(last_tile, S - BANK, S)
-        pick(last_tile)
+        messages(last_tile, 0, S)
+        pick(last_tile, 0, M - LATE)
+        prepare_wc(0, 0)
+        prepare_wc(0, PAIR)
+        pick(last_tile, M - LATE, M)
 
         e2, e3 = range(q1, q2, EIGHTH)
         e6, e7 = range(q3, M, EIGHTH)
-        quantise(wc_codes[1][:], wc_scales[1][:], interleave_wc(1)[:])
-        z_first = z_tile([(0, q0, QUARTER), (1, q0, QUARTER)], "table_words")
-        maxima(z_first, 0, q0)
-        gain_on_scalar(second[:, EIGHTH * PACK :], cs_raw[q1][:, :, EIGHTH:QUARTER], "h2")
-        quantise_cs(q1, second)
-        maxima(z_first, 1, q0)
-        z_second = z_tile([(0, e2, EIGHTH), (0, e3, EIGHTH), (1, q1, QUARTER)], "h4")
+        e0, e1 = range(q0, q1, EIGHTH)
+        z_first = z_tile([(0, e0, EIGHTH), (0, e1, EIGHTH), (1, q0, QUARTER)], "h4")
+        maxima(z_first, 0, e0)
+        prepare_wc(1, 0)
+        maxima(z_first, 0, e1)
+        prepare_wc(1, PAIR)
+        z_second = z_tile([(0, e2, EIGHTH), (0, e3, EIGHTH), (1, e2, EIGHTH), (1, e3, EIGHTH)], "table_words")
         maxima(z_second, 0, e2)
+        maxima(z_first, 1, q0)
+        fourth_eighth = held([P, EIGHTH * PACK], BF16, "fourth_eighth")
+        gain_on_scalar(fourth_eighth[:], cs_raw[q1][:, :, EIGHTH:QUARTER], "h2")
+        quantise_cs(e3, fourth_eighth)
         quantise_z(z_first)
         second_half = reuse([P, HALF * PACK], BF16, "second_half", "h3")
         gain_on_scalar(second_half[:], cs_raw[HALF][:], "h5")
 
+        maxima(z_second, 1, e2)
         maxima(z_second, 0, e3)
-        maxima(z_second, 1, q1)
+        maxima(z_second, 1, e3)
         update_on_gpsimd(q0, QUARTER)
         quantise_cs(q2, second_half)
-        quantise_z(z_second)
+        quantise_z(z_second, "h5")
 
         z_third = z_tile([(0, q2, QUARTER), (1, q2, QUARTER)], "h6")
         z_fourth = [z_tile([(b, e6, EIGHTH), (b, e7, EIGHTH)], used_up) for b, used_up in enumerate(("h2", "h7"))]

@@ -31,9 +31,8 @@ QUARTER = M // 4
 HALF = M // 2
 SPARE = P - QUADRANT_ROWS * QUADRANTS
 RUN = 4
-PAIR = 2
-LATE = 2 * EIGHTH
 RESULT_BANKS = 8
+LATE = 3 * EIGHTH
 
 
 def tile_list_clause_state_round_kernel(
@@ -112,16 +111,15 @@ def tile_list_clause_state_round_kernel(
         nc.sync.dma_start(slot_lists[:], offs2)
         carry_scale_rows(nc.scalar, 0)
         carry_scale_rows(nc.scalar, 1)
-        cs_first = reuse([P, 2, M], F32, "cs_first", "wl_scales_raw")
+        cs_first = reuse([P, PACK * (QUARTER + EIGHTH)], F32, "cs_first", "wl_scales_raw")
         cs_raw = {}
-        for piece, m0 in enumerate((0, QUARTER)):
-            cs_raw[m0] = cs_first[:, piece, :].rearrange("p (j m) -> p j m", j=PACK)
-            nc.sync.dma_start(cs_raw[m0], cs_rows[:, :, m0 : m0 + QUARTER])
+        for m0, width in ((0, QUARTER), (QUARTER, EIGHTH)):
+            cs_raw[m0] = cs_first[:, PACK * m0 : PACK * (m0 + width)].rearrange("p (j m) -> p j m", j=PACK)
+            nc.sync.dma_start(cs_raw[m0], cs_rows[:, :, m0 : m0 + width])
         weight = reuse([P, M], F32, "weight", "gathered_scales0")[:]
         nc.sync.dma_start(weight, wgt)
-        shared = reuse([P, PACK * M - LATE + PACK * HALF], F32, "shared", "gathered_scales1")
-        wc_raw = [shared[:, PACK * M - LATE :].rearrange("p (j r) -> p j r", j=PACK)]
-        nc.sync.dma_start(wc_raw[0], wc_rows[:, :, 0:HALF])
+        wc_raw = [reuse([P, PACK, HALF], F32, "wc_raw0", "gathered_scales1")]
+        nc.sync.dma_start(wc_raw[0][:], wc_rows[:, :, 0:HALF])
 
         v_words = held([P, S], U32, "v_words")
         h = [held([P, S], F32, "h%d" % row_tile) for row_tile in range(ROW_TILES)]
@@ -147,19 +145,16 @@ def tile_list_clause_state_round_kernel(
                 )
                 nc.scalar.activation(h[row_tile][:, j0 : j0 + width], acc[:], ACT.Identity, bias=bias[:, b, t : t + 1])
 
-        wc_operand = {}
+        wc_codes = [held([P, HALF], U32, "wc_codes%d" % b) for b in range(PASSES)]
+        wc_scales = [held([P, HALF], U8, "wc_scales%d" % b) for b in range(PASSES)]
 
-        def prepare_wc(b, t0):
-            interleaved = held([P, PAIR * P * PACK], BF16, "wc_interleaved%d_%d" % (b, t0))
+        def interleave_wc(b):
+            interleaved = ring.tile([P, HALF * PACK], BF16, name="wc_interleaved", tag="interleaved", align_bytes=64)
             nc.scalar.copy(
-                interleaved[:].rearrange("k (t p j) -> k p j t", t=PAIR, j=PACK),
-                wc_raw[b].rearrange("k j (p t) -> k p j t", t=PACK)[:, :, :, t0 : t0 + PAIR],
+                interleaved[:].rearrange("k (t p j) -> k p j t", t=PACK, j=PACK),
+                wc_raw[b][:].rearrange("k j (p t) -> k p j t", t=PACK),
             )
-            codes = held([P, PAIR * P], U32, "wc_codes%d_%d" % (b, t0))
-            scales = held([P, PAIR * P], U8, "wc_scales%d_%d" % (b, t0))
-            quantise(codes[:], scales[:], interleaved[:])
-            for t in range(PAIR):
-                wc_operand[b, t0 + t] = (codes[:, P * t : P * (t + 1)], scales[:, P * t : P * (t + 1)])
+            return interleaved
 
         def gain_interleaved(engine, target, states):
             groups = states.shape[2] // RUN
@@ -189,7 +184,7 @@ def tile_list_clause_state_round_kernel(
             for s0 in range(0, width, EIGHTH):
                 cs_operand[m0 + s0] = (codes[:, s0 : s0 + EIGHTH], scales[:, s0 : s0 + EIGHTH])
 
-        x = [held([P, PACK, M], F32, "x0")[:], shared[:, 0 : PACK * M].rearrange("p (t m) -> p t m", t=PACK)]
+        x = [held([P, PACK, M], F32, "x0")[:]]
 
         def pick(row_tile, first=0, end=M):
             b, t = divmod(row_tile, PACK)
@@ -203,8 +198,8 @@ def tile_list_clause_state_round_kernel(
                 for t in range(PACK):
                     nc.tensor.matmul_mx(
                         out=c[:, t, :],
-                        lhsT=wc_operand[b, t][0].bitcast(FP8X4),
-                        lhsT_scale=wc_operand[b, t][1],
+                        lhsT=wc_codes[b][:, P * t : P * (t + 1)].bitcast(FP8X4),
+                        lhsT_scale=wc_scales[b][:, P * t : P * (t + 1)],
                         rhs=cs_codes.bitcast(FP8X4),
                         rhs_scale=cs_scales,
                         start=True,
@@ -232,11 +227,11 @@ def tile_list_clause_state_round_kernel(
             column, width = places[b, m0]
             strongest(tile[:, PACK * column : PACK * (column + width)], b, m0)
 
-        def quantise_z(z, used_up=None):
+        def quantise_z(z, used_up):
             tile, places = z
             columns = tile.shape[1] // PACK
             name = "z%d_%d" % min(places)
-            codes = reuse([P, columns], U32, name + "_codes", used_up or name + "_codes")
+            codes = reuse([P, columns], U32, name + "_codes", used_up)
             scales = held([P, columns], U8, name + "_scales")
             quantise(codes[:], scales[:], tile[:])
             for b, m0 in places:
@@ -267,18 +262,18 @@ def tile_list_clause_state_round_kernel(
         def result_tile(shape):
             return ring.tile(shape, F32, name="result", tag="result", bufs=RESULT_BANKS)
 
-        def update_on_gpsimd(m0, width, out_end=OUT_TILES):
-            tiles = BANK // width
-            for o0 in range(0, out_end, tiles):
-                y = product(m0, width, o0)
-                result = result_tile([P, tiles, width])
-                nc.scalar.copy(result[:], y[:])
-                for r0 in range(0, tiles, tiles // 2):
-                    rows = slice(r0, r0 + tiles // 2)
-                    out_tiles = slice(o0 + r0, o0 + r0 + tiles // 2)
-                    states = residual[m0 // HALF][:, out_tiles, m0 % HALF : m0 % HALF + width]
-                    nc.gpsimd.tensor_tensor(result[:, rows, :], result[:, rows, :], states, ALU.add)
-                    nc.sync.dma_start(out_rows[:, out_tiles, m0 : m0 + width], result[:, rows, :])
+        def copied(m0, o0):
+            y = product(m0, QUARTER, o0)
+            staged = result_tile([P, BANK // QUARTER, QUARTER])
+            nc.scalar.copy(staged[:], y[:])
+            return staged
+
+        def update_on_gpsimd(m0, o0, staged, used_up=None):
+            out_tiles = slice(o0, o0 + BANK // QUARTER)
+            result = reuse([P, BANK // QUARTER, QUARTER], F32, "sum", used_up) if used_up else staged
+            states = residual[m0 // HALF][:, out_tiles, m0 % HALF : m0 % HALF + QUARTER]
+            nc.gpsimd.tensor_tensor(result[:], staged[:], states, ALU.add)
+            nc.sync.dma_start(out_rows[:, out_tiles, m0 : m0 + QUARTER], result[:])
 
         def update_on_vector(m0, width, o0, y, pieces):
             tiles = BANK // width
@@ -300,24 +295,24 @@ def tile_list_clause_state_round_kernel(
         messages(2, 0, BANK)
         gather_words(BANK, 2 * BANK)
         messages(0, BANK, 2 * BANK)
+        messages(1, BANK, 2 * BANK)
         gather_words(2 * BANK, 3 * BANK)
         messages(0, 2 * BANK, 3 * BANK)
         gather_words(3 * BANK, S - SHORT)
         messages(0, 3 * BANK, S - SHORT)
         gather_words(S - SHORT, S)
         messages(0, S - SHORT, S)
-        messages(1, BANK, S)
+        messages(1, 2 * BANK, S)
 
         q0, q1, q2, q3 = range(0, M, QUARTER)
         first = held([P, QUARTER * PACK], BF16, "first")
         gain_interleaved(nc.gpsimd, first[:], cs_raw[q0])
-        third_eighth = held([P, EIGHTH * PACK], BF16, "third_eighth")
-        gain_interleaved(nc.vector, third_eighth[:], cs_raw[q1][:, :, 0:EIGHTH])
+        second = held([P, QUARTER * PACK], BF16, "second")
+        gain_interleaved(nc.vector, second[:, 0 : EIGHTH * PACK], cs_raw[q1])
         quantise_cs(q0, first)
-        quantise_cs(q1, third_eighth)
 
-        wc_raw.append(reuse([P, PACK, HALF], F32, "wc_raw1", "table_words")[:])
-        nc.sync.dma_start(wc_raw[1], wc_rows[:, :, HALF:H])
+        wc_raw.append(reuse([P, PACK, HALF], F32, "wc_raw1", "table_words"))
+        nc.sync.dma_start(wc_raw[1][:], wc_rows[:, :, HALF:H])
         cs_raw[HALF] = reuse([P, PACK, HALF], F32, "cs_raw2", "first")
         nc.sync.dma_start(cs_raw[HALF][:], cs_rows[:, :, HALF:M])
         w2_word_tile = reuse([P, PASSES, N], I32, "w2_word_tile", "v_words")
@@ -333,56 +328,63 @@ def tile_list_clause_state_round_kernel(
             nc.sync.dma_start(residual[half][:], cs_plain[:, :, half * HALF : (half + 1) * HALF])
 
         last_tile = ROW_TILES - 1
+        e0, e1, e2, e3, e4, e5, e6, e7 = range(0, M, EIGHTH)
         messages(2, BANK, S)
         pick(2)
+        shared = reuse([P, PACK * M - LATE + PACK * EIGHTH], F32, "shared", "h2")
+        x.append(shared[:, 0 : PACK * M].rearrange("p (t m) -> p t m", t=PACK))
+        cs_raw[e3] = shared[:, PACK * M - LATE :].rearrange("p (j m) -> p j m", j=PACK)
+        nc.sync.dma_start(cs_raw[e3], cs_rows[:, :, e3:q2])
         for row_tile in range(3, last_tile):
             messages(row_tile, 0, S)
             pick(row_tile)
-        messages(last_tile, 0, S)
+        messages(last_tile, 0, S - BANK)
+        quantise(wc_codes[0][:], wc_scales[0][:], interleave_wc(0)[:])
+        messages(last_tile, S - BANK, S)
         pick(last_tile, 0, M - LATE)
-        prepare_wc(0, 0)
-        prepare_wc(0, PAIR)
-        pick(last_tile, M - LATE, M)
+        quantise(wc_codes[1][:], wc_scales[1][:], interleave_wc(1)[:])
 
-        e2, e3 = range(q1, q2, EIGHTH)
-        e6, e7 = range(q3, M, EIGHTH)
-        e0, e1 = range(q0, q1, EIGHTH)
-        z_first = z_tile([(0, e0, EIGHTH), (0, e1, EIGHTH), (1, q0, QUARTER)], "h4")
-        maxima(z_first, 0, e0)
-        prepare_wc(1, 0)
-        maxima(z_first, 0, e1)
-        prepare_wc(1, PAIR)
-        z_second = z_tile([(0, e2, EIGHTH), (0, e3, EIGHTH), (1, e2, EIGHTH), (1, e3, EIGHTH)], "table_words")
-        maxima(z_second, 0, e2)
+        middle = OUT_TILES // 2
+        z_first = z_tile([(0, q0, QUARTER), (1, q0, QUARTER)], "table_words")
+        maxima(z_first, 0, q0)
         maxima(z_first, 1, q0)
-        fourth_eighth = held([P, EIGHTH * PACK], BF16, "fourth_eighth")
-        gain_on_scalar(fourth_eighth[:], cs_raw[q1][:, :, EIGHTH:QUARTER], "h2")
-        quantise_cs(e3, fourth_eighth)
-        quantise_z(z_first)
-        second_half = reuse([P, HALF * PACK], BF16, "second_half", "h3")
-        gain_on_scalar(second_half[:], cs_raw[HALF][:], "h5")
+        gain_on_scalar(second[:, EIGHTH * PACK :], cs_raw[e3], "table_scales")
+        quantise_cs(q1, second)
+        quantise_z(z_first, "z_first_codes")
+        pick(last_tile, M - LATE, M)
+        third = reuse([P, QUARTER * PACK], BF16, "third", "h3")
+        gain_on_scalar(third[:], cs_raw[HALF][:, :, 0:QUARTER], "h5")
+        quantise_cs(q2, third)
 
-        maxima(z_second, 1, e2)
-        maxima(z_second, 0, e3)
-        maxima(z_second, 1, e3)
-        update_on_gpsimd(q0, QUARTER)
-        quantise_cs(q2, second_half)
-        quantise_z(z_second, "h5")
+        z_second = z_tile([(0, q1, QUARTER), (1, q1, QUARTER)], "h4")
+        maxima(z_second, 0, q1)
+        update_on_gpsimd(q0, 0, copied(q0, 0))
+        later = product(q0, QUARTER, middle)
+        maxima(z_second, 1, q1)
+        fourth = reuse([P, QUARTER * PACK], BF16, "fourth", "z_first_codes")
+        gain_on_scalar(fourth[:], cs_raw[HALF][:, :, QUARTER:HALF], "h6")
+        quantise_cs(q3, fourth)
+        quantise_z(z_second, "h6")
+        staged = result_tile([P, middle, QUARTER])
+        nc.scalar.copy(staged[:], later[:])
+        update_on_gpsimd(q0, middle, staged, "h4")
+        update_on_gpsimd(q1, 0, copied(q1, 0))
 
-        z_third = z_tile([(0, q2, QUARTER), (1, q2, QUARTER)], "h6")
-        z_fourth = [z_tile([(b, e6, EIGHTH), (b, e7, EIGHTH)], used_up) for b, used_up in enumerate(("h2", "h7"))]
+        z_third = z_tile([(0, q2, QUARTER), (1, q2, QUARTER)], "z_first_codes")
+        z_fourth = [z_tile([(b, e6, EIGHTH), (b, e7, EIGHTH)], used_up) for b, used_up in enumerate(("h5", "h7"))]
         maxima(z_third, 0, q2)
+        staged = copied(q1, middle)
         maxima(z_third, 1, q2)
         maxima(z_fourth[0], 0, e6)
-        update_on_gpsimd(q1, QUARTER)
-        quantise_z(z_third)
+        quantise_z(z_third, "z_third_codes")
+        update_on_gpsimd(q1, middle, staged, "z_first_codes")
         maxima(z_fourth[0], 0, e7)
+        staged = copied(q2, 0)
         maxima(z_fourth[1], 1, e6)
         maxima(z_fourth[1], 1, e7)
-        middle = OUT_TILES // 2
-        update_on_gpsimd(q2, QUARTER, middle)
-        quantise_z(z_fourth[0])
-        quantise_z(z_fourth[1])
+        quantise_z(z_fourth[0], "z_fourth_codes0")
+        quantise_z(z_fourth[1], "z_fourth_codes1")
+        update_on_gpsimd(q2, 0, staged, "h7")
         update_on_vector(q2, QUARTER, middle, product(q2, QUARTER, middle), 1)
         update_on_vector(q3, QUARTER, 0, product(q3, QUARTER, 0), 2)
         update_on_vector(q3, QUARTER, middle, product(q3, QUARTER, middle), 2)

@@ -32,6 +32,7 @@ HALF = M // 2
 SPARE = P - QUADRANT_ROWS * QUADRANTS
 RUN = 4
 RESULT_BANKS = 8
+KIB = 1024
 LATE = 3 * EIGHTH
 
 
@@ -42,12 +43,15 @@ def tile_list_clause_state_round_kernel(
     with ExitStack() as ctx:
         keep = ctx.enter_context(tc.tile_pool(name="keep", bufs=1))
         ring = ctx.enter_context(tc.tile_pool(name="ring", bufs=PASSES))
+        laid = ctx.enter_context(tc.tile_pool(name="laid", bufs=1))
         psum = ctx.enter_context(tc.psum_pool(name="psum", bufs=4))
 
         def held(shape, dtype, name):
             return keep.tile(shape, dtype, name=name, tag=name, align_bytes=64)
 
         def reuse(shape, dtype, name, used_up):
+            if isinstance(used_up, int):
+                return laid.tile(shape, dtype, name=name, tag="%s%d" % (name, used_up), align_bytes=64, offset=used_up)
             return keep.tile(shape, dtype, name=name, tag=used_up, align_bytes=64)
 
         def load_scale_rows(queue, tile, rows, places):
@@ -75,8 +79,8 @@ def tile_list_clause_state_round_kernel(
         for part in v_scales:
             nc.vector.memset(part[:].bitcast(I32), 0)
 
-        nc.sync.dma_start(literal_list[:], offs)
         nc.sync.dma_start(table_scales[SPARE:P].bitcast(I32), tab_scales[0].bitcast(I32))
+        nc.sync.dma_start(literal_list[:], offs)
         nc.sync.dma_start(wl_words_raw[:].bitcast(I32), wl_words[0].bitcast(I32))
         load_scale_rows(nc.sync, wl_scales_raw[:], wl_scales[0], range(QUADRANT_ROWS // 2))
         load_scale_rows(nc.scalar, wl_scales_raw[:], wl_scales[0], range(QUADRANT_ROWS // 2, QUADRANT_ROWS))
@@ -145,16 +149,20 @@ def tile_list_clause_state_round_kernel(
                 )
                 nc.scalar.activation(h[row_tile][:, j0 : j0 + width], acc[:], ACT.Identity, bias=bias[:, b, t : t + 1])
 
-        wc_codes = [held([P, HALF], U32, "wc_codes%d" % b) for b in range(PASSES)]
-        wc_scales = [held([P, HALF], U8, "wc_scales%d" % b) for b in range(PASSES)]
+        wc_operand = {}
 
-        def interleave_wc(b):
-            interleaved = ring.tile([P, HALF * PACK], BF16, name="wc_interleaved", tag="interleaved", align_bytes=64)
+        def prepare_wc(b, t0, tiles):
+            name = "%d_%d" % (b, t0)
+            interleaved = held([P, tiles * P * PACK], BF16, "wc_interleaved" + name)
             nc.scalar.copy(
-                interleaved[:].rearrange("k (t p j) -> k p j t", t=PACK, j=PACK),
-                wc_raw[b][:].rearrange("k j (p t) -> k p j t", t=PACK),
+                interleaved[:].rearrange("k (t p j) -> k p j t", t=tiles, j=PACK),
+                wc_raw[b][:].rearrange("k j (p t) -> k p j t", t=PACK)[:, :, :, t0 : t0 + tiles],
             )
-            return interleaved
+            codes = held([P, tiles * P], U32, "wc_codes" + name)
+            scales = held([P, tiles * P], U8, "wc_scales" + name)
+            quantise(codes[:], scales[:], interleaved[:])
+            for t in range(tiles):
+                wc_operand[b, t0 + t] = (codes[:, P * t : P * (t + 1)], scales[:, P * t : P * (t + 1)])
 
         def gain_interleaved(engine, target, states):
             groups = states.shape[2] // RUN
@@ -198,8 +206,8 @@ def tile_list_clause_state_round_kernel(
                 for t in range(PACK):
                     nc.tensor.matmul_mx(
                         out=c[:, t, :],
-                        lhsT=wc_codes[b][:, P * t : P * (t + 1)].bitcast(FP8X4),
-                        lhsT_scale=wc_scales[b][:, P * t : P * (t + 1)],
+                        lhsT=wc_operand[b, t][0].bitcast(FP8X4),
+                        lhsT_scale=wc_operand[b, t][1],
                         rhs=cs_codes.bitcast(FP8X4),
                         rhs_scale=cs_scales,
                         start=True,
@@ -270,7 +278,7 @@ def tile_list_clause_state_round_kernel(
 
         def update_on_gpsimd(m0, o0, staged, used_up=None):
             out_tiles = slice(o0, o0 + BANK // QUARTER)
-            result = reuse([P, BANK // QUARTER, QUARTER], F32, "sum", used_up) if used_up else staged
+            result = reuse([P, BANK // QUARTER, QUARTER], F32, "sum", used_up) if used_up is not None else staged
             states = residual[m0 // HALF][:, out_tiles, m0 % HALF : m0 % HALF + QUARTER]
             nc.gpsimd.tensor_tensor(result[:], staged[:], states, ALU.add)
             nc.sync.dma_start(out_rows[:, out_tiles, m0 : m0 + QUARTER], result[:])
@@ -339,10 +347,10 @@ def tile_list_clause_state_round_kernel(
             messages(row_tile, 0, S)
             pick(row_tile)
         messages(last_tile, 0, S - BANK)
-        quantise(wc_codes[0][:], wc_scales[0][:], interleave_wc(0)[:])
+        prepare_wc(0, 0, PACK)
         messages(last_tile, S - BANK, S)
         pick(last_tile, 0, M - LATE)
-        quantise(wc_codes[1][:], wc_scales[1][:], interleave_wc(1)[:])
+        prepare_wc(1, 0, PACK)
 
         middle = OUT_TILES // 2
         z_first = z_tile([(0, q0, QUARTER), (1, q0, QUARTER)], "table_words")
@@ -350,7 +358,7 @@ def tile_list_clause_state_round_kernel(
         maxima(z_first, 1, q0)
         gain_on_scalar(second[:, EIGHTH * PACK :], cs_raw[e3], "table_scales")
         quantise_cs(q1, second)
-        quantise_z(z_first, "z_first_codes")
+        quantise_z(z_first, KIB)
         pick(last_tile, M - LATE, M)
         third = reuse([P, QUARTER * PACK], BF16, "third", "h3")
         gain_on_scalar(third[:], cs_raw[HALF][:, :, 0:QUARTER], "h5")
@@ -361,30 +369,30 @@ def tile_list_clause_state_round_kernel(
         update_on_gpsimd(q0, 0, copied(q0, 0))
         later = product(q0, QUARTER, middle)
         maxima(z_second, 1, q1)
-        fourth = reuse([P, QUARTER * PACK], BF16, "fourth", "z_first_codes")
+        fourth = reuse([P, QUARTER * PACK], BF16, "fourth", KIB)
         gain_on_scalar(fourth[:], cs_raw[HALF][:, :, QUARTER:HALF], "h6")
         quantise_cs(q3, fourth)
         quantise_z(z_second, "h6")
         staged = result_tile([P, middle, QUARTER])
         nc.scalar.copy(staged[:], later[:])
-        update_on_gpsimd(q0, middle, staged, "h4")
+        update_on_gpsimd(q0, middle, staged, 0)
         update_on_gpsimd(q1, 0, copied(q1, 0))
 
-        z_third = z_tile([(0, q2, QUARTER), (1, q2, QUARTER)], "z_first_codes")
+        z_third = z_tile([(0, q2, QUARTER), (1, q2, QUARTER)], 2 * KIB)
         z_fourth = [z_tile([(b, e6, EIGHTH), (b, e7, EIGHTH)], used_up) for b, used_up in enumerate(("h5", "h7"))]
         maxima(z_third, 0, q2)
         staged = copied(q1, middle)
         maxima(z_third, 1, q2)
         maxima(z_fourth[0], 0, e6)
         quantise_z(z_third, "z_third_codes")
-        update_on_gpsimd(q1, middle, staged, "z_first_codes")
+        update_on_gpsimd(q1, middle, staged, 4 * KIB)
         maxima(z_fourth[0], 0, e7)
         staged = copied(q2, 0)
         maxima(z_fourth[1], 1, e6)
         maxima(z_fourth[1], 1, e7)
         quantise_z(z_fourth[0], "z_fourth_codes0")
         quantise_z(z_fourth[1], "z_fourth_codes1")
-        update_on_gpsimd(q2, 0, staged, "h7")
+        update_on_gpsimd(q2, 0, staged, "h5")
         update_on_vector(q2, QUARTER, middle, product(q2, QUARTER, middle), 1)
         update_on_vector(q3, QUARTER, 0, product(q3, QUARTER, 0), 2)
         update_on_vector(q3, QUARTER, middle, product(q3, QUARTER, middle), 2)

@@ -315,9 +315,10 @@ def tile_list_clause_state_round_kernel(
         q0, q1, q2, q3 = range(0, M, QUARTER)
         first = held([P, QUARTER * PACK], BF16, "first")
         gain_interleaved(nc.gpsimd, first[:], cs_raw[q0])
-        second = held([P, QUARTER * PACK], BF16, "second")
-        gain_interleaved(nc.vector, second[:, 0 : EIGHTH * PACK], cs_raw[q1])
+        third_eighth = held([P, EIGHTH * PACK], BF16, "third_eighth")
+        gain_interleaved(nc.vector, third_eighth[:], cs_raw[q1])
         quantise_cs(q0, first)
+        quantise_cs(q1, third_eighth)
 
         wc_raw.append(reuse([P, PACK, HALF], F32, "wc_raw1", "table_words"))
         nc.sync.dma_start(wc_raw[1][:], wc_rows[:, :, HALF:H])
@@ -356,19 +357,23 @@ def tile_list_clause_state_round_kernel(
         z_first = z_tile([(0, q0, QUARTER), (1, q0, QUARTER)], "table_words")
         maxima(z_first, 0, q0)
         maxima(z_first, 1, q0)
-        gain_on_scalar(second[:, EIGHTH * PACK :], cs_raw[e3], "table_scales")
-        quantise_cs(q1, second)
+        fourth_eighth = held([P, EIGHTH * PACK], BF16, "fourth_eighth")
+        gain_on_scalar(fourth_eighth[:], cs_raw[e3], "table_scales")
+        quantise_cs(e3, fourth_eighth)
+        pick(last_tile, M - LATE, q3)
         quantise_z(z_first, KIB)
-        pick(last_tile, M - LATE, M)
+        pick(last_tile, q3, M)
         third = reuse([P, QUARTER * PACK], BF16, "third", "h3")
         gain_on_scalar(third[:], cs_raw[HALF][:, :, 0:QUARTER], "h5")
         quantise_cs(q2, third)
 
-        z_second = z_tile([(0, q1, QUARTER), (1, q1, QUARTER)], "h4")
-        maxima(z_second, 0, q1)
+        z_second = z_tile([(b, m0, EIGHTH) for b in range(PASSES) for m0 in (e2, e3)], "h5")
+        maxima(z_second, 0, e2)
+        maxima(z_second, 1, e2)
+        maxima(z_second, 0, e3)
         update_on_gpsimd(q0, 0, copied(q0, 0))
         later = product(q0, QUARTER, middle)
-        maxima(z_second, 1, q1)
+        maxima(z_second, 1, e3)
         fourth = reuse([P, QUARTER * PACK], BF16, "fourth", KIB)
         gain_on_scalar(fourth[:], cs_raw[HALF][:, :, QUARTER:HALF], "h6")
         quantise_cs(q3, fourth)
@@ -379,7 +384,7 @@ def tile_list_clause_state_round_kernel(
         update_on_gpsimd(q1, 0, copied(q1, 0))
 
         z_third = z_tile([(0, q2, QUARTER), (1, q2, QUARTER)], 2 * KIB)
-        z_fourth = [z_tile([(b, e6, EIGHTH), (b, e7, EIGHTH)], used_up) for b, used_up in enumerate(("h5", "h7"))]
+        z_fourth = [z_tile([(b, e6, EIGHTH), (b, e7, EIGHTH)], used_up) for b, used_up in enumerate(("h4", "h7"))]
         maxima(z_third, 0, q2)
         staged = copied(q1, middle)
         maxima(z_third, 1, q2)
@@ -392,7 +397,7 @@ def tile_list_clause_state_round_kernel(
         maxima(z_fourth[1], 1, e7)
         quantise_z(z_fourth[0], "z_fourth_codes0")
         quantise_z(z_fourth[1], "z_fourth_codes1")
-        update_on_gpsimd(q2, 0, staged, "h5")
+        update_on_gpsimd(q2, 0, staged, "h4")
         update_on_vector(q2, QUARTER, middle, product(q2, QUARTER, middle), 1)
         update_on_vector(q3, QUARTER, 0, product(q3, QUARTER, 0), 2)
         update_on_vector(q3, QUARTER, middle, product(q3, QUARTER, middle), 2)

@@ -274,14 +274,15 @@ def tile_list_clause_state_round_kernel(
             y = product(m0, QUARTER, o0)
             staged = result_tile([P, BANK // QUARTER, QUARTER])
             nc.scalar.copy(staged[:], y[:])
-            return staged
+            return staged[:]
 
         def update_on_gpsimd(m0, o0, staged, used_up=None):
-            out_tiles = slice(o0, o0 + BANK // QUARTER)
-            result = reuse([P, BANK // QUARTER, QUARTER], F32, "sum", used_up) if used_up is not None else staged
+            tiles = staged.shape[1]
+            out_tiles = slice(o0, o0 + tiles)
+            result = reuse([P, tiles, QUARTER], F32, "sum", used_up)[:] if used_up is not None else staged
             states = residual[m0 // HALF][:, out_tiles, m0 % HALF : m0 % HALF + QUARTER]
-            nc.gpsimd.tensor_tensor(result[:], staged[:], states, ALU.add)
-            nc.sync.dma_start(out_rows[:, out_tiles, m0 : m0 + QUARTER], result[:])
+            nc.gpsimd.tensor_tensor(result, staged, states, ALU.add)
+            nc.sync.dma_start(out_rows[:, out_tiles, m0 : m0 + QUARTER], result)
 
         def update_on_vector(m0, width, o0, y, pieces):
             tiles = BANK // width
@@ -360,44 +361,45 @@ def tile_list_clause_state_round_kernel(
         fourth_eighth = held([P, EIGHTH * PACK], BF16, "fourth_eighth")
         gain_on_scalar(fourth_eighth[:], cs_raw[e3], "table_scales")
         quantise_cs(e3, fourth_eighth)
-        pick(last_tile, M - LATE, q3)
+        pick(last_tile, e5, e6)
         quantise_z(z_first, KIB)
-        pick(last_tile, q3, M)
+        pick(last_tile, e6, e7)
         third = reuse([P, QUARTER * PACK], BF16, "third", "h3")
         gain_on_scalar(third[:], cs_raw[HALF][:, :, 0:QUARTER], "h5")
         quantise_cs(q2, third)
 
         z_second = z_tile([(b, m0, EIGHTH) for b in range(PASSES) for m0 in (e2, e3)], "h5")
+        z_third = z_tile([(b, m0, EIGHTH) for b in range(PASSES) for m0 in (e4, e5)], "h4")
         maxima(z_second, 0, e2)
         maxima(z_second, 1, e2)
         maxima(z_second, 0, e3)
         update_on_gpsimd(q0, 0, copied(q0, 0))
-        later = product(q0, QUARTER, middle)
+        staged = copied(q0, middle)
         maxima(z_second, 1, e3)
+        maxima(z_third, 0, e4)
+        quantise_z(z_second, "z_second_codes")
         fourth = reuse([P, QUARTER * PACK], BF16, "fourth", KIB)
         gain_on_scalar(fourth[:], cs_raw[HALF][:, :, QUARTER:HALF], "h6")
         quantise_cs(q3, fourth)
-        quantise_z(z_second, "h6")
-        staged = result_tile([P, middle, QUARTER])
-        nc.scalar.copy(staged[:], later[:])
-        update_on_gpsimd(q0, middle, staged, 0)
+        pick(last_tile, e7, M)
+        update_on_gpsimd(q0, middle, staged, KIB)
         update_on_gpsimd(q1, 0, copied(q1, 0))
 
-        z_third = z_tile([(0, q2, QUARTER), (1, q2, QUARTER)], 2 * KIB)
-        z_fourth = [z_tile([(b, e6, EIGHTH), (b, e7, EIGHTH)], used_up) for b, used_up in enumerate(("h4", "h7"))]
-        maxima(z_third, 0, q2)
+        z_fourth = [z_tile([(b, e6, EIGHTH), (b, e7, EIGHTH)], used_up) for b, used_up in enumerate(("h3", "h7"))]
+        maxima(z_third, 0, e5)
         staged = copied(q1, middle)
-        maxima(z_third, 1, q2)
+        maxima(z_third, 1, e4)
+        maxima(z_third, 1, e5)
         maxima(z_fourth[0], 0, e6)
-        quantise_z(z_third, "z_third_codes")
-        update_on_gpsimd(q1, middle, staged, 4 * KIB)
         maxima(z_fourth[0], 0, e7)
-        staged = copied(q2, 0)
+        quantise_z(z_third, "z_third_codes")
+        update_on_gpsimd(q1, middle, staged[:, 0:1, :], "h4")
         maxima(z_fourth[1], 1, e6)
         maxima(z_fourth[1], 1, e7)
         quantise_z(z_fourth[0], "z_fourth_codes0")
         quantise_z(z_fourth[1], "z_fourth_codes1")
-        update_on_gpsimd(q2, 0, staged, "h4")
+        update_on_gpsimd(q1, middle + 1, staged[:, 1:2, :], "h3")
+        update_on_gpsimd(q2, 0, copied(q2, 0), "h7")
         update_on_vector(q2, QUARTER, middle, product(q2, QUARTER, middle), 1)
         update_on_vector(q3, QUARTER, 0, product(q3, QUARTER, 0), 2)
         update_on_vector(q3, QUARTER, middle, product(q3, QUARTER, middle), 2)

@@ -31,7 +31,7 @@ QUARTER = M // 4
 HALF = M // 2
 SPARE = P - QUADRANT_ROWS * QUADRANTS
 RUN = 4
-RESULT_BANKS = 8
+RESULT_BANKS = 10
 KIB = 1024
 LATE = 3 * EIGHTH
 
@@ -270,22 +270,24 @@ def tile_list_clause_state_round_kernel(
         def result_tile(shape):
             return ring.tile(shape, F32, name="result", tag="result", bufs=RESULT_BANKS)
 
-        def copied(m0, o0):
-            y = product(m0, QUARTER, o0)
-            staged = result_tile([P, BANK // QUARTER, QUARTER])
-            nc.scalar.copy(staged[:], y[:])
+        def copy_out(y):
+            staged = result_tile(list(y.shape))
+            nc.scalar.copy(staged[:], y)
             return staged[:]
 
-        def update_on_gpsimd(m0, o0, staged, used_up=None):
-            tiles = staged.shape[1]
-            out_tiles = slice(o0, o0 + tiles)
-            result = reuse([P, tiles, QUARTER], F32, "sum", used_up)[:] if used_up is not None else staged
-            states = residual[m0 // HALF][:, out_tiles, m0 % HALF : m0 % HALF + QUARTER]
-            nc.gpsimd.tensor_tensor(result, staged, states, ALU.add)
-            nc.sync.dma_start(out_rows[:, out_tiles, m0 : m0 + QUARTER], result)
+        def copied(m0, o0):
+            return copy_out(product(m0, QUARTER, o0)[:])
 
-        def update_on_vector(m0, width, o0, y, pieces):
-            tiles = BANK // width
+        def update_on_gpsimd(m0, o0, staged, used_up=None):
+            tiles, width = staged.shape[1:]
+            out_tiles = slice(o0, o0 + tiles)
+            result = reuse([P, tiles, width], F32, "sum", used_up)[:] if used_up is not None else staged
+            states = residual[m0 // HALF][:, out_tiles, m0 % HALF : m0 % HALF + width]
+            nc.gpsimd.tensor_tensor(result, staged, states, ALU.add)
+            nc.sync.dma_start(out_rows[:, out_tiles, m0 : m0 + width], result)
+
+        def update_on_vector(m0, o0, y, pieces):
+            tiles, width = y.shape[1:]
             result = result_tile([P, tiles, width])
             step = tiles // pieces
             for r0 in range(0, tiles, step):
@@ -393,13 +395,16 @@ def tile_list_clause_state_round_kernel(
         maxima(z_fourth[0], 0, e6)
         maxima(z_fourth[0], 0, e7)
         quantise_z(z_third, "z_third_codes")
-        update_on_gpsimd(q1, middle, staged[:, 0:1, :], "h4")
+        update_on_gpsimd(q1, middle, staged, "h4")
         maxima(z_fourth[1], 1, e6)
         maxima(z_fourth[1], 1, e7)
+        upper, lower = product(q2, QUARTER, middle), product(q2, QUARTER, 0)
+        update_on_vector(q2, middle, upper[:, 0:1, :], 1)
+        staged = copy_out(lower[:, 1:2, :])
         quantise_z(z_fourth[0], "z_fourth_codes0")
         quantise_z(z_fourth[1], "z_fourth_codes1")
-        update_on_gpsimd(q1, middle + 1, staged[:, 1:2, :], "h3")
-        update_on_gpsimd(q2, 0, copied(q2, 0), "h7")
-        update_on_vector(q2, QUARTER, middle, product(q2, QUARTER, middle), 1)
-        update_on_vector(q3, QUARTER, 0, product(q3, QUARTER, 0), 2)
-        update_on_vector(q3, QUARTER, middle, product(q3, QUARTER, middle), 2)
+        update_on_gpsimd(q2, 1, staged, "h3")
+        update_on_vector(q2, middle + 1, upper[:, 1:2, :], 1)
+        update_on_vector(q2, 0, lower[:, 0:1, :], 1)
+        update_on_vector(q3, 0, product(q3, QUARTER, 0)[:], 2)
+        update_on_vector(q3, middle, product(q3, QUARTER, middle)[:], 2)

@@ -33,7 +33,7 @@ SPARE = P - QUADRANT_ROWS * QUADRANTS
 RUN = 4
 RESULT_BANKS = 10
 KIB = 1024
-LATE = 3 * EIGHTH
+LATE = 2 * EIGHTH
 
 
 def tile_list_clause_state_round_kernel(
@@ -164,9 +164,9 @@ def tile_list_clause_state_round_kernel(
             for t in range(tiles):
                 wc_operand[b, t0 + t] = (codes[:, P * t : P * (t + 1)], scales[:, P * t : P * (t + 1)])
 
-        def gain_interleaved(engine, target, states):
+        def gain_on_vector(target, states):
             groups = states.shape[2] // RUN
-            engine.tensor_tensor(
+            nc.vector.tensor_tensor(
                 target.rearrange("p (g i j) -> p g j i", i=RUN, j=PACK),
                 states.rearrange("p j (g i) -> p g j i", i=RUN),
                 gain[:].unsqueeze(1).unsqueeze(3).to_broadcast([P, groups, PACK, RUN]),
@@ -317,9 +317,14 @@ def tile_list_clause_state_round_kernel(
 
         q0, q1, q2, q3 = range(0, M, QUARTER)
         first = held([P, QUARTER * PACK], BF16, "first")
-        gain_interleaved(nc.gpsimd, first[:], cs_raw[q0])
+        nc.gpsimd.tensor_tensor(
+            first[:].rearrange("p (m j) -> p m j", j=PACK),
+            cs_raw[q0].rearrange("p j m -> p m j"),
+            gain[:].unsqueeze(1).to_broadcast([P, QUARTER, PACK]),
+            ALU.mult,
+        )
         third_eighth = held([P, EIGHTH * PACK], BF16, "third_eighth")
-        gain_interleaved(nc.vector, third_eighth[:], cs_raw[q1])
+        gain_on_vector(third_eighth[:], cs_raw[q1])
         quantise_cs(q0, first)
         quantise_cs(q1, third_eighth)
 
@@ -357,14 +362,14 @@ def tile_list_clause_state_round_kernel(
         prepare_wc(1, 0, PACK)
 
         middle = OUT_TILES // 2
-        z_first = z_tile([(0, q0, QUARTER), (1, q0, QUARTER)], "table_words")
-        maxima(z_first, 0, q0)
-        maxima(z_first, 1, q0)
+        z_first = [z_tile([(b, q0, QUARTER)], used_up) for b, used_up in enumerate(("table_words", "z_first1"))]
+        maxima(z_first[0], 0, q0)
+        maxima(z_first[1], 1, q0)
         fourth_eighth = held([P, EIGHTH * PACK], BF16, "fourth_eighth")
         gain_on_scalar(fourth_eighth[:], cs_raw[e3], "table_scales")
         quantise_cs(e3, fourth_eighth)
-        pick(last_tile, e5, e6)
-        quantise_z(z_first, KIB)
+        quantise_z(z_first[0], KIB)
+        quantise_z(z_first[1], 2 * KIB)
         pick(last_tile, e6, e7)
         third = reuse([P, QUARTER * PACK], BF16, "third", "h3")
         gain_on_scalar(third[:], cs_raw[HALF][:, :, 0:QUARTER], "h5")
@@ -395,15 +400,15 @@ def tile_list_clause_state_round_kernel(
         maxima(z_fourth[0], 0, e6)
         maxima(z_fourth[0], 0, e7)
         quantise_z(z_third, "z_third_codes")
+        quantise_z(z_fourth[0], "z_fourth_codes0")
         update_on_gpsimd(q1, middle, staged, "h4")
         maxima(z_fourth[1], 1, e6)
         maxima(z_fourth[1], 1, e7)
         upper, lower = product(q2, QUARTER, middle), product(q2, QUARTER, 0)
         update_on_vector(q2, middle, upper[:, 0:1, :], 1)
         staged = copy_out(lower[:, 1:2, :])
-        quantise_z(z_fourth[0], "z_fourth_codes0")
         quantise_z(z_fourth[1], "z_fourth_codes1")
-        update_on_gpsimd(q2, 1, staged, "h3")
+        update_on_gpsimd(q2, 1, staged, "h7")
         update_on_vector(q2, middle + 1, upper[:, 1:2, :], 1)
         update_on_vector(q2, 0, lower[:, 0:1, :], 1)
         update_on_vector(q3, 0, product(q3, QUARTER, 0)[:], 2)

@@ -31,9 +31,9 @@ QUARTER = M // 4
 HALF = M // 2
 SPARE = P - QUADRANT_ROWS * QUADRANTS
 RUN = 4
-RESULT_BANKS = 10
+RESULT_BANKS = 8
 KIB = 1024
-LATE = 2 * EIGHTH
+LATE = 3 * EIGHTH
 
 
 def tile_list_clause_state_round_kernel(
@@ -370,46 +370,40 @@ def tile_list_clause_state_round_kernel(
         quantise_cs(e3, fourth_eighth)
         quantise_z(z_first[0], KIB)
         quantise_z(z_first[1], 2 * KIB)
-        pick(last_tile, e6, e7)
+        pick(last_tile, e5, e7)
         third = reuse([P, QUARTER * PACK], BF16, "third", "h3")
         gain_on_scalar(third[:], cs_raw[HALF][:, :, 0:QUARTER], "h5")
         quantise_cs(q2, third)
 
-        z_second = z_tile([(b, m0, EIGHTH) for b in range(PASSES) for m0 in (e2, e3)], "h5")
-        z_third = z_tile([(b, m0, EIGHTH) for b in range(PASSES) for m0 in (e4, e5)], "h4")
-        maxima(z_second, 0, e2)
-        maxima(z_second, 1, e2)
-        maxima(z_second, 0, e3)
+        z_second = [z_tile([(b, q1, QUARTER)], used_up) for b, used_up in enumerate(("h5", "z_first1"))]
+        maxima(z_second[0], 0, q1)
         update_on_gpsimd(q0, 0, copied(q0, 0))
-        staged = copied(q0, middle)
-        maxima(z_second, 1, e3)
-        maxima(z_third, 0, e4)
-        quantise_z(z_second, "z_second_codes")
+        waiting = product(q0, QUARTER, middle)
+        maxima(z_second[1], 1, q1)
+        quantise_z(z_second[0], "z_second_codes0")
+        quantise_z(z_second[1], "z_second_codes1")
         fourth = reuse([P, QUARTER * PACK], BF16, "fourth", KIB)
         gain_on_scalar(fourth[:], cs_raw[HALF][:, :, QUARTER:HALF], "h6")
         quantise_cs(q3, fourth)
         pick(last_tile, e7, M)
-        update_on_gpsimd(q0, middle, staged, KIB)
+        update_on_gpsimd(q0, middle, copy_out(waiting[:]), KIB)
         update_on_gpsimd(q1, 0, copied(q1, 0))
 
+        z_third = z_tile([(0, q2, QUARTER), (1, q2, QUARTER)], "h4")
         z_fourth = [z_tile([(b, e6, EIGHTH), (b, e7, EIGHTH)], used_up) for b, used_up in enumerate(("h3", "h7"))]
-        maxima(z_third, 0, e5)
+        maxima(z_third, 0, q2)
         staged = copied(q1, middle)
-        maxima(z_third, 1, e4)
-        maxima(z_third, 1, e5)
+        maxima(z_third, 1, q2)
         maxima(z_fourth[0], 0, e6)
-        maxima(z_fourth[0], 0, e7)
         quantise_z(z_third, "z_third_codes")
-        quantise_z(z_fourth[0], "z_fourth_codes0")
         update_on_gpsimd(q1, middle, staged, "h4")
+        maxima(z_fourth[0], 0, e7)
+        staged = copied(q2, 0)
         maxima(z_fourth[1], 1, e6)
         maxima(z_fourth[1], 1, e7)
-        upper, lower = product(q2, QUARTER, middle), product(q2, QUARTER, 0)
-        update_on_vector(q2, middle, upper[:, 0:1, :], 1)
-        staged = copy_out(lower[:, 1:2, :])
+        quantise_z(z_fourth[0], "z_fourth_codes0")
         quantise_z(z_fourth[1], "z_fourth_codes1")
-        update_on_gpsimd(q2, 1, staged, "h7")
-        update_on_vector(q2, middle + 1, upper[:, 1:2, :], 1)
-        update_on_vector(q2, 0, lower[:, 0:1, :], 1)
+        update_on_gpsimd(q2, 0, staged, "h3")
+        update_on_vector(q2, middle, product(q2, QUARTER, middle)[:], 2)
         update_on_vector(q3, 0, product(q3, QUARTER, 0)[:], 2)
         update_on_vector(q3, middle, product(q3, QUARTER, middle)[:], 2)

from contextlib import ExitStack

import concourse.mybir as mybir

K, H, N, T, S, M = 512, 1024, 512, 4096, 2048, 1024
FLOPS = 2 * K * H * S + 2 * N * H * M + 2 * H * N * M

F32 = mybir.dt.float32
BF16 = mybir.dt.bfloat16
I32 = mybir.dt.int32
U32 = mybir.dt.uint32
U16 = mybir.dt.uint16
U8 = mybir.dt.uint8
FP8X4 = mybir.dt.float8_e4m3fn_x4
FP4X4 = mybir.dt.float4_e2m1fn_x4
ALU = mybir.AluOpType
ACT = mybir.ActivationFunctionType

P = 128
PACK = 4
QUADRANTS = 4
QUADRANT_ROWS = 4
PASSES = H // (P * PACK)
ROW_TILES = PASSES * PACK
BANK = 512
SHORT = BANK // 2
LIST_ROWS = 16
OUT_TILES = N // P
EIGHTH = BANK // PACK
QUARTER = M // 4
HALF = M // 2
SPARE = P - QUADRANT_ROWS * QUADRANTS
RUN = 4
RESULT_BANKS = 8
KIB = 1024
LATE = 3 * EIGHTH


def tile_list_clause_state_round_kernel(
    tc, tab_words, tab_scales, offs, offs2, wl_words, wl_scales, bl, wgt, cs, gc, wc, w2_words, w2_scales, out
):
    nc = tc.nc
    with ExitStack() as ctx:
        keep = ctx.enter_context(tc.tile_pool(name="keep", bufs=1))
        ring = ctx.enter_context(tc.tile_pool(name="ring", bufs=PASSES))
        laid = ctx.enter_context(tc.tile_pool(name="laid", bufs=1))
        psum = ctx.enter_context(tc.psum_pool(name="psum", bufs=4))

        def held(shape, dtype, name):
            return keep.tile(shape, dtype, name=name, tag=name, align_bytes=64)

        def reuse(shape, dtype, name, used_up):
            if isinstance(used_up, int):
                return laid.tile(shape, dtype, name=name, tag="%s%d" % (name, used_up), align_bytes=64, offset=used_up)
            return keep.tile(shape, dtype, name=name, tag=used_up, align_bytes=64)

        def load_scale_rows(queue, tile, rows, places):
            for r in places:
                queue.dma_start(tile[r:P:32].bitcast(I32), rows[r : QUADRANT_ROWS * QUADRANTS : QUADRANT_ROWS].bitcast(I32))

        def quantise(codes, scales, values):
            nc.vector.quantize_mx(out=codes.bitcast(FP8X4), scales=scales, in_=values)

        literal_list = held([P, S // LIST_ROWS], U16, "literal_list")
        slot_lists = held([P, M // LIST_ROWS], U16, "slot_lists")
        table_scales = held([P, T], U8, "table_scales")
        table_words = held([P, T], I32, "table_words")
        wl_words_raw = held([P, 2 * H], U8, "wl_words_raw")
        wl_scales_raw = held([P, H], U8, "wl_scales_raw")
        bias = held([P, PASSES, PACK], F32, "bias")
        gain = held([P, PACK], F32, "gain")
        scale_parts = [(0, BANK), (BANK, S)]
        v_scales = [held([P, end - first], U8, "v_scales%d" % first) for first, end in scale_parts]

        nc.gpsimd.dma_start(bias[:], bl.rearrange("(b p t) -> p b t", b=PASSES, t=PACK))
        nc.gpsimd.dma_start(gain[:], gc.rearrange("(p j) -> p j", j=PACK))
        nc.vector.memset(wl_scales_raw[:].bitcast(I32), 0)
        nc.vector.memset(table_scales[0:SPARE].bitcast(I32), 0)
        for part in v_scales:
            nc.vector.memset(part[:].bitcast(I32), 0)

        nc.sync.dma_start(table_scales[SPARE:P].bitcast(I32), tab_scales[0].bitcast(I32))
        nc.sync.dma_start(literal_list[:], offs)
        nc.sync.dma_start(wl_words_raw[:].bitcast(I32), wl_words[0].bitcast(I32))
        load_scale_rows(nc.sync, wl_scales_raw[:], wl_scales[0], range(QUADRANT_ROWS // 2))
        load_scale_rows(nc.scalar, wl_scales_raw[:], wl_scales[0], range(QUADRANT_ROWS // 2, QUADRANT_ROWS))
        nc.sync.dma_start(table_words[:], tab_words[0].rearrange("p t i -> p (t i)").bitcast(I32))

        wl_dealt_words = [held([P, 2 * HALF], U8, "wl_dealt_words%d" % b) for b in range(PASSES)]
        wl_dealt_scales = [held([P, HALF], U8, "wl_dealt_scales%d" % b) for b in range(PASSES)]
        for b in range(PASSES):
            nc.scalar.copy(
                wl_dealt_words[b][:].bitcast(U16).rearrange("k (t p) -> k t p", t=PACK),
                wl_words_raw[:, 2 * HALF * b : 2 * HALF * (b + 1)].bitcast(U16).rearrange("k (p t) -> k t p", t=PACK),
            )
            nc.gpsimd.tensor_copy(
                wl_dealt_scales[b][:].rearrange("k (t p) -> k t p", t=PACK),
                wl_scales_raw[:, HALF * b : HALF * (b + 1)].rearrange("k (p t) -> k t p", t=PACK),
            )

        def entries(first, end):
            return literal_list[:, first // LIST_ROWS : end // LIST_ROWS]

        gathered = [held([P, end - first], U8, "gathered_scales%d" % part) for part, (first, end) in enumerate(scale_parts)]
        for part, (first, end) in enumerate(scale_parts):
            nc.vector.tensor_copy(gathered[part][:], table_scales[:].indirect(entries(first, end)))

        def carry_scale_rows(queue, half):
            for r in range(QUADRANT_ROWS):
                rows = gathered[half][SPARE + r : P : QUADRANT_ROWS]
                queue.dma_start(v_scales[half][r:P:32].bitcast(I32), rows.bitcast(I32))

        wc_rows = wc.rearrange("(p j) r -> p j r", j=PACK)
        cs_rows = cs.rearrange("(p j) m -> p j m", j=PACK)
        nc.sync.dma_start(slot_lists[:], offs2)
        carry_scale_rows(nc.scalar, 0)
        carry_scale_rows(nc.scalar, 1)
        cs_first = reuse([P, PACK * (QUARTER + EIGHTH)], F32, "cs_first", "wl_scales_raw")
        cs_raw = {}
        for m0, width in ((0, QUARTER), (QUARTER, EIGHTH)):
            cs_raw[m0] = cs_first[:, PACK * m0 : PACK * (m0 + width)].rearrange("p (j m) -> p j m", j=PACK)
            nc.sync.dma_start(cs_raw[m0], cs_rows[:, :, m0 : m0 + width])
        weight = reuse([P, M], F32, "weight", "gathered_scales0")[:]
        nc.sync.dma_start(weight, wgt)
        wc_raw = [reuse([P, PACK, HALF], F32, "wc_raw0", "gathered_scales1")]
        nc.sync.dma_start(wc_raw[0][:], wc_rows[:, :, 0:HALF])

        v_words = held([P, S], U32, "v_words")
        h = [held([P, S], F32, "h%d" % row_tile) for row_tile in range(ROW_TILES)]

        def gather_words(first, end):
            nc.vector.tensor_copy(v_words[:, first:end], table_words[:].bitcast(U32).indirect(entries(first, end)))

        def messages(row_tile, first, end):
            b, t = divmod(row_tile, PACK)
            for j0 in range(first, end, BANK):
                width = min(BANK, end - j0)
                half = 0 if j0 < BANK else 1
                column = j0 - scale_parts[half][0]
                acc = psum.tile([P, width], F32, name="acc", tag="wide")
                nc.tensor.matmul_mx(
                    out=acc[:],
                    lhsT=wl_dealt_words[b][:, 2 * P * t : 2 * P * (t + 1)].bitcast(FP4X4),
                    lhsT_scale=wl_dealt_scales[b][:, P * t : P * (t + 1)],
                    rhs=v_words[:, j0 : j0 + width].bitcast(FP8X4),
                    rhs_scale=v_scales[half][:, column : column + width],
                    start=True,
                    stop=True,
                )
                nc.scalar.activation(h[row_tile][:, j0 : j0 + width], acc[:], ACT.Identity, bias=bias[:, b, t : t + 1])

        wc_operand = {}

        def prepare_wc(b, t0, tiles):
            name = "%d_%d" % (b, t0)
            interleaved = held([P, tiles * P * PACK], BF16, "wc_interleaved" + name)
            nc.scalar.copy(
                interleaved[:].rearrange("k (t p j) -> k p j t", t=tiles, j=PACK),
                wc_raw[b][:].rearrange("k j (p t) -> k p j t", t=PACK)[:, :, :, t0 : t0 + tiles],
            )
            codes = held([P, tiles * P], U32, "wc_codes" + name)
            scales = held([P, tiles * P], U8, "wc_scales" + name)
            quantise(codes[:], scales[:], interleaved[:])
            for t in range(tiles):
                wc_operand[b, t0 + t] = (codes[:, P * t : P * (t + 1)], scales[:, P * t : P * (t + 1)])

        def gain_on_vector(target, states):
            groups = states.shape[2] // RUN
            nc.vector.tensor_tensor(
                target.rearrange("p (g i j) -> p g j i", i=RUN, j=PACK),
                states.rearrange("p j (g i) -> p g j i", i=RUN),
                gain[:].unsqueeze(1).unsqueeze(3).to_broadcast([P, groups, PACK, RUN]),
                ALU.mult,
            )

        def gain_on_scalar(target, states, used_up):
            gained = reuse([P, PACK, states.shape[2]], BF16, "gained", used_up)
            for j in range(PACK):
                nc.scalar.activation(gained[:, j, :], states[:, j, :], ACT.Copy, scale=gain[:, j : j + 1])
            nc.scalar.copy(
                target.rearrange("p (g i j) -> p g j i", i=RUN, j=PACK),
                gained[:].rearrange("p j (g i) -> p g j i", i=RUN),
            )

        cs_operand = {}

        def quantise_cs(m0, interleaved):
            width = interleaved.shape[1] // PACK
            codes = held([P, width], U32, "cs_codes%d" % m0)
            scales = held([P, width], U8, "cs_scales%d" % m0)
            quantise(codes[:], scales[:], interleaved[:])
            for s0 in range(0, width, EIGHTH):
                cs_operand[m0 + s0] = (codes[:, s0 : s0 + EIGHTH], scales[:, s0 : s0 + EIGHTH])

        x = [held([P, PACK, M], F32, "x0")[:]]

        def pick(row_tile, first=0, end=M):
            b, t = divmod(row_tile, PACK)
            clauses = slot_lists[:, first // LIST_ROWS : end // LIST_ROWS]
            nc.vector.tensor_tensor(x[b][:, t, first:end], h[row_tile][:].indirect(clauses), weight[:, first:end], ALU.mult)

        def strongest(z, b, m0):
            for s0 in range(0, z.shape[1] // PACK, EIGHTH):
                cs_codes, cs_scales = cs_operand[m0 + s0]
                c = psum.tile([P, PACK, EIGHTH], F32, name="c", tag="proj")
                for t in range(PACK):
                    nc.tensor.matmul_mx(
                        out=c[:, t, :],
                        lhsT=wc_operand[b, t][0].bitcast(FP8X4),
                        lhsT_scale=wc_operand[b, t][1],
                        rhs=cs_codes.bitcast(FP8X4),
                        rhs_scale=cs_scales,
                        start=True,
                        stop=True,
                    )
                nc.vector.tensor_tensor(
                    z[:, PACK * s0 : PACK * (s0 + EIGHTH)].rearrange("p (g i t) -> p g t i", i=RUN, t=PACK),
                    c[:].rearrange("p t (g i) -> p g t i", i=RUN),
                    x[b][:, :, m0 + s0 : m0 + s0 + EIGHTH].rearrange("p t (g i) -> p g t i", i=RUN),
                    ALU.max,
                )

        z_operand = {}

        def z_tile(pieces, used_up):
            tile = reuse([P, PACK * sum(width for b, m0, width in pieces)], BF16, "z", used_up)
            places, column = {}, 0
            for b, m0, width in pieces:
                places[b, m0] = (column, width)
                column = column + width
            return tile, places

        def maxima(z, b, m0):
            tile, places = z
            column, width = places[b, m0]
            strongest(tile[:, PACK * column : PACK * (column + width)], b, m0)

        def quantise_z(z, used_up):
            tile, places = z
            columns = tile.shape[1] // PACK
            name = "z%d_%d" % min(places)
            codes = reuse([P, columns], U32, name + "_codes", used_up)
            scales = held([P, columns], U8, name + "_scales")
            quantise(codes[:], scales[:], tile[:])
            for b, m0 in places:
                column, width = places[b, m0]
                for s0 in range(0, width, EIGHTH):
                    z_operand[b, m0 + s0] = (codes, scales, column + s0)

        out_rows = out.rearrange("(o p) m -> p o m", p=P)
        residual = []

        def product(m0, width, o0):
            tiles = BANK // width
            y = psum.tile([P, tiles, width], F32, name="y", tag="wide")
            for b in range(PASSES):
                for o in range(o0, o0 + tiles):
                    codes, scales, z0 = z_operand[b, m0]
                    nc.tensor.matmul_mx(
                        out=y[:, o - o0, :],
                        lhsT=w2_word_tile[:, b, P * o : P * (o + 1)].bitcast(FP8X4),
                        lhsT_scale=w2_scale_tile[:, b, P * o : P * (o + 1)],
                        rhs=codes[:, z0 : z0 + width].bitcast(FP8X4),
                        rhs_scale=scales[:, z0 : z0 + width],
                        start=(b == 0 and o == o0),
                        stop=(b == PASSES - 1 and o == o0 + tiles - 1),
                    )
            return y

        def result_tile(shape):
            return ring.tile(shape, F32, name="result", tag="result", bufs=RESULT_BANKS)

        def copy_out(y):
            staged = result_tile(list(y.shape))
            nc.scalar.copy(staged[:], y)
            return staged[:]

        def copied(m0, o0):
            return copy_out(product(m0, QUARTER, o0)[:])

        def update_on_gpsimd(m0, o0, staged, used_up=None):
            tiles, width = staged.shape[1:]
            out_tiles = slice(o0, o0 + tiles)
            result = reuse([P, tiles, width], F32, "sum", used_up)[:] if used_up is not None else staged
            states = residual[m0 // HALF][:, out_tiles, m0 % HALF : m0 % HALF + width]
            nc.gpsimd.tensor_tensor(result, staged, states, ALU.add)
            nc.sync.dma_start(out_rows[:, out_tiles, m0 : m0 + width], result)

        def update_on_vector(m0, o0, y, pieces):
            tiles, width = y.shape[1:]
            result = result_tile([P, tiles, width])
            step = tiles // pieces
            for r0 in range(0, tiles, step):
                rows = slice(r0, r0 + step)
                out_tiles = slice(o0 + r0, o0 + r0 + step)
                states = residual[m0 // HALF][:, out_tiles, m0 % HALF : m0 % HALF + width]
                nc.vector.tensor_tensor(result[:, rows, :], y[:, rows, :], states, ALU.add)
                nc.scalar.dma_start(out_rows[:, out_tiles, m0 : m0 + width], result[:, rows, :])

        gather_words(0, SHORT)
        messages(0, 0, SHORT)
        messages(1, 0, SHORT)
        gather_words(SHORT, BANK)
        messages(0, SHORT, BANK)
        messages(1, SHORT, BANK)
        messages(2, 0, BANK)
        gather_words(BANK, 2 * BANK)
        messages(0, BANK, 2 * BANK)
        messages(1, BANK, 2 * BANK)
        gather_words(2 * BANK, 3 * BANK)
        messages(0, 2 * BANK, 3 * BANK)
        gather_words(3 * BANK, S - SHORT)
        messages(0, 3 * BANK, S - SHORT)
        gather_words(S - SHORT, S)
        messages(0, S - SHORT, S)
        messages(1, 2 * BANK, S)

        q0, q1, q2, q3 = range(0, M, QUARTER)
        first = held([P, QUARTER * PACK], BF16, "first")
        nc.gpsimd.tensor_tensor(
            first[:].rearrange("p (m j) -> p m j", j=PACK),
            cs_raw[q0].rearrange("p j m -> p m j"),
            gain[:].unsqueeze(1).to_broadcast([P, QUARTER, PACK]),
            ALU.mult,
        )
        third_eighth = held([P, EIGHTH * PACK], BF16, "third_eighth")
        gain_on_vector(third_eighth[:], cs_raw[q1])
        quantise_cs(q0, first)
        quantise_cs(q1, third_eighth)

        wc_raw.append(reuse([P, PACK, HALF], F32, "wc_raw1", "table_words"))
        nc.sync.dma_start(wc_raw[1][:], wc_rows[:, :, HALF:H])
        cs_raw[HALF] = reuse([P, PACK, HALF], F32, "cs_raw2", "first")
        nc.sync.dma_start(cs_raw[HALF][:], cs_rows[:, :, HALF:M])
        w2_word_tile = reuse([P, PASSES, N], I32, "w2_word_tile", "v_words")
        nc.sync.dma_start(w2_word_tile[:], w2_words.rearrange("a p n i -> p a (n i)").bitcast(I32))
        w2_scale_tile = reuse([P, PASSES, N], U8, "w2_scale_tile", "wl_words_raw")
        nc.gpsimd.memset(w2_scale_tile[:].rearrange("p a n -> p (a n)").bitcast(I32), 0)
        load_scale_rows(nc.sync, w2_scale_tile[:], w2_scales.rearrange("a q n -> q a n"), range(QUADRANT_ROWS))
        pick(0)
        pick(1)
        cs_plain = cs.rearrange("(o p) m -> p o m", p=P)
        for half, used_up in enumerate(("h1", "h0")):
            residual.append(reuse([P, OUT_TILES, HALF], F32, "residual", used_up))
            nc.sync.dma_start(residual[half][:], cs_plain[:, :, half * HALF : (half + 1) * HALF])

        last_tile = ROW_TILES - 1
        e0, e1, e2, e3, e4, e5, e6, e7 = range(0, M, EIGHTH)
        messages(2, BANK, S)
        pick(2)
        shared = reuse([P, PACK * M - LATE + PACK * EIGHTH], F32, "shared", "h2")
        x.append(shared[:, 0 : PACK * M].rearrange("p (t m) -> p t m", t=PACK))
        cs_raw[e3] = shared[:, PACK * M - LATE :].rearrange("p (j m) -> p j m", j=PACK)
        nc.sync.dma_start(cs_raw[e3], cs_rows[:, :, e3:q2])
        for row_tile in range(3, last_tile):
            messages(row_tile, 0, S)
            pick(row_tile)
        messages(last_tile, 0, S - BANK)
        prepare_wc(0, 0, PACK)
        messages(last_tile, S - BANK, S)
        pick(last_tile, 0, M - LATE)
        prepare_wc(1, 0, PACK)

        middle = OUT_TILES // 2
        z_first = [z_tile([(b, q0, QUARTER)], used_up) for b, used_up in enumerate(("table_words", "z_first1"))]
        maxima(z_first[0], 0, q0)
        maxima(z_first[1], 1, q0)
        fourth_eighth = held([P, EIGHTH * PACK], BF16, "fourth_eighth")
        gain_on_scalar(fourth_eighth[:], cs_raw[e3], "table_scales")
        quantise_cs(e3, fourth_eighth)
        quantise_z(z_first[0], KIB)
        quantise_z(z_first[1], 2 * KIB)
        pick(last_tile, e5, e7)
        third = reuse([P, QUARTER * PACK], BF16, "third", "h3")
        gain_on_scalar(third[:], cs_raw[HALF][:, :, 0:QUARTER], "h5")
        quantise_cs(q2, third)

        z_second = [z_tile([(b, q1, QUARTER)], used_up) for b, used_up in enumerate(("h5", "z_first1"))]
        maxima(z_second[0], 0, q1)
        update_on_gpsimd(q0, 0, copied(q0, 0))
        waiting = product(q0, QUARTER, middle)
        maxima(z_second[1], 1, q1)
        quantise_z(z_second[0], "z_second_codes0")
        quantise_z(z_second[1], "z_second_codes1")
        fourth = reuse([P, QUARTER * PACK], BF16, "fourth", KIB)
        gain_on_scalar(fourth[:], cs_raw[HALF][:, :, QUARTER:HALF], "h6")
        quantise_cs(q3, fourth)
        pick(last_tile, e7, M)
        update_on_gpsimd(q0, middle, copy_out(waiting[:]), KIB)
        update_on_gpsimd(q1, 0, copied(q1, 0))

        z_third = z_tile([(0, q2, QUARTER), (1, q2, QUARTER)], "h4")
        z_fourth = [z_tile([(b, e6, EIGHTH), (b, e7, EIGHTH)], used_up) for b, used_up in enumerate(("h3", "h7"))]
        maxima(z_third, 0, q2)
        staged = copied(q1, middle)
        maxima(z_third, 1, q2)
        maxima(z_fourth[0], 0, e6)
        quantise_z(z_third, "z_third_codes")
        update_on_gpsimd(q1, middle, staged, "h4")
        maxima(z_fourth[0], 0, e7)
        staged = copied(q2, 0)
        maxima(z_fourth[1], 1, e6)
        maxima(z_fourth[1], 1, e7)
        quantise_z(z_fourth[0], "z_fourth_codes0")
        quantise_z(z_fourth[1], "z_fourth_codes1")
        update_on_gpsimd(q2, 0, staged, "h3")
        update_on_vector(q2, middle, product(q2, QUARTER, middle)[:], 2)
        update_on_vector(q3, 0, product(q3, QUARTER, 0)[:], 2)
        update_on_vector(q3, middle, product(q3, QUARTER, middle)[:], 2)
